import numpy as np
import ml_dtypes


def mxq(x, axis, fmt="e4m3"):
    dtype, down = {"e4m3": (ml_dtypes.float8_e4m3fn, 7), "e5m2": (ml_dtypes.float8_e5m2, 14)}[fmt]
    v = np.moveaxis(np.asarray(x, np.float32).astype(ml_dtypes.bfloat16).astype(np.float64), axis, -1)
    blocks = v.reshape(v.shape[:-1] + (-1, 32))
    amax = np.abs(blocks).max(-1, keepdims=True)
    byte = np.maximum(np.where(amax > 0, np.frexp(amax)[1] - 1 + 127, 0) - down, 1)
    scale = np.exp2(byte - 127.0)
    codes = (blocks / scale).astype(np.float32).astype(dtype).astype(np.float64)
    return np.moveaxis((codes * scale).reshape(v.shape), -1, axis)


WIDE = False


def mx_kscale(k):
    if not WIDE:
        return np.ones(k)
    levels = np.array([24, -24, 12, -12, 0])
    if k % 512:
        return np.exp2(np.random.permutation(np.resize(levels, k // 32))).repeat(32)
    a = np.empty((k // 512, 16))
    for p in range(k // 512):
        a[p, :8] = np.random.permutation(np.resize(levels, 8))
        for g in range(8):
            far = levels[np.abs(levels - a[p, g]) >= 10]
            a[p, g + 8] = far[np.random.randint(len(far))]
    return np.exp2(a.ravel()).repeat(32)


def f64(x):
    return np.asarray(x).astype(np.float64)


def striped(idx):
    return np.tile(idx.reshape(-1, 16).T, (8, 1)).astype(np.uint16)


def unstriped(offs):
    return offs[:16].T.reshape(-1).astype(np.int64)


E2M1 = np.array([0.0, 0.5, 1.0, 1.5, 2.0, 3.0, 4.0, 6.0, -0.0, -0.5, -1.0, -1.5, -2.0, -3.0, -4.0, -6.0])


def pack_weight(w, fmt):
    k, n = w.shape
    w = f64(np.asarray(w, np.float32).astype(ml_dtypes.bfloat16)).reshape(k // 32, 32, n)
    amax = np.abs(w).max(1)
    if fmt == "e4m3":
        byte = np.frexp(amax)[1] - 1 + 127 - 7
    else:
        mant, ex = np.frexp(amax / 6.0)
        byte = np.where(mant > 0.5, ex, ex - 1) + 127
    byte = np.clip(np.where(amax > 0, byte, 1), 1, 254)
    scaled = (w * np.exp2(127.0 - byte)[:, None, :]).reshape(k, n).astype(np.float32)
    by_word = np.ascontiguousarray(scaled.reshape(k // 512, 128, 4, n).transpose(0, 1, 3, 2))
    if fmt == "e4m3":
        words = by_word.astype(ml_dtypes.float8_e4m3fn).view(np.uint8)
    else:
        c = by_word.astype(ml_dtypes.float4_e2m1fn).view(np.uint8) & 0xF
        words = (c[..., 0::2] | (c[..., 1::2] << 4)).reshape(k // 512, 128, 2 * n)
    return np.ascontiguousarray(words), np.ascontiguousarray(byte.astype(np.uint8).reshape(k // 512, 16, n))


def unpack_weight(words, scales, fmt):
    g, _, n = scales.shape
    words = np.ascontiguousarray(words).reshape(g, 128, n, -1)
    if fmt == "e4m3":
        vals = words.view(ml_dtypes.float8_e4m3fn).astype(np.float64)
    else:
        nib = np.empty((g, 128, n, 4), np.uint8)
        nib[..., 0::2] = words & 0xF
        nib[..., 1::2] = words >> 4
        vals = E2M1[nib]
    vals = vals * np.repeat(np.exp2(scales.astype(np.float64) - 127.0), 8, axis=1)[..., None]
    return vals.transpose(0, 1, 3, 2).reshape(g * 512, n)


def sigm(f):
    return 1.0 / (1.0 + np.exp(-np.maximum(f, -700.0)))


K, R, M, N, T, J = 1024, 512, 512, 256, 4096, 2048


def setup_inputs():
    n = np.random.standard_normal
    s = mx_kscale(K)[:, None]
    s2 = mx_kscale(K)[:, None]
    u = mx_kscale(R)[:, None]
    p_tab = pack_weight(n((K, T)) * s2, "e4m3")
    p_wq = pack_weight(n((K, R)) / np.sqrt(K) / s / u.T, "e2m1")
    p_wv4 = pack_weight(n((K, N)) / np.sqrt(K) / s2, "e2m1")
    return {
        "tab_words": p_tab[0],
        "tab_scales": p_tab[1],
        "x": (n((K, M)) * s).astype(np.float32),
        "wq_words": p_wq[0],
        "wq_scales": p_wq[1],
        "wk": (n((K, R)) / np.sqrt(K) / s2 * u.T).astype(np.float32),
        "wv4_words": p_wv4[0],
        "wv4_scales": p_wv4[1],
        "wvd": (0.4 * (n((K, N)) / np.sqrt(K) / s2)).astype(np.float32),
        "offs": striped(np.random.permutation(T)[:J]),
    }


def reference(tab_words, tab_scales, x, wq_words, wq_scales, wk, wv4_words, wv4_scales, wvd, offs):
    idx = unstriped(offs)
    tab_ = unpack_weight(tab_words, tab_scales, "e4m3")[:, idx]
    x_ = mxq(f64(x), 0, "e4m3")
    wq_ = unpack_weight(wq_words, wq_scales, "e2m1")
    wk_ = mxq(f64(wk), 0, "e4m3")
    qr = wq_.T @ x_
    kr = wk_.T @ tab_
    qr_ = mxq(qr, 0, "e4m3")
    kr_ = mxq(kr, 0, "e4m3")
    sc = qr_.T @ kr_
    wv4_ = unpack_weight(wv4_words, wv4_scales, "e2m1")
    wvd_ = mxq(f64(wvd), 0, "e4m3")
    vv = wv4_.T @ tab_ + wvd_.T @ tab_
    return sigm(sc * 0.03125), vv

@@ -1,0 +1,356 @@
+from contextlib import ExitStack
+
+import concourse.mybir as mybir
+
+K, R, M, N, T, J = 1024, 512, 512, 256, 4096, 2048
+FLOPS = 2 * (K * R * M + K * R * J + R * M * J + 2 * K * N * J)
+
+F32 = mybir.dt.float32
+BF16 = mybir.dt.bfloat16
+I32 = mybir.dt.int32
+U32 = mybir.dt.uint32
+U16 = mybir.dt.uint16
+U8 = mybir.dt.uint8
+FP8X4 = mybir.dt.float8_e4m3fn_x4
+FP4X4 = mybir.dt.float4_e2m1fn_x4
+SIGMOID = mybir.ActivationFunctionType.Sigmoid
+
+P = 128
+PASSES = K // 512
+CH = 512
+NCH = J // CH
+KIB = 1024
+MOVES = "SG"
+LOADS = [["tab0","wv4w","w4s","wvd0","tab1","wvd1"],[],["wk0","wk1","wk2","wk3","wq","x0","x1","x2","x3"]]
+ORDER = [
+    ["cw",0,"V"],
+    ["g",3],
+    ["g",0],
+    ["wk",1,"SSSS"],
+    ["p"],
+    ["cw",1,"V"],
+    ["qw",0],
+    ["x",2,"V"],
+    ["x",1,"V"],
+    ["x",0,"V"],
+    ["g",1],
+    ["g",2],
+    ["x",3,"V"],
+    ["qw",1],
+    ["V",2],
+    ["V",1],
+    ["wk",0,"SSVS"],
+    ["wk",2,"SSSS"],
+    ["v",1,1,"S"],
+    ["wk",3,"VVVS"],
+    ["v",2,1,"S"],
+    ["v",2,0,"S"],
+    ["V",0],
+    ["V",3],
+    ["v",0,1,"S"],
+    ["v",3,0,"S"],
+    ["v",0,0,"V"],
+    ["qx",0],
+    ["qwk",0],
+    ["v",3,1,"S"],
+    ["qwk",1],
+    ["v",1,0,"S"],
+    ["k",0,3,"S"],
+    ["qx",1],
+    ["k",2,3,"S"],
+    ["k",0,1,"V"],
+    ["q",0,1,"S"],
+    ["k",0,0,"V"],
+    ["k",0,2,"S"],
+    ["k",1,3,"S"],
+    ["k",2,0,"V"],
+    ["qk",0],
+    ["q",0,0,"S"],
+    ["qq",0],
+    ["k",1,0,"V"],
+    ["k",1,2,"V"],
+    ["s",0,0,1],
+    ["q",1,0,"S"],
+    ["k",1,1,"V"],
+    ["q",1,1,"S"],
+    ["k",2,2,"S"],
+    ["k",2,1,"V"],
+    ["qk",1],
+    ["s",1,0,1],
+    ["qq",1],
+    ["k",3,0,"V"],
+    ["s",0,1,1],
+    ["qk",2],
+    ["s",1,1,1],
+    ["k",3,2,"V"],
+    ["k",3,3,"V"],
+    ["k",3,1,"V"],
+    ["s",2,0,1],
+    ["qk",3],
+    ["s",3,1,1],
+    ["s",2,1,1],
+    ["s",3,0,1],
+]
+
+
+def tile_list_kvt_dl_sig_kernel(
+    tc, tab_words, tab_scales, x, wq_words, wq_scales, wk, wv4_words, wv4_scales, wvd, offs, out_0, out_1
+):
+    nc = tc.nc
+    with ExitStack() as ctx:
+        keep = ctx.enter_context(tc.tile_pool(name="keep", bufs=1))
+        shared = ctx.enter_context(tc.tile_pool(name="shared", bufs=1))
+        psum = ctx.enter_context(tc.psum_pool(name="psum", bufs=1))
+
+        def copy_on(engine, out, in_):
+            if engine == "S":
+                nc.scalar.copy(out=out, in_=in_)
+            elif engine == "G":
+                nc.gpsimd.tensor_copy(out=out, in_=in_)
+            else:
+                nc.vector.tensor_copy(out=out, in_=in_)
+
+        offsets = keep.tile([P, J // 16], U16, name="offsets")
+        nc.sync.dma_start(offsets[:], offs)
+
+        wv4_sc = keep.tile([P, PASSES, N // 4], I32, name="wv4_sc", align_bytes=64)
+        wq_sc_raw = keep.tile([P, PASSES, R // 4], I32, name="wq_sc_raw", align_bytes=64)
+        tsc_win = shared.tile([P, T // 4], I32, name="tsc_win", offset=34 * KIB)
+        planes = keep.tile([P, PASSES, J // 4], I32, name="planes", align_bytes=64)
+        warm = keep.tile([P, 8], F32, name="warm")
+        nc.vector.memset(wv4_sc[:], 0)
+        nc.vector.memset(wq_sc_raw[:], 0)
+        nc.vector.memset(warm[:, 0:1], 0.0)
+        nc.scalar.activation(out=warm[:, 1:2], in_=warm[:, 0:1], func=SIGMOID)
+        nc.vector.memset(tsc_win[32:64, :], 0)
+        nc.vector.memset(tsc_win[64:128, :], 0)
+        nc.gpsimd.memset(planes[:], 0)
+
+        nc.sync.dma_start(tsc_win[0:32, :], tab_scales.rearrange("a q t -> (a q) t").bitcast(I32))
+        tab_win = [
+            shared.tile([P, T], I32, name="tab_win0", offset=14 * KIB),
+            shared.tile([P, T], I32, name="tab_win1", offset=(34 if "tab1" in LOADS[1] else 38) * KIB),
+        ]
+        wv4_w = keep.tile([P, PASSES, N // 2], I32, name="wv4_w", align_bytes=64)
+        wvd_raw = keep.tile([P, PASSES, 4, N], F32, name="wvd_raw")
+        wk_raw = shared.tile([P, PASSES, 2, 4, R // 2], F32, name="wk_raw", offset=0)
+        wq_raw = shared.tile([P, PASSES, R // 2], I32, name="wq_raw", offset=16 * KIB)
+        x_raw = shared.tile([P, 2, PASSES, 4, M // 2], F32, name="x_raw", offset=18 * KIB)
+
+        def load(what):
+            if what in ("tab0", "tab1"):
+                a = int(what[3])
+                nc.sync.dma_start(tab_win[a][:], tab_words[a].rearrange("p t i -> p (t i)").bitcast(I32))
+            elif what == "wv4w":
+                nc.sync.dma_start(wv4_w[:], wv4_words.rearrange("a p b -> p a b").bitcast(I32))
+            elif what == "w4s":
+                for q in range(4):
+                    nc.sync.dma_start(
+                        wv4_sc[32 * q : 32 * q + 4],
+                        wv4_scales[:, 4 * q : 4 * q + 4, :].rearrange("a r n -> r a n").bitcast(I32),
+                    )
+            elif what == "wvd":
+                nc.sync.dma_start(
+                    wvd_raw[:].rearrange("p a j n -> p a (j n)"), wvd.rearrange("(a p j) n -> p a (j n)", a=PASSES, j=4)
+                )
+            elif what in ("wvd0", "wvd1"):
+                a = int(what[3])
+                nc.sync.dma_start(wvd_raw[:, a], wvd[512 * a : 512 * (a + 1), :].rearrange("(p j) n -> p j n", j=4))
+            elif what == "wq":
+                nc.sync.dma_start(wq_raw[:], wq_words.rearrange("a p b -> p a b").bitcast(I32))
+            elif what[0] == "w":
+                a, h = divmod(int(what[2]), 2)
+                nc.sync.dma_start(
+                    wk_raw[:, a, h], wk[512 * a : 512 * (a + 1), 256 * h : 256 * (h + 1)].rearrange("(p j) n -> p j n", j=4)
+                )
+            else:
+                h, a = divmod(int(what[1]), 2)
+                nc.sync.dma_start(
+                    x_raw[:, h, a], x[512 * a : 512 * (a + 1), 256 * h : 256 * (h + 1)].rearrange("(p j) n -> p j n", j=4)
+                )
+
+        for what in LOADS[0]:
+            load(what)
+        for q in range(4):
+            nc.gpsimd.dma_start(
+                wq_sc_raw[32 * q : 32 * q + 4], wq_scales[:, 4 * q : 4 * q + 4, :].rearrange("a r n -> r a n").bitcast(I32)
+            )
+
+        tsc_g = keep.tile([P, J // 4], I32, name="tsc_g", align_bytes=64)
+        nc.vector.tensor_copy(tsc_g[:].bitcast(U8), tsc_win[:].bitcast(U8).indirect(offsets[:]))
+        for a in range(PASSES):
+            for q in range(4):
+                queue = nc.scalar if MOVES[a] == "S" else nc.gpsimd
+                queue.dma_start(planes[32 * q : 32 * q + 4, a, :], tsc_g[16 * a + 4 * q : 16 * a + 4 * q + 4, :])
+            if a == 0:
+                for what in LOADS[1]:
+                    load(what)
+
+        tab_g = keep.tile([P, PASSES, J], I32, name="tab_g", align_bytes=64)
+
+        def gather(a, c):
+            nc.vector.tensor_copy(
+                tab_g[:, a, c * CH : (c + 1) * CH].bitcast(U32),
+                tab_win[a][:].bitcast(U32).indirect(offsets[:, c * CH // 16 : (c + 1) * CH // 16]),
+            )
+
+        def tab_operand(a, j0, width):
+            return tab_g[:, a, j0 : j0 + width].bitcast(FP8X4), planes[:, a, j0 // 4 : (j0 + width) // 4].bitcast(U8)
+
+        def interleave(engine, dst, src):
+            copy_on(engine, dst.rearrange("p (c i j) -> p c j i", i=4, j=4), src.rearrange("p j (c i) -> p c j i", i=4))
+
+        bank_count = [0]
+
+        def next_bank():
+            b = bank_count[0] % 8
+            bank_count[0] += 1
+            return psum.tile([P, CH], F32, name="bank", tag="bank%d" % b)
+
+        for c in range(NCH):
+            gather(0, c)
+        for what in LOADS[2]:
+            load(what)
+
+        wq_w = keep.tile([P, 4, PASSES, 64], I32, name="wq_w", align_bytes=64)
+        wq_sc = keep.tile([P, 4, PASSES, 32], I32, name="wq_sc", align_bytes=64)
+        nc.gpsimd.tensor_copy(
+            out=wq_sc[:].rearrange("p t a g -> p t (a g)"),
+            in_=wq_sc_raw[:].rearrange("p a (g t) -> p t (a g)", t=4),
+        )
+        wvd_bf = keep.tile([P, PASSES, 4 * N], BF16, name="wvd_bf", align_bytes=64)
+        wvd_c = keep.tile([P, PASSES, N], U32, name="wvd_c", align_bytes=64)
+        wvd_s = keep.tile([P, PASSES, N], U8, name="wvd_s", align_bytes=64)
+        wk_bf = keep.tile([P, PASSES, 4, 4 * P], BF16, name="wk_bf", align_bytes=64)
+        wk_c = keep.tile([P, PASSES, R], U32, name="wk_c", align_bytes=64)
+        wk_s = keep.tile([P, PASSES, R], U8, name="wk_s", align_bytes=64)
+        x_bf = keep.tile([P, 2, PASSES, 4 * 256], BF16, name="x_bf", align_bytes=64)
+        x_c = keep.tile([P, 2, PASSES, 256], U32, name="x_c", align_bytes=64)
+        x_s = keep.tile([P, 2, PASSES, 256], U8, name="x_s", align_bytes=64)
+        vv_sb = keep.tile([P, 2, J], F32, name="vv_sb")
+        k_bf = keep.tile([P, NCH, 4 * CH], BF16, name="k_bf", align_bytes=64)
+        k_c = keep.tile([P, J], U32, name="k_c", align_bytes=64)
+        k_s = keep.tile([P, J], U8, name="k_s", align_bytes=64)
+        q_bf = keep.tile([P, 2, 4 * 256], BF16, name="q_bf", align_bytes=64)
+        q_c = keep.tile([P, M], U32, name="q_c", align_bytes=64)
+        q_s = keep.tile([P, M], U8, name="q_s", align_bytes=64)
+        sc_sb = keep.tile([P, NCH, 4, CH], F32, name="sc_sb")
+        vv_bank = {}
+        vv_done = set()
+
+        def chain_out(engine, dst, bank):
+            copy_on(engine, dst.rearrange("p (n t) -> p n t", t=4), bank[:].rearrange("p (t n) -> p n t", t=4))
+
+        for step in ORDER:
+            kind = step[0]
+            if kind == "g":
+                gather(1, step[1])
+            elif kind == "cw":
+                interleave(step[2], wvd_bf[:, step[1]], wvd_raw[:, step[1]])
+            elif kind == "qw":
+                a = step[1]
+                nc.vector.quantize_mx(out=wvd_c[:, a].bitcast(FP8X4), scales=wvd_s[:, a], in_=wvd_bf[:, a])
+            elif kind == "wk":
+                a, h = divmod(step[1], 2)
+                src = wk_raw[:, a, h].rearrange("p j (g t i) -> p t g j i", t=4, i=4)
+                for t in range(4):
+                    dst = wk_bf[:, a, t, 256 * h : 256 * (h + 1)].rearrange("p (g i j) -> p g j i", i=4, j=4)
+                    copy_on(step[2][t], dst, src[:, t])
+            elif kind == "qwk":
+                a = step[1]
+                nc.vector.quantize_mx(
+                    out=wk_c[:, a].bitcast(FP8X4), scales=wk_s[:, a], in_=wk_bf[:, a].rearrange("p t c -> p (t c)")
+                )
+            elif kind == "V":
+                c = step[1]
+                vv_bank[c] = [next_bank() for nt in range(2)]
+                for a in range(PASSES):
+                    rhs, rhs_sc = tab_operand(a, c * CH, CH)
+                    for nt in range(2):
+                        nc.tensor.matmul_mx(
+                            out=vv_bank[c][nt][:],
+                            lhsT=wv4_w[:, a, 64 * nt : 64 * (nt + 1)].bitcast(FP4X4),
+                            lhsT_scale=wv4_sc[:, a, 32 * nt : 32 * (nt + 1)].bitcast(U8),
+                            rhs=rhs, rhs_scale=rhs_sc, start=(a == 0), stop=False,
+                        )
+                    for nt in range(2):
+                        nc.tensor.matmul_mx(
+                            out=vv_bank[c][nt][:],
+                            lhsT=wvd_c[:, a, P * nt : P * (nt + 1)].bitcast(FP8X4),
+                            lhsT_scale=wvd_s[:, a, P * nt : P * (nt + 1)],
+                            rhs=rhs, rhs_scale=rhs_sc, start=False, stop=(a == PASSES - 1),
+                        )
+            elif kind == "v":
+                c, nt = step[1], step[2]
+                copy_on(step[3], vv_sb[:, nt, c * CH : (c + 1) * CH], vv_bank[c][nt][:])
+                vv_done.add((c, nt))
+                if (c ^ 1, nt) in vv_done:
+                    cols = slice((c // 2) * 2 * CH, (c // 2 + 1) * 2 * CH)
+                    nc.sync.dma_start(out_1[P * nt : P * (nt + 1), cols], vv_sb[:, nt, cols])
+            elif kind == "x":
+                h, a = divmod(step[1], 2)
+                interleave(step[2], x_bf[:, h, a], x_raw[:, h, a])
+            elif kind == "qx":
+                h = step[1]
+                nc.vector.quantize_mx(
+                    out=x_c[:, h].rearrange("p a m -> p (a m)").bitcast(FP8X4),
+                    scales=x_s[:, h].rearrange("p a m -> p (a m)"),
+                    in_=x_bf[:, h].rearrange("p a m -> p (a m)"),
+                )
+            elif kind == "p":
+                nc.vector.tensor_copy(
+                    out=wq_w[:].rearrange("p t a (g w) -> p t (a g) w", w=2),
+                    in_=wq_raw[:].rearrange("p a (g t w) -> p t (a g) w", t=4, w=2),
+                )
+            elif kind == "k":
+                c, u = step[1], step[2]
+                bank = next_bank()
+                for t in range(4):
+                    for a in range(PASSES):
+                        rhs, rhs_sc = tab_operand(a, c * CH + u * P, P)
+                        nc.tensor.matmul_mx(
+                            out=bank[:, t * P : (t + 1) * P],
+                            lhsT=wk_c[:, a, t * P : (t + 1) * P].bitcast(FP8X4),
+                            lhsT_scale=wk_s[:, a, t * P : (t + 1) * P],
+                            rhs=rhs, rhs_scale=rhs_sc, start=(a == 0), stop=(a == PASSES - 1),
+                        )
+                chain_out(step[3], k_bf[:, c, u * CH : (u + 1) * CH], bank)
+            elif kind == "qk":
+                cols = slice(step[1] * CH, (step[1] + 1) * CH)
+                nc.vector.quantize_mx(out=k_c[:, cols].bitcast(FP8X4), scales=k_s[:, cols], in_=k_bf[:, step[1]])
+            elif kind == "q":
+                h, u = step[1], step[2]
+                bank = next_bank()
+                for t in range(4):
+                    for a in range(PASSES):
+                        nc.tensor.matmul_mx(
+                            out=bank[:, t * P : (t + 1) * P],
+                            lhsT=wq_w[:, t, a].bitcast(FP4X4),
+                            lhsT_scale=wq_sc[:, t, a].bitcast(U8),
+                            rhs=x_c[:, h, a, u * P : (u + 1) * P].bitcast(FP8X4),
+                            rhs_scale=x_s[:, h, a, u * P : (u + 1) * P],
+                            start=(a == 0), stop=(a == PASSES - 1),
+                        )
+                chain_out(step[3], q_bf[:, h, u * CH : (u + 1) * CH], bank)
+            elif kind == "qq":
+                cols = slice(step[1] * 256, (step[1] + 1) * 256)
+                nc.vector.quantize_mx(out=q_c[:, cols].bitcast(FP8X4), scales=q_s[:, cols], in_=q_bf[:, step[1]])
+            else:
+                c, h, split = step[1], step[2], step[3]
+                cols = slice(c * CH, (c + 1) * CH)
+                for mt in (2 * h, 2 * h + 1):
+                    bank = next_bank()
+                    nc.tensor.matmul_mx(
+                        out=bank[:],
+                        lhsT=q_c[:, mt * P : (mt + 1) * P].bitcast(FP8X4),
+                        lhsT_scale=q_s[:, mt * P : (mt + 1) * P],
+                        rhs=k_c[:, cols].bitcast(FP8X4), rhs_scale=k_s[:, cols], start=True, stop=True,
+                    )
+                    nc.scalar.activation(out=sc_sb[:, c, mt], in_=bank[:], func=SIGMOID, scale=0.03125)
+                    if split:
+                        nc.sync.dma_start(out_0[mt * P : (mt + 1) * P, cols], sc_sb[:, c, mt])
+                if not split:
+                    nc.sync.dma_start(
+                        out_0[h * 256 : (h + 1) * 256, cols].rearrange("(u p) n -> p u n", p=P),
+                        sc_sb[:, c, 2 * h : 2 * h + 2],
+                    )

@@ -20,76 +20,79 @@ PASSES = K // 512
 CH = 512
 NCH = J // CH
 KIB = 1024
-MOVES = "SG"
-LOADS = [["tab0","wv4w","w4s","wvd0","tab1","wvd1"],[],["wk0","wk1","wk2","wk3","wq","x0","x1","x2","x3"]]
+WV4_AT = J // 4
+WQ_AT = WV4_AT + N // 4
+PLANE = WQ_AT + R // 4
+MOVES = "SS"
+LOADS = [["tab0","wv4w","wvd","tab1"],[],["wk0","wk1","wk2","wk3","wq","x0","x1","x2","x3"]]
 ORDER = [
-    ["cw",0,"V"],
-    ["g",3],
-    ["g",0],
-    ["wk",1,"SSSS"],
-    ["p"],
-    ["cw",1,"V"],
+    ["cw",0,"S"],
     ["qw",0],
-    ["x",2,"V"],
-    ["x",1,"V"],
-    ["x",0,"V"],
+    ["cw",1,"S"],
+    ["g",0],
     ["g",1],
-    ["g",2],
-    ["x",3,"V"],
     ["qw",1],
-    ["V",2],
-    ["V",1],
-    ["wk",0,"SSVS"],
-    ["wk",2,"SSSS"],
-    ["v",1,1,"S"],
-    ["wk",3,"VVVS"],
-    ["v",2,1,"S"],
-    ["v",2,0,"S"],
+    ["g",2],
+    ["g",3],
     ["V",0],
+    ["V",1],
+    ["V",2],
     ["V",3],
-    ["v",0,1,"S"],
-    ["v",3,0,"S"],
-    ["v",0,0,"V"],
-    ["qx",0],
+    ["wk",0,"SSSS"],
+    ["wk",1,"SSSS"],
     ["qwk",0],
-    ["v",3,1,"S"],
+    ["wk",2,"VVSS"],
+    ["wk",3,"VVVS"],
     ["qwk",1],
+    ["v",0,0,"S"],
+    ["v",0,1,"S"],
     ["v",1,0,"S"],
-    ["k",0,3,"S"],
-    ["qx",1],
-    ["k",2,3,"S"],
-    ["k",0,1,"V"],
-    ["q",0,1,"S"],
-    ["k",0,0,"V"],
+    ["v",1,1,"S"],
+    ["x",0,"V"],
+    ["x",1,"V"],
+    ["qx",0],
+    ["p"],
+    ["v",2,0,"S"],
+    ["v",2,1,"S"],
+    ["k",0,0,"S"],
+    ["k",0,1,"S"],
     ["k",0,2,"S"],
-    ["k",1,3,"S"],
-    ["k",2,0,"V"],
+    ["k",0,3,"S"],
     ["qk",0],
     ["q",0,0,"S"],
+    ["q",0,1,"S"],
     ["qq",0],
-    ["k",1,0,"V"],
-    ["k",1,2,"V"],
-    ["s",0,0,1],
-    ["q",1,0,"S"],
+    ["x",2,"V"],
+    ["x",3,"V"],
+    ["qx",1],
+    ["v",3,0,"V"],
+    ["v",3,1,"V"],
+    ["k",1,0,"S"],
     ["k",1,1,"V"],
-    ["q",1,1,"S"],
-    ["k",2,2,"S"],
-    ["k",2,1,"V"],
+    ["s",0,0,1],
+    ["k",1,2,"S"],
+    ["k",1,3,"V"],
     ["qk",1],
-    ["s",1,0,1],
+    ["q",1,0,"V"],
+    ["q",1,1,"S"],
     ["qq",1],
-    ["k",3,0,"V"],
-    ["s",0,1,1],
+    ["k",2,0,"V"],
+    ["k",2,1,"S"],
+    ["s",1,0,1],
+    ["k",2,2,"V"],
+    ["k",2,3,"V"],
     ["qk",2],
+    ["s",0,1,1],
+    ["k",3,0,"V"],
+    ["k",3,1,"V"],
     ["s",1,1,1],
     ["k",3,2,"V"],
     ["k",3,3,"V"],
-    ["k",3,1,"V"],
-    ["s",2,0,1],
     ["qk",3],
-    ["s",3,1,1],
+    ["s",2,0,1],
     ["s",2,1,1],
     ["s",3,0,1],
+    ["s",3,1,1],
 ]
 
 
@@ -113,13 +116,11 @@ def tile_list_kvt_dl_sig_kernel(
         offsets = keep.tile([P, J // 16], U16, name="offsets")
         nc.sync.dma_start(offsets[:], offs)
 
-        wv4_sc = keep.tile([P, PASSES, N // 4], I32, name="wv4_sc", align_bytes=64)
-        wq_sc_raw = keep.tile([P, PASSES, R // 4], I32, name="wq_sc_raw", align_bytes=64)
-        tsc_win = shared.tile([P, T // 4], I32, name="tsc_win", offset=34 * KIB)
-        planes = keep.tile([P, PASSES, J // 4], I32, name="planes", align_bytes=64)
+        rows = keep.tile([32, PLANE], I32, name="rows", align_bytes=64)
+        wq_rows = keep.tile([32, R // 4], I32, name="wq_rows", align_bytes=64)
+        tsc_win = keep.tile([P, T // 4], I32, name="tsc_win", align_bytes=64)
+        planes = keep.tile([P, PASSES, PLANE], I32, name="planes", align_bytes=64)
         warm = keep.tile([P, 8], F32, name="warm")
-        nc.vector.memset(wv4_sc[:], 0)
-        nc.vector.memset(wq_sc_raw[:], 0)
         nc.vector.memset(warm[:, 0:1], 0.0)
         nc.scalar.activation(out=warm[:, 1:2], in_=warm[:, 0:1], func=SIGMOID)
         nc.vector.memset(tsc_win[32:64, :], 0)
@@ -127,15 +128,18 @@ def tile_list_kvt_dl_sig_kernel(
         nc.gpsimd.memset(planes[:], 0)
 
         nc.sync.dma_start(tsc_win[0:32, :], tab_scales.rearrange("a q t -> (a q) t").bitcast(I32))
+        nc.sync.dma_start(wq_rows[:], wq_scales.rearrange("a q r -> (a q) r").bitcast(I32))
+        nc.sync.dma_start(rows[:, WV4_AT:WQ_AT], wv4_scales.rearrange("a q n -> (a q) n").bitcast(I32))
         tab_win = [
             shared.tile([P, T], I32, name="tab_win0", offset=14 * KIB),
-            shared.tile([P, T], I32, name="tab_win1", offset=(34 if "tab1" in LOADS[1] else 38) * KIB),
+            shared.tile([P, T], I32, name="tab_win1", offset=(35 if "tab1" in LOADS[1] else 39) * KIB),
         ]
         wv4_w = keep.tile([P, PASSES, N // 2], I32, name="wv4_w", align_bytes=64)
         wvd_raw = keep.tile([P, PASSES, 4, N], F32, name="wvd_raw")
-        wk_raw = shared.tile([P, PASSES, 2, 4, R // 2], F32, name="wk_raw", offset=0)
+        wk_all = shared.tile([P, 4, 4, R // 2], F32, name="wk_all", offset=0)
+        wk_raw = [wk_all[:, i] for i in range(4)]
         wq_raw = shared.tile([P, PASSES, R // 2], I32, name="wq_raw", offset=16 * KIB)
-        x_raw = shared.tile([P, 2, PASSES, 4, M // 2], F32, name="x_raw", offset=18 * KIB)
+        x_raw = shared.tile([P, 2, PASSES, 4, M // 2], F32, name="x_raw", offset=19 * KIB)
 
         def load(what):
             if what in ("tab0", "tab1"):
@@ -143,12 +147,6 @@ def tile_list_kvt_dl_sig_kernel(
                 nc.sync.dma_start(tab_win[a][:], tab_words[a].rearrange("p t i -> p (t i)").bitcast(I32))
             elif what == "wv4w":
                 nc.sync.dma_start(wv4_w[:], wv4_words.rearrange("a p b -> p a b").bitcast(I32))
-            elif what == "w4s":
-                for q in range(4):
-                    nc.sync.dma_start(
-                        wv4_sc[32 * q : 32 * q + 4],
-                        wv4_scales[:, 4 * q : 4 * q + 4, :].rearrange("a r n -> r a n").bitcast(I32),
-                    )
             elif what == "wvd":
                 nc.sync.dma_start(
                     wvd_raw[:].rearrange("p a j n -> p a (j n)"), wvd.rearrange("(a p j) n -> p a (j n)", a=PASSES, j=4)
@@ -161,7 +159,7 @@ def tile_list_kvt_dl_sig_kernel(
             elif what[0] == "w":
                 a, h = divmod(int(what[2]), 2)
                 nc.sync.dma_start(
-                    wk_raw[:, a, h], wk[512 * a : 512 * (a + 1), 256 * h : 256 * (h + 1)].rearrange("(p j) n -> p j n", j=4)
+                    wk_raw[2 * a + h], wk[512 * a : 512 * (a + 1), 256 * h : 256 * (h + 1)].rearrange("(p j) n -> p j n", j=4)
                 )
             else:
                 h, a = divmod(int(what[1]), 2)
@@ -171,17 +169,17 @@ def tile_list_kvt_dl_sig_kernel(
 
         for what in LOADS[0]:
             load(what)
-        for q in range(4):
-            nc.gpsimd.dma_start(
-                wq_sc_raw[32 * q : 32 * q + 4], wq_scales[:, 4 * q : 4 * q + 4, :].rearrange("a r n -> r a n").bitcast(I32)
-            )
 
-        tsc_g = keep.tile([P, J // 4], I32, name="tsc_g", align_bytes=64)
+        nc.vector.tensor_copy(
+            out=rows[:, WQ_AT:PLANE].rearrange("p (t g) -> p t g", t=4), in_=wq_rows[:].rearrange("p (g t) -> p t g", t=4)
+        )
+        tsc_g = shared.tile([P, J // 4], I32, name="tsc_g", offset=35 * KIB)
         nc.vector.tensor_copy(tsc_g[:].bitcast(U8), tsc_win[:].bitcast(U8).indirect(offsets[:]))
+        nc.vector.tensor_copy(out=rows[:, 0:WV4_AT], in_=tsc_g[0:32, :])
         for a in range(PASSES):
             for q in range(4):
                 queue = nc.scalar if MOVES[a] == "S" else nc.gpsimd
-                queue.dma_start(planes[32 * q : 32 * q + 4, a, :], tsc_g[16 * a + 4 * q : 16 * a + 4 * q + 4, :])
+                queue.dma_start(planes[32 * q : 32 * q + 4, a, :], rows[16 * a + 4 * q : 16 * a + 4 * q + 4, :])
             if a == 0:
                 for what in LOADS[1]:
                     load(what)
@@ -213,11 +211,6 @@ def tile_list_kvt_dl_sig_kernel(
             load(what)
 
         wq_w = keep.tile([P, 4, PASSES, 64], I32, name="wq_w", align_bytes=64)
-        wq_sc = keep.tile([P, 4, PASSES, 32], I32, name="wq_sc", align_bytes=64)
-        nc.gpsimd.tensor_copy(
-            out=wq_sc[:].rearrange("p t a g -> p t (a g)"),
-            in_=wq_sc_raw[:].rearrange("p a (g t) -> p t (a g)", t=4),
-        )
         wvd_bf = keep.tile([P, PASSES, 4 * N], BF16, name="wvd_bf", align_bytes=64)
         wvd_c = keep.tile([P, PASSES, N], U32, name="wvd_c", align_bytes=64)
         wvd_s = keep.tile([P, PASSES, N], U8, name="wvd_s", align_bytes=64)
@@ -252,7 +245,7 @@ def tile_list_kvt_dl_sig_kernel(
                 nc.vector.quantize_mx(out=wvd_c[:, a].bitcast(FP8X4), scales=wvd_s[:, a], in_=wvd_bf[:, a])
             elif kind == "wk":
                 a, h = divmod(step[1], 2)
-                src = wk_raw[:, a, h].rearrange("p j (g t i) -> p t g j i", t=4, i=4)
+                src = wk_raw[step[1]].rearrange("p j (g t i) -> p t g j i", t=4, i=4)
                 for t in range(4):
                     dst = wk_bf[:, a, t, 256 * h : 256 * (h + 1)].rearrange("p (g i j) -> p g j i", i=4, j=4)
                     copy_on(step[2][t], dst, src[:, t])
@@ -270,7 +263,7 @@ def tile_list_kvt_dl_sig_kernel(
                         nc.tensor.matmul_mx(
                             out=vv_bank[c][nt][:],
                             lhsT=wv4_w[:, a, 64 * nt : 64 * (nt + 1)].bitcast(FP4X4),
-                            lhsT_scale=wv4_sc[:, a, 32 * nt : 32 * (nt + 1)].bitcast(U8),
+                            lhsT_scale=planes[:, a, WV4_AT + 32 * nt : WV4_AT + 32 * (nt + 1)].bitcast(U8),
                             rhs=rhs, rhs_scale=rhs_sc, start=(a == 0), stop=False,
                         )
                     for nt in range(2):
@@ -326,7 +319,7 @@ def tile_list_kvt_dl_sig_kernel(
                         nc.tensor.matmul_mx(
                             out=bank[:, t * P : (t + 1) * P],
                             lhsT=wq_w[:, t, a].bitcast(FP4X4),
-                            lhsT_scale=wq_sc[:, t, a].bitcast(U8),
+                            lhsT_scale=planes[:, a, WQ_AT + 32 * t : WQ_AT + 32 * (t + 1)].bitcast(U8),
                             rhs=x_c[:, h, a, u * P : (u + 1) * P].bitcast(FP8X4),
                             rhs_scale=x_s[:, h, a, u * P : (u + 1) * P],
                             start=(a == 0), stop=(a == PASSES - 1),

@@ -24,75 +24,78 @@ WV4_AT = J // 4
 WQ_AT = WV4_AT + N // 4
 PLANE = WQ_AT + R // 4
 MOVES = "SS"
-LOADS = [["tab0","wv4w","wvd","tab1"],[],["wk0","wk1","wk2","wk3","wq","x0","x1","x2","x3"]]
+LOADS = [["tab0","wv4w","wvd0","tab1","wvd1","wk0","wk1","wk2","wk3","wq","x0","x1","x2","x3"],[],[]]
 ORDER = [
-    ["cw",0,"S"],
-    ["qw",0],
-    ["cw",1,"S"],
     ["g",0],
+    ["wk",3,"VVVV"],
     ["g",1],
-    ["qw",1],
+    ["cw",0,"S"],
+    ["cw",1,"V"],
     ["g",2],
+    ["wk",2,"VSSS"],
     ["g",3],
-    ["V",0],
+    ["p"],
+    ["qw",0],
+    ["x",0,"S"],
+    ["x",1,"V"],
+    ["qw",1],
     ["V",1],
-    ["V",2],
-    ["V",3],
-    ["wk",0,"SSSS"],
-    ["wk",1,"SSSS"],
-    ["qwk",0],
-    ["wk",2,"VVSS"],
-    ["wk",3,"VVVS"],
+    ["x",3,"V"],
     ["qwk",1],
+    ["V",0],
+    ["V",3],
     ["v",0,0,"S"],
-    ["v",0,1,"S"],
+    ["wk",1,"SSSV"],
+    ["qx",0],
+    ["V",2],
+    ["v",0,1,"V"],
     ["v",1,0,"S"],
     ["v",1,1,"S"],
-    ["x",0,"V"],
-    ["x",1,"V"],
-    ["qx",0],
-    ["p"],
-    ["v",2,0,"S"],
-    ["v",2,1,"S"],
-    ["k",0,0,"S"],
-    ["k",0,1,"S"],
-    ["k",0,2,"S"],
-    ["k",0,3,"S"],
-    ["qk",0],
-    ["q",0,0,"S"],
-    ["q",0,1,"S"],
-    ["qq",0],
-    ["x",2,"V"],
-    ["x",3,"V"],
+    ["wk",0,"VSSS"],
+    ["v",2,0,"V"],
+    ["v",3,0,"S"],
+    ["qwk",0],
+    ["k",0,2,"V"],
+    ["v",3,1,"S"],
+    ["x",2,"S"],
     ["qx",1],
-    ["v",3,0,"V"],
-    ["v",3,1,"V"],
-    ["k",1,0,"S"],
+    ["k",1,2,"V"],
     ["k",1,1,"V"],
-    ["s",0,0,1],
-    ["k",1,2,"S"],
-    ["k",1,3,"V"],
+    ["k",0,1,"V"],
+    ["q",0,1,"V"],
+    ["k",1,0,"S"],
+    ["v",2,1,"S"],
+    ["q",0,0,"S"],
+    ["k",1,3,"S"],
+    ["k",0,3,"S"],
     ["qk",1],
+    ["k",0,0,"S"],
+    ["k",2,1,"S"],
     ["q",1,0,"V"],
-    ["q",1,1,"S"],
+    ["qq",0],
+    ["qk",0],
+    ["k",2,3,"S"],
+    ["q",1,1,"V"],
+    ["s",0,0,1],
+    ["s",1,0,1],
     ["qq",1],
     ["k",2,0,"V"],
-    ["k",2,1,"S"],
-    ["s",1,0,1],
     ["k",2,2,"V"],
-    ["k",2,3,"V"],
+    ["s",1,1,0],
+    ["s",0,1,0],
     ["qk",2],
-    ["s",0,1,1],
-    ["k",3,0,"V"],
-    ["k",3,1,"V"],
-    ["s",1,1,1],
+    ["s",2,0,0],
     ["k",3,2,"V"],
     ["k",3,3,"V"],
-    ["qk",3],
-    ["s",2,0,1],
-    ["s",2,1,1],
-    ["s",3,0,1],
-    ["s",3,1,1],
+    ["s",2,1,0],
+    ["qkh",3,1],
+    ["k",3,1,"V"],
+    ["k",3,0,"V"],
+    ["sh",3,1,1],
+    ["qkh",3,0],
+    ["sh",3,1,0],
+    ["sh",3,0,0],
+    ["sh",3,0,1],
 ]
 
 
@@ -131,15 +134,15 @@ def tile_list_kvt_dl_sig_kernel(
         nc.sync.dma_start(wq_rows[:], wq_scales.rearrange("a q r -> (a q) r").bitcast(I32))
         nc.sync.dma_start(rows[:, WV4_AT:WQ_AT], wv4_scales.rearrange("a q n -> (a q) n").bitcast(I32))
         tab_win = [
-            shared.tile([P, T], I32, name="tab_win0", offset=14 * KIB),
-            shared.tile([P, T], I32, name="tab_win1", offset=(35 if "tab1" in LOADS[1] else 39) * KIB),
+            shared.tile([P, T], I32, name="tab_win0", offset=0),
+            keep.tile([P, T], I32, name="tab_win1", align_bytes=64),
         ]
         wv4_w = keep.tile([P, PASSES, N // 2], I32, name="wv4_w", align_bytes=64)
         wvd_raw = keep.tile([P, PASSES, 4, N], F32, name="wvd_raw")
-        wk_all = shared.tile([P, 4, 4, R // 2], F32, name="wk_all", offset=0)
+        wk_all = keep.tile([P, 4, 4, R // 2], F32, name="wk_all")
         wk_raw = [wk_all[:, i] for i in range(4)]
-        wq_raw = shared.tile([P, PASSES, R // 2], I32, name="wq_raw", offset=16 * KIB)
-        x_raw = shared.tile([P, 2, PASSES, 4, M // 2], F32, name="x_raw", offset=19 * KIB)
+        wq_raw = keep.tile([P, PASSES, R // 2], I32, name="wq_raw")
+        x_raw = keep.tile([P, 2, PASSES, 4, M // 2], F32, name="x_raw")
 
         def load(what):
             if what in ("tab0", "tab1"):
@@ -173,16 +176,11 @@ def tile_list_kvt_dl_sig_kernel(
         nc.vector.tensor_copy(
             out=rows[:, WQ_AT:PLANE].rearrange("p (t g) -> p t g", t=4), in_=wq_rows[:].rearrange("p (g t) -> p t g", t=4)
         )
-        tsc_g = shared.tile([P, J // 4], I32, name="tsc_g", offset=35 * KIB)
+        tsc_g = keep.tile([P, J // 4], I32, name="tsc_g", align_bytes=64)
         nc.vector.tensor_copy(tsc_g[:].bitcast(U8), tsc_win[:].bitcast(U8).indirect(offsets[:]))
         nc.vector.tensor_copy(out=rows[:, 0:WV4_AT], in_=tsc_g[0:32, :])
-        for a in range(PASSES):
-            for q in range(4):
-                queue = nc.scalar if MOVES[a] == "S" else nc.gpsimd
-                queue.dma_start(planes[32 * q : 32 * q + 4, a, :], rows[16 * a + 4 * q : 16 * a + 4 * q + 4, :])
-            if a == 0:
-                for what in LOADS[1]:
-                    load(what)
+        for q in range(4):
+            nc.scalar.dma_start(planes[32 * q : 32 * q + 4, 0, :], rows[4 * q : 4 * q + 4, :])
 
         tab_g = keep.tile([P, PASSES, J], I32, name="tab_g", align_bytes=64)
 
@@ -207,8 +205,10 @@ def tile_list_kvt_dl_sig_kernel(
 
         for c in range(NCH):
             gather(0, c)
-        for what in LOADS[2]:
-            load(what)
+        rows_late = shared.tile([32, PLANE], I32, name="rows_late", offset=0)
+        nc.vector.tensor_copy(out=rows_late[:], in_=rows[:])
+        for q in range(4):
+            nc.scalar.dma_start(planes[32 * q : 32 * q + 4, 1, :], rows_late[16 + 4 * q : 16 + 4 * q + 4, :])
 
         wq_w = keep.tile([P, 4, PASSES, 64], I32, name="wq_w", align_bytes=64)
         wvd_bf = keep.tile([P, PASSES, 4 * N], BF16, name="wvd_bf", align_bytes=64)
@@ -251,8 +251,39 @@ def tile_list_kvt_dl_sig_kernel(
                     copy_on(step[2][t], dst, src[:, t])
             elif kind == "qwk":
                 a = step[1]
+                if a == 0:
+                    nc.vector.quantize_mx(
+                        out=wk_c[:, a].bitcast(FP8X4), scales=wk_s[:, a], in_=wk_bf[:, a].rearrange("p t c -> p (t c)")
+                    )
+                else:
+                    for t in range(4):
+                        cols = slice(t * P, (t + 1) * P)
+                        nc.vector.quantize_mx(
+                            out=wk_c[:, a, cols].bitcast(FP8X4), scales=wk_s[:, a, cols], in_=wk_bf[:, a, t]
+                        )
+            elif kind == "qkh":
+                c, half = step[1], step[2]
+                cols = slice(c * CH + half * 256, c * CH + (half + 1) * 256)
                 nc.vector.quantize_mx(
-                    out=wk_c[:, a].bitcast(FP8X4), scales=wk_s[:, a], in_=wk_bf[:, a].rearrange("p t c -> p (t c)")
+                    out=k_c[:, cols].bitcast(FP8X4), scales=k_s[:, cols], in_=k_bf[:, c, half * 1024 : (half + 1) * 1024]
+                )
+            elif kind == "sh":
+                c, half, h = step[1], step[2], step[3]
+                cols = slice(c * CH + half * 256, c * CH + (half + 1) * 256)
+                bank = next_bank()
+                for u in range(2):
+                    mt = 2 * h + u
+                    nc.tensor.matmul_mx(
+                        out=bank[:, u * 256 : (u + 1) * 256],
+                        lhsT=q_c[:, mt * P : (mt + 1) * P].bitcast(FP8X4),
+                        lhsT_scale=q_s[:, mt * P : (mt + 1) * P],
+                        rhs=k_c[:, cols].bitcast(FP8X4), rhs_scale=k_s[:, cols], start=True, stop=True,
+                    )
+                stage = sc_sb[:, c, 2 * half + h]
+                nc.scalar.activation(out=stage, in_=bank[:], func=SIGMOID, scale=0.03125)
+                nc.sync.dma_start(
+                    out_0[h * 256 : (h + 1) * 256, cols].rearrange("(u p) n -> p u n", p=P),
+                    stage.rearrange("p (u n) -> p u n", u=2),
                 )
             elif kind == "V":
                 c = step[1]

@@ -23,79 +23,79 @@ KIB = 1024
 WV4_AT = J // 4
 WQ_AT = WV4_AT + N // 4
 PLANE = WQ_AT + R // 4
-MOVES = "SS"
-LOADS = [["tab0","wv4w","wvd0","tab1","wvd1","wk0","wk1","wk2","wk3","wq","x0","x1","x2","x3"],[],[]]
+CHAIN = [(4, 0), (4, 1), (8, 0), (8, 1)]
+LOADS = [["tab0","tab1b","wv4w","wvd0"],["tab1a"],["wvd1","wk1","wk0","wk3","wk2","wq","x1","x0","x2","x3"]]
 ORDER = [
-    ["g",0],
-    ["wk",3,"VVVV"],
+    ["cw",1,"S"],
+    ["x",2,"V"],
     ["g",1],
-    ["cw",0,"S"],
-    ["cw",1,"V"],
-    ["g",2],
-    ["wk",2,"VSSS"],
-    ["g",3],
-    ["p"],
-    ["qw",0],
-    ["x",0,"S"],
-    ["x",1,"V"],
-    ["qw",1],
-    ["V",1],
-    ["x",3,"V"],
-    ["qwk",1],
-    ["V",0],
-    ["V",3],
-    ["v",0,0,"S"],
-    ["wk",1,"SSSV"],
+    ["x",1,"S"],
+    ["wk",3,"VSVV"],
+    ["x",3,"S"],
+    ["wk",1,"VVSS"],
+    ["x",0,"V"],
     ["qx",0],
+    ["wk",2,"VVSS"],
+    ["cw",0,"S"],
+    ["qw",1],
+    ["qw",0],
+    ["g",0],
+    ["g",2],
+    ["V",0],
+    ["wk",0,"SSVS"],
+    ["V",1],
     ["V",2],
+    ["v",0,0,"S"],
+    ["qwk",1],
     ["v",0,1,"V"],
-    ["v",1,0,"S"],
     ["v",1,1,"S"],
-    ["wk",0,"VSSS"],
-    ["v",2,0,"V"],
-    ["v",3,0,"S"],
     ["qwk",0],
-    ["k",0,2,"V"],
-    ["v",3,1,"S"],
-    ["x",2,"S"],
-    ["qx",1],
-    ["k",1,2,"V"],
-    ["k",1,1,"V"],
-    ["k",0,1,"V"],
-    ["q",0,1,"V"],
-    ["k",1,0,"S"],
+    ["v",1,0,"S"],
+    ["g",3],
     ["v",2,1,"S"],
-    ["q",0,0,"S"],
-    ["k",1,3,"S"],
-    ["k",0,3,"S"],
-    ["qk",1],
+    ["v",2,0,"S"],
+    ["V",3],
+    ["p"],
+    ["k",1,3,"V"],
+    ["k",3,1,"S"],
+    ["v",3,1,"V"],
+    ["v",3,0,"S"],
+    ["k",0,1,"V"],
     ["k",0,0,"S"],
-    ["k",2,1,"S"],
-    ["q",1,0,"V"],
+    ["qx",1],
+    ["q",0,1,"V"],
+    ["q",0,0,"S"],
+    ["k",1,1,"V"],
+    ["k",1,2,"V"],
+    ["k",0,3,"S"],
+    ["k",0,2,"S"],
+    ["k",3,0,"S"],
     ["qq",0],
-    ["qk",0],
-    ["k",2,3,"S"],
-    ["q",1,1,"V"],
-    ["s",0,0,1],
-    ["s",1,0,1],
-    ["qq",1],
-    ["k",2,0,"V"],
-    ["k",2,2,"V"],
-    ["s",1,1,0],
-    ["s",0,1,0],
-    ["qk",2],
-    ["s",2,0,0],
-    ["k",3,2,"V"],
-    ["k",3,3,"V"],
-    ["s",2,1,0],
-    ["qkh",3,1],
-    ["k",3,1,"V"],
-    ["k",3,0,"V"],
-    ["sh",3,1,1],
+    ["k",1,0,"S"],
     ["qkh",3,0],
-    ["sh",3,1,0],
+    ["qk",1],
+    ["q",1,0,"V"],
     ["sh",3,0,0],
+    ["qk",0],
+    ["s",0,0,1],
+    ["k",2,1,"S"],
+    ["q",1,1,"V"],
+    ["s",1,0,1],
+    ["k",2,2,"V"],
+    ["k",2,3,"V"],
+    ["qq",1],
+    ["s",0,1,1],
+    ["k",2,0,"V"],
+    ["s",1,1,1],
     ["sh",3,0,1],
+    ["k",3,3,"V"],
+    ["qk",2],
+    ["s",2,1,1],
+    ["k",3,2,"V"],
+    ["qkh",3,1],
+    ["s",2,0,1],
+    ["sh",3,1,1],
+    ["sh",3,1,0],
 ]
 
 
@@ -105,7 +105,6 @@ def tile_list_kvt_dl_sig_kernel(
     nc = tc.nc
     with ExitStack() as ctx:
         keep = ctx.enter_context(tc.tile_pool(name="keep", bufs=1))
-        shared = ctx.enter_context(tc.tile_pool(name="shared", bufs=1))
         psum = ctx.enter_context(tc.psum_pool(name="psum", bufs=1))
 
         def copy_on(engine, out, in_):
@@ -134,7 +133,7 @@ def tile_list_kvt_dl_sig_kernel(
         nc.sync.dma_start(wq_rows[:], wq_scales.rearrange("a q r -> (a q) r").bitcast(I32))
         nc.sync.dma_start(rows[:, WV4_AT:WQ_AT], wv4_scales.rearrange("a q n -> (a q) n").bitcast(I32))
         tab_win = [
-            shared.tile([P, T], I32, name="tab_win0", offset=0),
+            keep.tile([P, T], I32, name="tab_win0", align_bytes=64),
             keep.tile([P, T], I32, name="tab_win1", align_bytes=64),
         ]
         wv4_w = keep.tile([P, PASSES, N // 2], I32, name="wv4_w", align_bytes=64)
@@ -144,10 +143,22 @@ def tile_list_kvt_dl_sig_kernel(
         wq_raw = keep.tile([P, PASSES, R // 2], I32, name="wq_raw")
         x_raw = keep.tile([P, 2, PASSES, 4, M // 2], F32, name="x_raw")
 
+        wk_big = wk_all[:].rearrange("p a b c -> p (a b c)").rearrange("p (a j n) -> p a j n", a=PASSES, j=4)
+        x_big = x_raw[:].rearrange("p a b c d -> p (a b c d)").rearrange("p (a j n) -> p a j n", a=PASSES, j=4)
+
         def load(what):
             if what in ("tab0", "tab1"):
                 a = int(what[3])
                 nc.sync.dma_start(tab_win[a][:], tab_words[a].rearrange("p t i -> p (t i)").bitcast(I32))
+            elif what in ("tab1a", "tab1b"):
+                cols = slice(0, T // 2) if what == "tab1a" else slice(T // 2, T)
+                nc.sync.dma_start(tab_win[1][:, cols], tab_words[1].rearrange("p t i -> p (t i)").bitcast(I32)[:, cols])
+            elif what in ("wkA", "wkB"):
+                a = 0 if what == "wkA" else 1
+                nc.sync.dma_start(wk_big[:, a], wk[512 * a : 512 * (a + 1), :].rearrange("(p j) n -> p j n", j=4))
+            elif what in ("xA", "xB"):
+                a = 0 if what == "xA" else 1
+                nc.sync.dma_start(x_big[:, a], x[512 * a : 512 * (a + 1), :].rearrange("(p j) n -> p j n", j=4))
             elif what == "wv4w":
                 nc.sync.dma_start(wv4_w[:], wv4_words.rearrange("a p b -> p a b").bitcast(I32))
             elif what == "wvd":
@@ -179,8 +190,11 @@ def tile_list_kvt_dl_sig_kernel(
         tsc_g = keep.tile([P, J // 4], I32, name="tsc_g", align_bytes=64)
         nc.vector.tensor_copy(tsc_g[:].bitcast(U8), tsc_win[:].bitcast(U8).indirect(offsets[:]))
         nc.vector.tensor_copy(out=rows[:, 0:WV4_AT], in_=tsc_g[0:32, :])
-        for q in range(4):
-            nc.scalar.dma_start(planes[32 * q : 32 * q + 4, 0, :], rows[4 * q : 4 * q + 4, :])
+        for a in range(PASSES):
+            for q in range(4):
+                nc.sync.dma_start(planes[32 * q : 32 * q + 4, a, :], rows[16 * a + 4 * q : 16 * a + 4 * q + 4, :])
+            for what in LOADS[1 + a]:
+                load(what)
 
         tab_g = keep.tile([P, PASSES, J], I32, name="tab_g", align_bytes=64)
 
@@ -205,10 +219,6 @@ def tile_list_kvt_dl_sig_kernel(
 
         for c in range(NCH):
             gather(0, c)
-        rows_late = shared.tile([32, PLANE], I32, name="rows_late", offset=0)
-        nc.vector.tensor_copy(out=rows_late[:], in_=rows[:])
-        for q in range(4):
-            nc.scalar.dma_start(planes[32 * q : 32 * q + 4, 1, :], rows_late[16 + 4 * q : 16 + 4 * q + 4, :])
 
         wq_w = keep.tile([P, 4, PASSES, 64], I32, name="wq_w", align_bytes=64)
         wvd_bf = keep.tile([P, PASSES, 4 * N], BF16, name="wvd_bf", align_bytes=64)
@@ -249,6 +259,11 @@ def tile_list_kvt_dl_sig_kernel(
                 for t in range(4):
                     dst = wk_bf[:, a, t, 256 * h : 256 * (h + 1)].rearrange("p (g i j) -> p g j i", i=4, j=4)
                     copy_on(step[2][t], dst, src[:, t])
+            elif kind == "wK":
+                a = step[1]
+                src = wk_big[:, a].rearrange("p j (g t i) -> p t g j i", t=4, i=4)
+                for t in range(4):
+                    copy_on(step[2][t], wk_bf[:, a, t].rearrange("p (g i j) -> p g j i", i=4, j=4), src[:, t])
             elif kind == "qwk":
                 a = step[1]
                 if a == 0:
@@ -288,21 +303,18 @@ def tile_list_kvt_dl_sig_kernel(
             elif kind == "V":
                 c = step[1]
                 vv_bank[c] = [next_bank() for nt in range(2)]
-                for a in range(PASSES):
+                for n_pass, (fmt, a) in enumerate(CHAIN):
                     rhs, rhs_sc = tab_operand(a, c * CH, CH)
                     for nt in range(2):
+                        if fmt == 4:
+                            lhsT = wv4_w[:, a, 64 * nt : 64 * (nt + 1)].bitcast(FP4X4)
+                            lhsT_sc = planes[:, a, WV4_AT + 32 * nt : WV4_AT + 32 * (nt + 1)].bitcast(U8)
+                        else:
+                            lhsT = wvd_c[:, a, P * nt : P * (nt + 1)].bitcast(FP8X4)
+                            lhsT_sc = wvd_s[:, a, P * nt : P * (nt + 1)]
                         nc.tensor.matmul_mx(
-                            out=vv_bank[c][nt][:],
-                            lhsT=wv4_w[:, a, 64 * nt : 64 * (nt + 1)].bitcast(FP4X4),
-                            lhsT_scale=planes[:, a, WV4_AT + 32 * nt : WV4_AT + 32 * (nt + 1)].bitcast(U8),
-                            rhs=rhs, rhs_scale=rhs_sc, start=(a == 0), stop=False,
-                        )
-                    for nt in range(2):
-                        nc.tensor.matmul_mx(
-                            out=vv_bank[c][nt][:],
-                            lhsT=wvd_c[:, a, P * nt : P * (nt + 1)].bitcast(FP8X4),
-                            lhsT_scale=wvd_s[:, a, P * nt : P * (nt + 1)],
-                            rhs=rhs, rhs_scale=rhs_sc, start=False, stop=(a == PASSES - 1),
+                            out=vv_bank[c][nt][:], lhsT=lhsT, lhsT_scale=lhsT_sc, rhs=rhs, rhs_scale=rhs_sc,
+                            start=(n_pass == 0), stop=(n_pass == 3),
                         )
             elif kind == "v":
                 c, nt = step[1], step[2]
@@ -313,7 +325,8 @@ def tile_list_kvt_dl_sig_kernel(
                     nc.sync.dma_start(out_1[P * nt : P * (nt + 1), cols], vv_sb[:, nt, cols])
             elif kind == "x":
                 h, a = divmod(step[1], 2)
-                interleave(step[2], x_bf[:, h, a], x_raw[:, h, a])
+                src = x_big[:, a, :, 256 * h : 256 * (h + 1)] if "xA" in LOADS[2] else x_raw[:, h, a]
+                interleave(step[2], x_bf[:, h, a], src)
             elif kind == "qx":
                 h = step[1]
                 nc.vector.quantize_mx(

@@ -4,6 +4,7 @@ import concourse.mybir as mybir
 
 K, R, M, N, T, J = 1024, 512, 512, 256, 4096, 2048
 FLOPS = 2 * (K * R * M + K * R * J + R * M * J + 2 * K * N * J)
+SCORE_SCALE = 0.03125
 
 F32 = mybir.dt.float32
 BF16 = mybir.dt.bfloat16
@@ -13,90 +14,41 @@ U16 = mybir.dt.uint16
 U8 = mybir.dt.uint8
 FP8X4 = mybir.dt.float8_e4m3fn_x4
 FP4X4 = mybir.dt.float4_e2m1fn_x4
-SIGMOID = mybir.ActivationFunctionType.Sigmoid
 
 P = 128
-PASSES = K // 512
-CH = 512
-NCH = J // CH
-KIB = 1024
+PACK = 4
+PASS_K = P * PACK
+PASSES = K // PASS_K
+BLOCKS = PASS_K // 32
+BANK = 512
+BANKS = 8
+CHUNK = 512
+CHUNKS = J // CHUNK
+HALF = 256
+
 WV4_AT = J // 4
 WQ_AT = WV4_AT + N // 4
 PLANE = WQ_AT + R // 4
-CHAIN = [(4, 0), (4, 1), (8, 0), (8, 1)]
-LOADS = [["tab0","tab1b","wv4w","wvd0"],["tab1a"],["wvd1","wk1","wk0","wk3","wk2","wq","x1","x0","x2","x3"]]
-ORDER = [
-    ["cw",1,"S"],
-    ["x",2,"V"],
-    ["g",1],
-    ["x",1,"S"],
-    ["wk",3,"VSVV"],
-    ["x",3,"S"],
-    ["wk",1,"VVSS"],
-    ["x",0,"V"],
-    ["qx",0],
-    ["wk",2,"VVSS"],
-    ["cw",0,"S"],
-    ["qw",1],
-    ["qw",0],
-    ["g",0],
-    ["g",2],
-    ["V",0],
-    ["wk",0,"SSVS"],
-    ["V",1],
-    ["V",2],
-    ["v",0,0,"S"],
-    ["qwk",1],
-    ["v",0,1,"V"],
-    ["v",1,1,"S"],
-    ["qwk",0],
-    ["v",1,0,"S"],
-    ["g",3],
-    ["v",2,1,"S"],
-    ["v",2,0,"S"],
-    ["V",3],
-    ["p"],
-    ["k",1,3,"V"],
-    ["k",3,1,"S"],
-    ["v",3,1,"V"],
-    ["v",3,0,"S"],
-    ["k",0,1,"V"],
-    ["k",0,0,"S"],
-    ["qx",1],
-    ["q",0,1,"V"],
-    ["q",0,0,"S"],
-    ["k",1,1,"V"],
-    ["k",1,2,"V"],
-    ["k",0,3,"S"],
-    ["k",0,2,"S"],
-    ["k",3,0,"S"],
-    ["qq",0],
-    ["k",1,0,"S"],
-    ["qkh",3,0],
-    ["qk",1],
-    ["q",1,0,"V"],
-    ["sh",3,0,0],
-    ["qk",0],
-    ["s",0,0,1],
-    ["k",2,1,"S"],
-    ["q",1,1,"V"],
-    ["s",1,0,1],
-    ["k",2,2,"V"],
-    ["k",2,3,"V"],
-    ["qq",1],
-    ["s",0,1,1],
-    ["k",2,0,"V"],
-    ["s",1,1,1],
-    ["sh",3,0,1],
-    ["k",3,3,"V"],
-    ["qk",2],
-    ["s",2,1,1],
-    ["k",3,2,"V"],
-    ["qkh",3,1],
-    ["s",2,0,1],
-    ["sh",3,1,1],
-    ["sh",3,1,0],
-]
+
+WK_ENGINES = ("SSVS", "VVSS")
+VALUE_ENGINES = "VVSSSSVV"
+X_ENGINES = "SVVV"
+
+JOBS = (
+    ("key", 0, 0, "V"), ("key", 0, 1, "S"), ("key", 0, 2, "V"), ("key", 0, 3, "S"), ("key", 1, 0, "S"),
+    ("query", 0, 0, "S"), ("query", 0, 1, "S"), ("key", 1, 1, "S"), ("key", 1, 2, "S"),
+    ("query", 1, 0, "V"), ("key", 1, 3, "S"), ("score", 0, 0, "S"), ("query", 1, 1, "V"),
+    ("key", 2, 0, "V"), ("score", 0, 1, "S"), ("score", 1, 0, "S"),
+    ("key", 2, 1, "V"), ("score", 1, 1, "S"),
+    ("key", 2, 2, "V"), ("score", 0, 2, "S"), ("score", 0, 3, "S"),
+    ("key", 2, 3, "V"), ("score", 1, 2, "S"), ("score", 1, 3, "S"), ("score", 2, 0, "S"),
+    ("key", 3, 0, "V"), ("key", 3, 1, "V"), ("score", 2, 1, "S"),
+    ("key", 3, 2, "V"), ("score", 2, 2, "S"),
+    ("key", 3, 3, "V"), ("score", 2, 3, "S"),
+    ("last", 0, 0, "S"), ("last", 0, 1, "S"), ("last", 1, 0, "S"), ("last", 1, 1, "S"),
+)
+LAG = 2
+WQ_BEFORE, X_SECOND_BEFORE, X_SECOND_CODES_BEFORE = 2, (6, 7), 8
 
 
 def tile_list_kvt_dl_sig_kernel(
@@ -104,290 +56,263 @@ def tile_list_kvt_dl_sig_kernel(
 ):
     nc = tc.nc
     with ExitStack() as ctx:
-        keep = ctx.enter_context(tc.tile_pool(name="keep", bufs=1))
+        sbuf = ctx.enter_context(tc.tile_pool(name="sbuf", bufs=1))
         psum = ctx.enter_context(tc.psum_pool(name="psum", bufs=1))
+
+        def mx_tile(name, shape, dtype):
+            return sbuf.tile(shape, dtype, name=name, align_bytes=64)
 
         def copy_on(engine, out, in_):
             if engine == "S":
                 nc.scalar.copy(out=out, in_=in_)
-            elif engine == "G":
-                nc.gpsimd.tensor_copy(out=out, in_=in_)
             else:
                 nc.vector.tensor_copy(out=out, in_=in_)
 
-        offsets = keep.tile([P, J // 16], U16, name="offsets")
-        nc.sync.dma_start(offsets[:], offs)
+        def span(index, width):
+            return slice(index * width, (index + 1) * width)
 
-        rows = keep.tile([32, PLANE], I32, name="rows", align_bytes=64)
-        wq_rows = keep.tile([32, R // 4], I32, name="wq_rows", align_bytes=64)
-        tsc_win = keep.tile([P, T // 4], I32, name="tsc_win", align_bytes=64)
-        planes = keep.tile([P, PASSES, PLANE], I32, name="planes", align_bytes=64)
-        warm = keep.tile([P, 8], F32, name="warm")
-        nc.vector.memset(warm[:, 0:1], 0.0)
-        nc.scalar.activation(out=warm[:, 1:2], in_=warm[:, 0:1], func=SIGMOID)
-        nc.vector.memset(tsc_win[32:64, :], 0)
-        nc.vector.memset(tsc_win[64:128, :], 0)
-        nc.gpsimd.memset(planes[:], 0)
+        def k_rows(source, a, cols):
+            return source[span(a, PASS_K), cols].rearrange("(p j) n -> p j n", j=PACK)
 
-        nc.sync.dma_start(tsc_win[0:32, :], tab_scales.rearrange("a q t -> (a q) t").bitcast(I32))
-        nc.sync.dma_start(wq_rows[:], wq_scales.rearrange("a q r -> (a q) r").bitcast(I32))
-        nc.sync.dma_start(rows[:, WV4_AT:WQ_AT], wv4_scales.rearrange("a q n -> (a q) n").bitcast(I32))
-        tab_win = [
-            keep.tile([P, T], I32, name="tab_win0", align_bytes=64),
-            keep.tile([P, T], I32, name="tab_win1", align_bytes=64),
-        ]
-        wv4_w = keep.tile([P, PASSES, N // 2], I32, name="wv4_w", align_bytes=64)
-        wvd_raw = keep.tile([P, PASSES, 4, N], F32, name="wvd_raw")
-        wk_all = keep.tile([P, 4, 4, R // 2], F32, name="wk_all")
-        wk_raw = [wk_all[:, i] for i in range(4)]
-        wq_raw = keep.tile([P, PASSES, R // 2], I32, name="wq_raw")
-        x_raw = keep.tile([P, 2, PASSES, 4, M // 2], F32, name="x_raw")
+        def round_and_interleave(engine, dst, src):
+            copy_on(engine, dst.rearrange("p (c i j) -> p c j i", i=4, j=PACK), src)
 
-        wk_big = wk_all[:].rearrange("p a b c -> p (a b c)").rearrange("p (a j n) -> p a j n", a=PASSES, j=4)
-        x_big = x_raw[:].rearrange("p a b c d -> p (a b c d)").rearrange("p (a j n) -> p a j n", a=PASSES, j=4)
+        def quantise(codes, scales, values):
+            nc.vector.quantize_mx(out=codes.bitcast(FP8X4), scales=scales, in_=values)
 
-        def load(what):
-            if what in ("tab0", "tab1"):
-                a = int(what[3])
-                nc.sync.dma_start(tab_win[a][:], tab_words[a].rearrange("p t i -> p (t i)").bitcast(I32))
-            elif what in ("tab1a", "tab1b"):
-                cols = slice(0, T // 2) if what == "tab1a" else slice(T // 2, T)
-                nc.sync.dma_start(tab_win[1][:, cols], tab_words[1].rearrange("p t i -> p (t i)").bitcast(I32)[:, cols])
-            elif what in ("wkA", "wkB"):
-                a = 0 if what == "wkA" else 1
-                nc.sync.dma_start(wk_big[:, a], wk[512 * a : 512 * (a + 1), :].rearrange("(p j) n -> p j n", j=4))
-            elif what in ("xA", "xB"):
-                a = 0 if what == "xA" else 1
-                nc.sync.dma_start(x_big[:, a], x[512 * a : 512 * (a + 1), :].rearrange("(p j) n -> p j n", j=4))
-            elif what == "wv4w":
-                nc.sync.dma_start(wv4_w[:], wv4_words.rearrange("a p b -> p a b").bitcast(I32))
-            elif what == "wvd":
-                nc.sync.dma_start(
-                    wvd_raw[:].rearrange("p a j n -> p a (j n)"), wvd.rearrange("(a p j) n -> p a (j n)", a=PASSES, j=4)
-                )
-            elif what in ("wvd0", "wvd1"):
-                a = int(what[3])
-                nc.sync.dma_start(wvd_raw[:, a], wvd[512 * a : 512 * (a + 1), :].rearrange("(p j) n -> p j n", j=4))
-            elif what == "wq":
-                nc.sync.dma_start(wq_raw[:], wq_words.rearrange("a p b -> p a b").bitcast(I32))
-            elif what[0] == "w":
-                a, h = divmod(int(what[2]), 2)
-                nc.sync.dma_start(
-                    wk_raw[2 * a + h], wk[512 * a : 512 * (a + 1), 256 * h : 256 * (h + 1)].rearrange("(p j) n -> p j n", j=4)
-                )
-            else:
-                h, a = divmod(int(what[1]), 2)
-                nc.sync.dma_start(
-                    x_raw[:, h, a], x[512 * a : 512 * (a + 1), 256 * h : 256 * (h + 1)].rearrange("(p j) n -> p j n", j=4)
-                )
-
-        for what in LOADS[0]:
-            load(what)
-
-        nc.vector.tensor_copy(
-            out=rows[:, WQ_AT:PLANE].rearrange("p (t g) -> p t g", t=4), in_=wq_rows[:].rearrange("p (g t) -> p t g", t=4)
-        )
-        tsc_g = keep.tile([P, J // 4], I32, name="tsc_g", align_bytes=64)
-        nc.vector.tensor_copy(tsc_g[:].bitcast(U8), tsc_win[:].bitcast(U8).indirect(offsets[:]))
-        nc.vector.tensor_copy(out=rows[:, 0:WV4_AT], in_=tsc_g[0:32, :])
-        for a in range(PASSES):
-            for q in range(4):
-                nc.sync.dma_start(planes[32 * q : 32 * q + 4, a, :], rows[16 * a + 4 * q : 16 * a + 4 * q + 4, :])
-            for what in LOADS[1 + a]:
-                load(what)
-
-        tab_g = keep.tile([P, PASSES, J], I32, name="tab_g", align_bytes=64)
-
-        def gather(a, c):
-            nc.vector.tensor_copy(
-                tab_g[:, a, c * CH : (c + 1) * CH].bitcast(U32),
-                tab_win[a][:].bitcast(U32).indirect(offsets[:, c * CH // 16 : (c + 1) * CH // 16]),
-            )
-
-        def tab_operand(a, j0, width):
-            return tab_g[:, a, j0 : j0 + width].bitcast(FP8X4), planes[:, a, j0 // 4 : (j0 + width) // 4].bitcast(U8)
-
-        def interleave(engine, dst, src):
-            copy_on(engine, dst.rearrange("p (c i j) -> p c j i", i=4, j=4), src.rearrange("p j (c i) -> p c j i", i=4))
-
-        bank_count = [0]
+        banks_taken = []
 
         def next_bank():
-            b = bank_count[0] % 8
-            bank_count[0] += 1
-            return psum.tile([P, CH], F32, name="bank", tag="bank%d" % b)
+            banks_taken.append(psum.tile([P, BANK], F32, name="bank", tag="bank%d" % (len(banks_taken) % BANKS)))
+            return banks_taken[-1]
 
-        for c in range(NCH):
-            gather(0, c)
+        offsets = sbuf.tile([P, J // 16], U16, name="offsets")
+        nc.sync.dma_start(offsets[:], offs)
+        scale_rows = mx_tile("scale_rows", [PASSES * BLOCKS, PLANE], I32)
+        wq_scale_rows = mx_tile("wq_scale_rows", [PASSES * BLOCKS, R // 4], I32)
+        scale_window = mx_tile("scale_window", [P, T // 4], I32)
+        planes = mx_tile("planes", [P, PASSES, PLANE], I32)
+        nc.vector.memset(scale_window[32:64, :], 0)
+        nc.vector.memset(scale_window[64:128, :], 0)
+        nc.gpsimd.memset(planes[:], 0)
+        nc.sync.dma_start(scale_window[0:32, :], tab_scales.rearrange("a b t -> (a b) t").bitcast(I32))
+        nc.sync.dma_start(wq_scale_rows[:], wq_scales.rearrange("a b r -> (a b) r").bitcast(I32))
+        nc.sync.dma_start(scale_rows[:, WV4_AT:WQ_AT], wv4_scales.rearrange("a b n -> (a b) n").bitcast(I32))
 
-        wq_w = keep.tile([P, 4, PASSES, 64], I32, name="wq_w", align_bytes=64)
-        wvd_bf = keep.tile([P, PASSES, 4 * N], BF16, name="wvd_bf", align_bytes=64)
-        wvd_c = keep.tile([P, PASSES, N], U32, name="wvd_c", align_bytes=64)
-        wvd_s = keep.tile([P, PASSES, N], U8, name="wvd_s", align_bytes=64)
-        wk_bf = keep.tile([P, PASSES, 4, 4 * P], BF16, name="wk_bf", align_bytes=64)
-        wk_c = keep.tile([P, PASSES, R], U32, name="wk_c", align_bytes=64)
-        wk_s = keep.tile([P, PASSES, R], U8, name="wk_s", align_bytes=64)
-        x_bf = keep.tile([P, 2, PASSES, 4 * 256], BF16, name="x_bf", align_bytes=64)
-        x_c = keep.tile([P, 2, PASSES, 256], U32, name="x_c", align_bytes=64)
-        x_s = keep.tile([P, 2, PASSES, 256], U8, name="x_s", align_bytes=64)
-        vv_sb = keep.tile([P, 2, J], F32, name="vv_sb")
-        k_bf = keep.tile([P, NCH, 4 * CH], BF16, name="k_bf", align_bytes=64)
-        k_c = keep.tile([P, J], U32, name="k_c", align_bytes=64)
-        k_s = keep.tile([P, J], U8, name="k_s", align_bytes=64)
-        q_bf = keep.tile([P, 2, 4 * 256], BF16, name="q_bf", align_bytes=64)
-        q_c = keep.tile([P, M], U32, name="q_c", align_bytes=64)
-        q_s = keep.tile([P, M], U8, name="q_s", align_bytes=64)
-        sc_sb = keep.tile([P, NCH, 4, CH], F32, name="sc_sb")
-        vv_bank = {}
-        vv_done = set()
+        windows = [mx_tile("window%d" % a, [P, T], I32) for a in range(PASSES)]
+        wv4_codes = mx_tile("wv4_codes", [P, PASSES, N // 2], I32)
+        wvd_raw = sbuf.tile([P, PASSES, PACK, N], F32, name="wvd_raw")
+        wk_raw = sbuf.tile([P, PASSES, PACK, R], F32, name="wk_raw")
+        wq_raw = sbuf.tile([P, PASSES, R // 2], I32, name="wq_raw")
+        x_raw = sbuf.tile([P, 2, PASSES, PACK, HALF], F32, name="x_raw")
 
-        def chain_out(engine, dst, bank):
-            copy_on(engine, dst.rearrange("p (n t) -> p n t", t=4), bank[:].rearrange("p (t n) -> p n t", t=4))
+        def load_window(a, cols):
+            nc.sync.dma_start(windows[a][:, cols], tab_words[a].rearrange("p t i -> p (t i)").bitcast(I32)[:, cols])
 
-        for step in ORDER:
-            kind = step[0]
-            if kind == "g":
-                gather(1, step[1])
-            elif kind == "cw":
-                interleave(step[2], wvd_bf[:, step[1]], wvd_raw[:, step[1]])
-            elif kind == "qw":
-                a = step[1]
-                nc.vector.quantize_mx(out=wvd_c[:, a].bitcast(FP8X4), scales=wvd_s[:, a], in_=wvd_bf[:, a])
-            elif kind == "wk":
-                a, h = divmod(step[1], 2)
-                src = wk_raw[step[1]].rearrange("p j (g t i) -> p t g j i", t=4, i=4)
-                for t in range(4):
-                    dst = wk_bf[:, a, t, 256 * h : 256 * (h + 1)].rearrange("p (g i j) -> p g j i", i=4, j=4)
-                    copy_on(step[2][t], dst, src[:, t])
-            elif kind == "wK":
-                a = step[1]
-                src = wk_big[:, a].rearrange("p j (g t i) -> p t g j i", t=4, i=4)
-                for t in range(4):
-                    copy_on(step[2][t], wk_bf[:, a, t].rearrange("p (g i j) -> p g j i", i=4, j=4), src[:, t])
-            elif kind == "qwk":
-                a = step[1]
-                if a == 0:
-                    nc.vector.quantize_mx(
-                        out=wk_c[:, a].bitcast(FP8X4), scales=wk_s[:, a], in_=wk_bf[:, a].rearrange("p t c -> p (t c)")
-                    )
-                else:
-                    for t in range(4):
-                        cols = slice(t * P, (t + 1) * P)
-                        nc.vector.quantize_mx(
-                            out=wk_c[:, a, cols].bitcast(FP8X4), scales=wk_s[:, a, cols], in_=wk_bf[:, a, t]
-                        )
-            elif kind == "qkh":
-                c, half = step[1], step[2]
-                cols = slice(c * CH + half * 256, c * CH + (half + 1) * 256)
-                nc.vector.quantize_mx(
-                    out=k_c[:, cols].bitcast(FP8X4), scales=k_s[:, cols], in_=k_bf[:, c, half * 1024 : (half + 1) * 1024]
-                )
-            elif kind == "sh":
-                c, half, h = step[1], step[2], step[3]
-                cols = slice(c * CH + half * 256, c * CH + (half + 1) * 256)
-                bank = next_bank()
-                for u in range(2):
-                    mt = 2 * h + u
-                    nc.tensor.matmul_mx(
-                        out=bank[:, u * 256 : (u + 1) * 256],
-                        lhsT=q_c[:, mt * P : (mt + 1) * P].bitcast(FP8X4),
-                        lhsT_scale=q_s[:, mt * P : (mt + 1) * P],
-                        rhs=k_c[:, cols].bitcast(FP8X4), rhs_scale=k_s[:, cols], start=True, stop=True,
-                    )
-                stage = sc_sb[:, c, 2 * half + h]
-                nc.scalar.activation(out=stage, in_=bank[:], func=SIGMOID, scale=0.03125)
+        def load_x(half):
+            for a in range(PASSES):
+                nc.sync.dma_start(x_raw[:, half, a], k_rows(x, a, span(half, HALF)))
+
+        def move_scale_rows(a):
+            for quad in range(4):
                 nc.sync.dma_start(
-                    out_0[h * 256 : (h + 1) * 256, cols].rearrange("(u p) n -> p u n", p=P),
-                    stage.rearrange("p (u n) -> p u n", u=2),
+                    planes[32 * quad : 32 * quad + 4, a, :], scale_rows[span(a * BLOCKS // 4 + quad, 4), :]
                 )
-            elif kind == "V":
-                c = step[1]
-                vv_bank[c] = [next_bank() for nt in range(2)]
-                for n_pass, (fmt, a) in enumerate(CHAIN):
-                    rhs, rhs_sc = tab_operand(a, c * CH, CH)
-                    for nt in range(2):
-                        if fmt == 4:
-                            lhsT = wv4_w[:, a, 64 * nt : 64 * (nt + 1)].bitcast(FP4X4)
-                            lhsT_sc = planes[:, a, WV4_AT + 32 * nt : WV4_AT + 32 * (nt + 1)].bitcast(U8)
+
+        load_window(0, slice(0, T))
+        nc.sync.dma_start(wv4_codes[:], wv4_words.rearrange("a p b -> p a b").bitcast(I32))
+        nc.sync.dma_start(wvd_raw[:, 0], k_rows(wvd, 0, slice(0, N)))
+        load_window(1, span(0, T // 2))
+
+        nc.vector.tensor_copy(
+            out=scale_rows[:, WQ_AT:PLANE].rearrange("p (t g) -> p t g", t=PACK),
+            in_=wq_scale_rows[:].rearrange("p (g t) -> p t g", t=PACK),
+        )
+        picked_scales = mx_tile("picked_scales", [P, J // 4], I32)
+        nc.vector.tensor_copy(picked_scales[:].bitcast(U8), scale_window[:].bitcast(U8).indirect(offsets[:]))
+        nc.vector.tensor_copy(out=scale_rows[:, 0:WV4_AT], in_=picked_scales[0:32, :])
+
+        move_scale_rows(0)
+        load_window(1, span(1, T // 2))
+        move_scale_rows(1)
+        nc.sync.dma_start(wvd_raw[:, 1], k_rows(wvd, 1, slice(0, N)))
+        for a in range(PASSES):
+            nc.sync.dma_start(wk_raw[:, a], k_rows(wk, a, slice(0, R)))
+        load_x(0)
+        nc.sync.dma_start(wq_raw[:], wq_words.rearrange("a p b -> p a b").bitcast(I32))
+        load_x(1)
+
+        picked = mx_tile("picked", [P, PASSES, J], I32)
+        wvd_bf = mx_tile("wvd_bf", [P, PASSES, PACK * N], BF16)
+        wvd_codes = mx_tile("wvd_codes", [P, PASSES, N], U32)
+        wvd_plane = mx_tile("wvd_plane", [P, PASSES, N], U8)
+
+        def gather(a, chunk):
+            nc.vector.tensor_copy(
+                picked[:, a, span(chunk, CHUNK)].bitcast(U32),
+                windows[a][:].bitcast(U32).indirect(offsets[:, span(chunk, CHUNK // 16)]),
+            )
+
+        def table_operand(a, index, width):
+            return picked[:, a, span(index, width)].bitcast(FP8X4), planes[:, a, span(index, width // 4)].bitcast(U8)
+
+        def round_wvd(a):
+            round_and_interleave("S", wvd_bf[:, a], wvd_raw[:, a].rearrange("p j (c i) -> p c j i", i=4))
+
+        for chunk in range(CHUNKS):
+            gather(0, chunk)
+        round_wvd(0)
+        quantise(wvd_codes[:, 0], wvd_plane[:, 0], wvd_bf[:, 0])
+        round_wvd(1)
+        for chunk in range(CHUNKS - 1):
+            gather(1, chunk)
+        quantise(wvd_codes[:, 1], wvd_plane[:, 1], wvd_bf[:, 1])
+        gather(1, CHUNKS - 1)
+
+        value_banks = []
+        for chunk in range(CHUNKS):
+            pair = [next_bank() for tile in range(N // P)]
+            value_banks.extend(pair)
+            for packed in (True, False):
+                for a in range(PASSES):
+                    rhs, rhs_scale = table_operand(a, chunk, CHUNK)
+                    for tile, bank in enumerate(pair):
+                        if packed:
+                            lhsT = wv4_codes[:, a, span(tile, P // 2)].bitcast(FP4X4)
+                            lhsT_scale = planes[:, a, WV4_AT:WQ_AT][:, span(tile, P // 4)].bitcast(U8)
                         else:
-                            lhsT = wvd_c[:, a, P * nt : P * (nt + 1)].bitcast(FP8X4)
-                            lhsT_sc = wvd_s[:, a, P * nt : P * (nt + 1)]
+                            lhsT = wvd_codes[:, a, span(tile, P)].bitcast(FP8X4)
+                            lhsT_scale = wvd_plane[:, a, span(tile, P)]
                         nc.tensor.matmul_mx(
-                            out=vv_bank[c][nt][:], lhsT=lhsT, lhsT_scale=lhsT_sc, rhs=rhs, rhs_scale=rhs_sc,
-                            start=(n_pass == 0), stop=(n_pass == 3),
+                            out=bank[:], lhsT=lhsT, lhsT_scale=lhsT_scale, rhs=rhs, rhs_scale=rhs_scale,
+                            start=(packed and a == 0), stop=(not packed and a == PASSES - 1),
                         )
-            elif kind == "v":
-                c, nt = step[1], step[2]
-                copy_on(step[3], vv_sb[:, nt, c * CH : (c + 1) * CH], vv_bank[c][nt][:])
-                vv_done.add((c, nt))
-                if (c ^ 1, nt) in vv_done:
-                    cols = slice((c // 2) * 2 * CH, (c // 2 + 1) * 2 * CH)
-                    nc.sync.dma_start(out_1[P * nt : P * (nt + 1), cols], vv_sb[:, nt, cols])
-            elif kind == "x":
-                h, a = divmod(step[1], 2)
-                src = x_big[:, a, :, 256 * h : 256 * (h + 1)] if "xA" in LOADS[2] else x_raw[:, h, a]
-                interleave(step[2], x_bf[:, h, a], src)
-            elif kind == "qx":
-                h = step[1]
-                nc.vector.quantize_mx(
-                    out=x_c[:, h].rearrange("p a m -> p (a m)").bitcast(FP8X4),
-                    scales=x_s[:, h].rearrange("p a m -> p (a m)"),
-                    in_=x_bf[:, h].rearrange("p a m -> p (a m)"),
-                )
-            elif kind == "p":
-                nc.vector.tensor_copy(
-                    out=wq_w[:].rearrange("p t a (g w) -> p t (a g) w", w=2),
-                    in_=wq_raw[:].rearrange("p a (g t w) -> p t (a g) w", t=4, w=2),
-                )
-            elif kind == "k":
-                c, u = step[1], step[2]
-                bank = next_bank()
-                for t in range(4):
+
+        wk_bf = mx_tile("wk_bf", [P, PASSES, PACK, PACK * P], BF16)
+        wk_codes = mx_tile("wk_codes", [P, PASSES, R], U32)
+        wk_plane = mx_tile("wk_plane", [P, PASSES, R], U8)
+
+        def round_wk(a):
+            by_tile = wk_raw[:, a].rearrange("p j (g t i) -> p t g j i", t=PACK, i=4)
+            for t in range(PACK):
+                round_and_interleave(WK_ENGINES[a][t], wk_bf[:, a, t], by_tile[:, t])
+
+        round_wk(0)
+        quantise(wk_codes[:, 0], wk_plane[:, 0], wk_bf[:, 0].rearrange("p t c -> p (t c)"))
+        round_wk(1)
+        for t in range(PACK):
+            quantise(wk_codes[:, 1, span(t, P)], wk_plane[:, 1, span(t, P)], wk_bf[:, 1, t])
+
+        values = sbuf.tile([P, N // P, J], F32, name="values")
+        for number, bank in enumerate(value_banks):
+            chunk, tile = divmod(number, N // P)
+            copy_on(VALUE_ENGINES[number], values[:, tile, span(chunk, CHUNK)], bank[:])
+            if chunk % 2 == 1:
+                cols = span(chunk // 2, 2 * CHUNK)
+                nc.sync.dma_start(out_1[span(tile, P), cols], values[:, tile, cols])
+
+        x_bf = mx_tile("x_bf", [P, 2, PASSES, PACK * HALF], BF16)
+        x_codes = mx_tile("x_codes", [P, 2, PASSES, HALF], U32)
+        x_plane = mx_tile("x_plane", [P, 2, PASSES, HALF], U8)
+        wq_codes = mx_tile("wq_codes", [P, PACK, PASSES, P // 2], I32)
+
+        def round_x(half, a):
+            src = x_raw[:, half, a].rearrange("p j (c i) -> p c j i", i=4)
+            round_and_interleave(X_ENGINES[PASSES * half + a], x_bf[:, half, a], src)
+
+        def quantise_x(half):
+            merged = "p a m -> p (a m)"
+            quantise(x_codes[:, half].rearrange(merged), x_plane[:, half].rearrange(merged), x_bf[:, half].rearrange(merged))
+
+        def order_wq_words():
+            nc.vector.tensor_copy(
+                out=wq_codes[:].rearrange("p t a (g w) -> p t (a g) w", w=2),
+                in_=wq_raw[:].rearrange("p a (g t w) -> p t (a g) w", t=PACK, w=2),
+            )
+
+        for a in range(PASSES):
+            round_x(0, a)
+        quantise_x(0)
+
+        key_bf = mx_tile("key_bf", [P, PACK * J], BF16)
+        key_codes = mx_tile("key_codes", [P, J], U32)
+        key_plane = mx_tile("key_plane", [P, J], U8)
+        query_bf = mx_tile("query_bf", [P, PACK * M], BF16)
+        query_codes = mx_tile("query_codes", [P, M], U32)
+        query_plane = mx_tile("query_plane", [P, M], U8)
+        scores = sbuf.tile([P, CHUNKS, M // P, BANK], F32, name="scores")
+        last = CHUNKS - 1
+
+        def score_pass(out, tile, cols):
+            nc.tensor.matmul_mx(
+                out=out, lhsT=query_codes[:, span(tile, P)].bitcast(FP8X4), lhsT_scale=query_plane[:, span(tile, P)],
+                rhs=key_codes[:, cols].bitcast(FP8X4), rhs_scale=key_plane[:, cols], start=True, stop=True,
+            )
+
+        def multiply(kind, first, second):
+            bank = next_bank()
+            if kind == "score":
+                score_pass(bank[:], second, span(first, CHUNK))
+            elif kind == "last":
+                for u in range(2):
+                    score_pass(bank[:, span(u, HALF)], 2 * second + u, span(2 * last + first, HALF))
+            else:
+                for t in range(PACK):
                     for a in range(PASSES):
-                        rhs, rhs_sc = tab_operand(a, c * CH + u * P, P)
+                        if kind == "key":
+                            lhsT, lhsT_scale = wk_codes[:, a, span(t, P)].bitcast(FP8X4), wk_plane[:, a, span(t, P)]
+                            rhs, rhs_scale = table_operand(a, first * (CHUNK // P) + second, P)
+                        else:
+                            lhsT = wq_codes[:, t, a].bitcast(FP4X4)
+                            lhsT_scale = planes[:, a, WQ_AT:PLANE][:, span(t, P // 4)].bitcast(U8)
+                            rhs = x_codes[:, first, a, span(second, P)].bitcast(FP8X4)
+                            rhs_scale = x_plane[:, first, a, span(second, P)]
                         nc.tensor.matmul_mx(
-                            out=bank[:, t * P : (t + 1) * P],
-                            lhsT=wk_c[:, a, t * P : (t + 1) * P].bitcast(FP8X4),
-                            lhsT_scale=wk_s[:, a, t * P : (t + 1) * P],
-                            rhs=rhs, rhs_scale=rhs_sc, start=(a == 0), stop=(a == PASSES - 1),
-                        )
-                chain_out(step[3], k_bf[:, c, u * CH : (u + 1) * CH], bank)
-            elif kind == "qk":
-                cols = slice(step[1] * CH, (step[1] + 1) * CH)
-                nc.vector.quantize_mx(out=k_c[:, cols].bitcast(FP8X4), scales=k_s[:, cols], in_=k_bf[:, step[1]])
-            elif kind == "q":
-                h, u = step[1], step[2]
-                bank = next_bank()
-                for t in range(4):
-                    for a in range(PASSES):
-                        nc.tensor.matmul_mx(
-                            out=bank[:, t * P : (t + 1) * P],
-                            lhsT=wq_w[:, t, a].bitcast(FP4X4),
-                            lhsT_scale=planes[:, a, WQ_AT + 32 * t : WQ_AT + 32 * (t + 1)].bitcast(U8),
-                            rhs=x_c[:, h, a, u * P : (u + 1) * P].bitcast(FP8X4),
-                            rhs_scale=x_s[:, h, a, u * P : (u + 1) * P],
+                            out=bank[:, span(t, P)], lhsT=lhsT, lhsT_scale=lhsT_scale, rhs=rhs, rhs_scale=rhs_scale,
                             start=(a == 0), stop=(a == PASSES - 1),
                         )
-                chain_out(step[3], q_bf[:, h, u * CH : (u + 1) * CH], bank)
-            elif kind == "qq":
-                cols = slice(step[1] * 256, (step[1] + 1) * 256)
-                nc.vector.quantize_mx(out=q_c[:, cols].bitcast(FP8X4), scales=q_s[:, cols], in_=q_bf[:, step[1]])
+            return bank
+
+        def sigmoid(out, bank):
+            nc.scalar.activation(out=out, in_=bank[:], func=mybir.ActivationFunctionType.Sigmoid, scale=SCORE_SCALE)
+
+        def empty(bank, kind, first, second, engine):
+            if kind == "score":
+                sigmoid(scores[:, first, second], bank)
+                nc.sync.dma_start(out_0[span(second, P), span(first, CHUNK)], scores[:, first, second])
+            elif kind == "last":
+                staged = scores[:, last, 2 * first + second]
+                sigmoid(staged, bank)
+                nc.sync.dma_start(
+                    out_0[span(second, HALF), span(2 * last + first, HALF)].rearrange("(u p) n -> p u n", p=P),
+                    staged.rearrange("p (u n) -> p u n", u=2),
+                )
             else:
-                c, h, split = step[1], step[2], step[3]
-                cols = slice(c * CH, (c + 1) * CH)
-                for mt in (2 * h, 2 * h + 1):
-                    bank = next_bank()
-                    nc.tensor.matmul_mx(
-                        out=bank[:],
-                        lhsT=q_c[:, mt * P : (mt + 1) * P].bitcast(FP8X4),
-                        lhsT_scale=q_s[:, mt * P : (mt + 1) * P],
-                        rhs=k_c[:, cols].bitcast(FP8X4), rhs_scale=k_s[:, cols], start=True, stop=True,
-                    )
-                    nc.scalar.activation(out=sc_sb[:, c, mt], in_=bank[:], func=SIGMOID, scale=0.03125)
-                    if split:
-                        nc.sync.dma_start(out_0[mt * P : (mt + 1) * P, cols], sc_sb[:, c, mt])
-                if not split:
-                    nc.sync.dma_start(
-                        out_0[h * 256 : (h + 1) * 256, cols].rearrange("(u p) n -> p u n", p=P),
-                        sc_sb[:, c, 2 * h : 2 * h + 2],
-                    )
+                if kind == "key":
+                    rounded, codes, plane = key_bf, key_codes, key_plane
+                    number, run = first * (CHUNK // P) + second, HALF if first == last else CHUNK
+                else:
+                    rounded, codes, plane = query_bf, query_codes, query_plane
+                    number, run = first * (HALF // P) + second, HALF
+                copy_on(
+                    engine,
+                    rounded[:, span(number, BANK)].rearrange("p (n t) -> p n t", t=PACK),
+                    bank[:].rearrange("p (t n) -> p n t", t=PACK),
+                )
+                if (number + 1) * P % run == 0:
+                    index = number * P // run
+                    quantise(codes[:, span(index, run)], plane[:, span(index, run)], rounded[:, span(index, PACK * run)])
+
+        filled = []
+        for number, (kind, first, second, engine) in enumerate(JOBS):
+            if number == WQ_BEFORE:
+                order_wq_words()
+            if number in X_SECOND_BEFORE:
+                round_x(1, X_SECOND_BEFORE.index(number))
+            if number == X_SECOND_CODES_BEFORE:
+                quantise_x(1)
+            filled.append(multiply(kind, first, second))
+            if number >= LAG:
+                empty(filled[number - LAG], *JOBS[number - LAG])
+        for number in range(len(JOBS) - LAG, len(JOBS)):
+            empty(filled[number], *JOBS[number])

@@ -14,6 +14,7 @@ U16 = mybir.dt.uint16
 U8 = mybir.dt.uint8
 FP8X4 = mybir.dt.float8_e4m3fn_x4
 FP4X4 = mybir.dt.float4_e2m1fn_x4
+SIGMOID = mybir.ActivationFunctionType.Sigmoid
 
 P = 128
 PACK = 4
@@ -24,31 +25,20 @@ BANK = 512
 BANKS = 8
 CHUNK = 512
 CHUNKS = J // CHUNK
+QUARTERS = CHUNK // P
+TILES = M // P
 HALF = 256
 
 WV4_AT = J // 4
 WQ_AT = WV4_AT + N // 4
 PLANE = WQ_AT + R // 4
 
-WK_ENGINES = ("SSVS", "VVSS")
-VALUE_ENGINES = "VVSSSSVV"
-X_ENGINES = "SVVV"
-
-JOBS = (
-    ("key", 0, 0, "V"), ("key", 0, 1, "S"), ("key", 0, 2, "V"), ("key", 0, 3, "S"), ("key", 1, 0, "S"),
-    ("query", 0, 0, "S"), ("query", 0, 1, "S"), ("key", 1, 1, "S"), ("key", 1, 2, "S"),
-    ("query", 1, 0, "V"), ("key", 1, 3, "S"), ("score", 0, 0, "S"), ("query", 1, 1, "V"),
-    ("key", 2, 0, "V"), ("score", 0, 1, "S"), ("score", 1, 0, "S"),
-    ("key", 2, 1, "V"), ("score", 1, 1, "S"),
-    ("key", 2, 2, "V"), ("score", 0, 2, "S"), ("score", 0, 3, "S"),
-    ("key", 2, 3, "V"), ("score", 1, 2, "S"), ("score", 1, 3, "S"), ("score", 2, 0, "S"),
-    ("key", 3, 0, "V"), ("key", 3, 1, "V"), ("score", 2, 1, "S"),
-    ("key", 3, 2, "V"), ("score", 2, 2, "S"),
-    ("key", 3, 3, "V"), ("score", 2, 3, "S"),
-    ("last", 0, 0, "S"), ("last", 0, 1, "S"), ("last", 1, 0, "S"), ("last", 1, 1, "S"),
-)
+LATE = {}
+SCORE_BANKS = (2, 3, 4, 5)
+QE = "SSVV"
+KE = "VVVVVVVVVV"
+NCH = 3
 LAG = 2
-WQ_BEFORE, X_SECOND_BEFORE, X_SECOND_CODES_BEFORE = 2, (6, 7), 8
 
 
 def tile_list_kvt_dl_sig_kernel(
@@ -59,8 +49,11 @@ def tile_list_kvt_dl_sig_kernel(
         sbuf = ctx.enter_context(tc.tile_pool(name="sbuf", bufs=1))
         psum = ctx.enter_context(tc.psum_pool(name="psum", bufs=1))
 
-        def mx_tile(name, shape, dtype):
-            return sbuf.tile(shape, dtype, name=name, align_bytes=64)
+        def mx_tile(name, shape, dtype, on=None):
+            return sbuf.tile(shape, dtype, name=name, tag=on or name, align_bytes=64)
+
+        def per_pass(name, shape, dtype):
+            return [mx_tile("%s%d" % (name, a), shape, dtype) for a in range(PASSES)]
 
         def copy_on(engine, out, in_):
             if engine == "S":
@@ -71,8 +64,8 @@ def tile_list_kvt_dl_sig_kernel(
         def span(index, width):
             return slice(index * width, (index + 1) * width)
 
-        def k_rows(source, a, cols):
-            return source[span(a, PASS_K), cols].rearrange("(p j) n -> p j n", j=PACK)
+        def k_rows(source, a):
+            return source[span(a, PASS_K), :].rearrange("(p j) n -> p j n", j=PACK)
 
         def round_and_interleave(engine, dst, src):
             copy_on(engine, dst.rearrange("p (c i j) -> p c j i", i=4, j=PACK), src)
@@ -80,49 +73,45 @@ def tile_list_kvt_dl_sig_kernel(
         def quantise(codes, scales, values):
             nc.vector.quantize_mx(out=codes.bitcast(FP8X4), scales=scales, in_=values)
 
-        banks_taken = []
-
-        def next_bank():
-            banks_taken.append(psum.tile([P, BANK], F32, name="bank", tag="bank%d" % (len(banks_taken) % BANKS)))
-            return banks_taken[-1]
+        def take_bank(number):
+            return psum.tile([P, BANK], F32, name="bank", tag="bank%d" % number)
 
         offsets = sbuf.tile([P, J // 16], U16, name="offsets")
         nc.sync.dma_start(offsets[:], offs)
         scale_rows = mx_tile("scale_rows", [PASSES * BLOCKS, PLANE], I32)
         wq_scale_rows = mx_tile("wq_scale_rows", [PASSES * BLOCKS, R // 4], I32)
         scale_window = mx_tile("scale_window", [P, T // 4], I32)
-        planes = mx_tile("planes", [P, PASSES, PLANE], I32)
+        planes = per_pass("plane", [P, PLANE], I32)
+        warm_in = sbuf.tile([P, 1], F32, name="warm_in")
+        warm_out = sbuf.tile([P, 1], F32, name="warm_out")
+        nc.gpsimd.memset(warm_in[:], 0.0)
+        nc.scalar.activation(out=warm_out[:], in_=warm_in[:], func=SIGMOID)
         nc.vector.memset(scale_window[32:64, :], 0)
         nc.vector.memset(scale_window[64:128, :], 0)
-        nc.gpsimd.memset(planes[:], 0)
+        for a in range(PASSES):
+            nc.gpsimd.memset(planes[a][:], 0)
         nc.sync.dma_start(scale_window[0:32, :], tab_scales.rearrange("a b t -> (a b) t").bitcast(I32))
         nc.sync.dma_start(wq_scale_rows[:], wq_scales.rearrange("a b r -> (a b) r").bitcast(I32))
         nc.sync.dma_start(scale_rows[:, WV4_AT:WQ_AT], wv4_scales.rearrange("a b n -> (a b) n").bitcast(I32))
 
-        windows = [mx_tile("window%d" % a, [P, T], I32) for a in range(PASSES)]
+        windows = per_pass("window", [P, T], I32)
         wv4_codes = mx_tile("wv4_codes", [P, PASSES, N // 2], I32)
-        wvd_raw = sbuf.tile([P, PASSES, PACK, N], F32, name="wvd_raw")
-        wk_raw = sbuf.tile([P, PASSES, PACK, R], F32, name="wk_raw")
+        wvd_raw = per_pass("wvd_raw", [P, PACK, N], F32)
+        wk_raw = per_pass("wk_raw", [P, PACK, R], F32)
+        x_raw = per_pass("x_raw", [P, PACK, M], F32)
         wq_raw = sbuf.tile([P, PASSES, R // 2], I32, name="wq_raw")
-        x_raw = sbuf.tile([P, 2, PASSES, PACK, HALF], F32, name="x_raw")
 
-        def load_window(a, cols):
-            nc.sync.dma_start(windows[a][:, cols], tab_words[a].rearrange("p t i -> p (t i)").bitcast(I32)[:, cols])
-
-        def load_x(half):
-            for a in range(PASSES):
-                nc.sync.dma_start(x_raw[:, half, a], k_rows(x, a, span(half, HALF)))
+        def load_window(a):
+            nc.sync.dma_start(windows[a][:], tab_words[a].rearrange("p t i -> p (t i)").bitcast(I32))
 
         def move_scale_rows(a):
-            for quad in range(4):
-                nc.sync.dma_start(
-                    planes[32 * quad : 32 * quad + 4, a, :], scale_rows[span(a * BLOCKS // 4 + quad, 4), :]
-                )
+            for row in range(4):
+                nc.sync.dma_start(planes[a][row:P:32, :], scale_rows[a * BLOCKS + row : (a + 1) * BLOCKS : 4, :])
 
-        load_window(0, slice(0, T))
+        load_window(0)
         nc.sync.dma_start(wv4_codes[:], wv4_words.rearrange("a p b -> p a b").bitcast(I32))
-        nc.sync.dma_start(wvd_raw[:, 0], k_rows(wvd, 0, slice(0, N)))
-        load_window(1, span(0, T // 2))
+        for a in range(PASSES):
+            nc.sync.dma_start(wvd_raw[a][:], k_rows(wvd, a))
 
         nc.vector.tensor_copy(
             out=scale_rows[:, WQ_AT:PLANE].rearrange("p (t g) -> p t g", t=PACK),
@@ -133,96 +122,104 @@ def tile_list_kvt_dl_sig_kernel(
         nc.vector.tensor_copy(out=scale_rows[:, 0:WV4_AT], in_=picked_scales[0:32, :])
 
         move_scale_rows(0)
-        load_window(1, span(1, T // 2))
+        load_window(1)
         move_scale_rows(1)
-        nc.sync.dma_start(wvd_raw[:, 1], k_rows(wvd, 1, slice(0, N)))
         for a in range(PASSES):
-            nc.sync.dma_start(wk_raw[:, a], k_rows(wk, a, slice(0, R)))
-        load_x(0)
+            nc.sync.dma_start(wk_raw[a][:], k_rows(wk, a))
+        nc.sync.dma_start(x_raw[0][:], k_rows(x, 0))
         nc.sync.dma_start(wq_raw[:], wq_words.rearrange("a p b -> p a b").bitcast(I32))
-        load_x(1)
+        nc.sync.dma_start(x_raw[1][:], k_rows(x, 1))
 
-        picked = mx_tile("picked", [P, PASSES, J], I32)
-        wvd_bf = mx_tile("wvd_bf", [P, PASSES, PACK * N], BF16)
-        wvd_codes = mx_tile("wvd_codes", [P, PASSES, N], U32)
-        wvd_plane = mx_tile("wvd_plane", [P, PASSES, N], U8)
+        picked = per_pass("picked", [P, J], I32)
+        wvd_bf = per_pass("wvd_bf", [P, PACK * N], BF16)
+        wvd_codes = per_pass("wvd_codes", [P, N], U32)
+        wvd_plane = per_pass("wvd_plane", [P, N], U8)
 
         def gather(a, chunk):
             nc.vector.tensor_copy(
-                picked[:, a, span(chunk, CHUNK)].bitcast(U32),
+                picked[a][:, span(chunk, CHUNK)].bitcast(U32),
                 windows[a][:].bitcast(U32).indirect(offsets[:, span(chunk, CHUNK // 16)]),
             )
 
         def table_operand(a, index, width):
-            return picked[:, a, span(index, width)].bitcast(FP8X4), planes[:, a, span(index, width // 4)].bitcast(U8)
+            return picked[a][:, span(index, width)].bitcast(FP8X4), planes[a][:, span(index, width // 4)].bitcast(U8)
 
-        def round_wvd(a):
-            round_and_interleave("S", wvd_bf[:, a], wvd_raw[:, a].rearrange("p j (c i) -> p c j i", i=4))
+        value_banks = [take_bank(number) for number in range(BANKS)]
 
+        def value_passes(a, packed, chunks):
+            for chunk in chunks:
+                rhs, rhs_scale = table_operand(a, chunk, CHUNK)
+                for tile in range(N // P):
+                    if packed:
+                        lhsT = wv4_codes[:, a, span(tile, P // 2)].bitcast(FP4X4)
+                        lhsT_scale = planes[a][:, WV4_AT:WQ_AT][:, span(tile, P // 4)].bitcast(U8)
+                    else:
+                        lhsT = wvd_codes[a][:, span(tile, P)].bitcast(FP8X4)
+                        lhsT_scale = wvd_plane[a][:, span(tile, P)]
+                    nc.tensor.matmul_mx(
+                        out=value_banks[chunk * (N // P) + tile][:], lhsT=lhsT, lhsT_scale=lhsT_scale,
+                        rhs=rhs, rhs_scale=rhs_scale,
+                        start=(packed and a == 0), stop=(not packed and a == PASSES - 1),
+                    )
+
+        for a in range(PASSES):
+            round_and_interleave("S", wvd_bf[a][:], wvd_raw[a][:].rearrange("p j (c i) -> p c j i", i=4))
         for chunk in range(CHUNKS):
             gather(0, chunk)
-        round_wvd(0)
-        quantise(wvd_codes[:, 0], wvd_plane[:, 0], wvd_bf[:, 0])
-        round_wvd(1)
-        for chunk in range(CHUNKS - 1):
-            gather(1, chunk)
-        quantise(wvd_codes[:, 1], wvd_plane[:, 1], wvd_bf[:, 1])
-        gather(1, CHUNKS - 1)
-
-        value_banks = []
+        for a in range(PASSES):
+            quantise(wvd_codes[a][:], wvd_plane[a][:], wvd_bf[a][:])
+        for packed in (True, False):
+            value_passes(0, packed, range(CHUNKS))
         for chunk in range(CHUNKS):
-            pair = [next_bank() for tile in range(N // P)]
-            value_banks.extend(pair)
+            gather(1, chunk)
             for packed in (True, False):
-                for a in range(PASSES):
-                    rhs, rhs_scale = table_operand(a, chunk, CHUNK)
-                    for tile, bank in enumerate(pair):
-                        if packed:
-                            lhsT = wv4_codes[:, a, span(tile, P // 2)].bitcast(FP4X4)
-                            lhsT_scale = planes[:, a, WV4_AT:WQ_AT][:, span(tile, P // 4)].bitcast(U8)
-                        else:
-                            lhsT = wvd_codes[:, a, span(tile, P)].bitcast(FP8X4)
-                            lhsT_scale = wvd_plane[:, a, span(tile, P)]
-                        nc.tensor.matmul_mx(
-                            out=bank[:], lhsT=lhsT, lhsT_scale=lhsT_scale, rhs=rhs, rhs_scale=rhs_scale,
-                            start=(packed and a == 0), stop=(not packed and a == PASSES - 1),
-                        )
+                value_passes(1, packed, [chunk])
 
-        wk_bf = mx_tile("wk_bf", [P, PASSES, PACK, PACK * P], BF16)
-        wk_codes = mx_tile("wk_codes", [P, PASSES, R], U32)
-        wk_plane = mx_tile("wk_plane", [P, PASSES, R], U8)
+        wk_bf = per_pass("wk_bf", [P, PACK, PACK * P], BF16)
+        wk_codes = per_pass("wk_codes", [P, R], U32)
+        wk_plane = per_pass("wk_plane", [P, R], U8)
+        values = [sbuf.tile([P, N // P, CHUNK], F32, name="values_first")]
 
-        def round_wk(a):
-            by_tile = wk_raw[:, a].rearrange("p j (g t i) -> p t g j i", t=PACK, i=4)
-            for t in range(PACK):
-                round_and_interleave(WK_ENGINES[a][t], wk_bf[:, a, t], by_tile[:, t])
+        def round_wk(engine, a, pair):
+            by_tile = wk_raw[a][:].rearrange("p j (g t i) -> p t g j i", t=PACK, i=4)
+            dst = wk_bf[a][:].rearrange("p t (g i j) -> p t g j i", i=4, j=PACK)
+            copy_on(engine, dst[:, span(pair, 2)], by_tile[:, span(pair, 2)])
 
-        round_wk(0)
-        quantise(wk_codes[:, 0], wk_plane[:, 0], wk_bf[:, 0].rearrange("p t c -> p (t c)"))
-        round_wk(1)
-        for t in range(PACK):
-            quantise(wk_codes[:, 1, span(t, P)], wk_plane[:, 1, span(t, P)], wk_bf[:, 1, t])
+        def quantise_wk(a, pair):
+            values_bf = wk_bf[a][:, span(pair, 2)].rearrange("p t c -> p (t c)")
+            quantise(wk_codes[a][:, span(pair, 2 * P)], wk_plane[a][:, span(pair, 2 * P)], values_bf)
 
-        values = sbuf.tile([P, N // P, J], F32, name="values")
-        for number, bank in enumerate(value_banks):
+        def empty_values(engine, number):
             chunk, tile = divmod(number, N // P)
-            copy_on(VALUE_ENGINES[number], values[:, tile, span(chunk, CHUNK)], bank[:])
-            if chunk % 2 == 1:
-                cols = span(chunk // 2, 2 * CHUNK)
-                nc.sync.dma_start(out_1[span(tile, P), cols], values[:, tile, cols])
+            copy_on(engine, values[min(chunk, 1)][:, tile, span(max(chunk - 1, 0), CHUNK)], value_banks[number][:])
 
-        x_bf = mx_tile("x_bf", [P, 2, PASSES, PACK * HALF], BF16)
-        x_codes = mx_tile("x_codes", [P, 2, PASSES, HALF], U32)
-        x_plane = mx_tile("x_plane", [P, 2, PASSES, HALF], U8)
+        for number in range(2):
+            empty_values("S", number)
+        for a in range(PASSES):
+            for pair in range(2):
+                round_wk("S" if a == pair == 0 else "V", a, pair)
+            for pair in range(2):
+                quantise_wk(a, pair)
+        values.append(mx_tile("values_second", [P, N // P, J - CHUNK], F32, on="wk_raw0"))
+        for number in range(2, BANKS):
+            empty_values("S", number)
+        nc.sync.dma_start(out_1[:, 0:CHUNK].rearrange("(u p) n -> p u n", p=P), values[0][:])
+        for tile in range(N // P):
+            nc.sync.dma_start(out_1[span(tile, P), CHUNK:J], values[1][:, tile, :])
+
+        x_bf = per_pass("x_bf", [P, PACK * M], BF16)
+        x_codes = per_pass("x_codes", [P, M], U32)
+        x_plane = per_pass("x_plane", [P, M], U8)
         wq_codes = mx_tile("wq_codes", [P, PACK, PASSES, P // 2], I32)
 
-        def round_x(half, a):
-            src = x_raw[:, half, a].rearrange("p j (c i) -> p c j i", i=4)
-            round_and_interleave(X_ENGINES[PASSES * half + a], x_bf[:, half, a], src)
-
-        def quantise_x(half):
-            merged = "p a m -> p (a m)"
-            quantise(x_codes[:, half].rearrange(merged), x_plane[:, half].rearrange(merged), x_bf[:, half].rearrange(merged))
+        def prepare_x(a, width):
+            for step in range(M // width + 1):
+                if step < M // width:
+                    src = x_raw[a][:, :, span(step, width)].rearrange("p j (c i) -> p c j i", i=4)
+                    round_and_interleave("V", x_bf[a][:, span(step, PACK * width)], src)
+                if step > 0:
+                    cols = span(step - 1, width)
+                    quantise(x_codes[a][:, cols], x_plane[a][:, cols], x_bf[a][:, span(step - 1, PACK * width)])
 
         def order_wq_words():
             nc.vector.tensor_copy(
@@ -230,58 +227,72 @@ def tile_list_kvt_dl_sig_kernel(
                 in_=wq_raw[:].rearrange("p a (g t w) -> p t (a g) w", t=PACK, w=2),
             )
 
-        for a in range(PASSES):
-            round_x(0, a)
-        quantise_x(0)
-
-        key_bf = mx_tile("key_bf", [P, PACK * J], BF16)
-        key_codes = mx_tile("key_codes", [P, J], U32)
+        key_bf = {}
+        late = {}
         key_plane = mx_tile("key_plane", [P, J], U8)
         query_bf = mx_tile("query_bf", [P, PACK * M], BF16)
         query_codes = mx_tile("query_codes", [P, M], U32)
         query_plane = mx_tile("query_plane", [P, M], U8)
-        scores = sbuf.tile([P, CHUNKS, M // P, BANK], F32, name="scores")
+        scores = sbuf.tile([P, TILES, J - CHUNK], F32, name="scores")
+        last_scores = sbuf.tile([P, 4, BANK], F32, name="last_scores")
         last = CHUNKS - 1
 
         def score_pass(out, tile, cols):
             nc.tensor.matmul_mx(
                 out=out, lhsT=query_codes[:, span(tile, P)].bitcast(FP8X4), lhsT_scale=query_plane[:, span(tile, P)],
-                rhs=key_codes[:, cols].bitcast(FP8X4), rhs_scale=key_plane[:, cols], start=True, stop=True,
+                rhs=late["key_codes"][:, cols].bitcast(FP8X4), rhs_scale=key_plane[:, cols], start=True, stop=True,
             )
 
+        def key_pass(bank, number, a, t):
+            rhs, rhs_scale = table_operand(a, number, P)
+            nc.tensor.matmul_mx(
+                out=bank[:, span(t, P)], lhsT=wk_codes[a][:, span(t, P)].bitcast(FP8X4),
+                lhsT_scale=wk_plane[a][:, span(t, P)], rhs=rhs, rhs_scale=rhs_scale,
+                start=(a == 0 and t == 0), stop=(a == PASSES - 1 and t == PACK - 1),
+            )
+
+        def query_pass(bank, number, a, t):
+            nc.tensor.matmul_mx(
+                out=bank[:, span(t, P)], lhsT=wq_codes[:, t, a].bitcast(FP4X4),
+                lhsT_scale=planes[a][:, WQ_AT:PLANE][:, span(t, P // 4)].bitcast(U8),
+                rhs=x_codes[a][:, span(number, P)].bitcast(FP8X4), rhs_scale=x_plane[a][:, span(number, P)],
+                start=(a == 0 and t == 0), stop=(a == PASSES - 1 and t == PACK - 1),
+            )
+
+        key_ring, score_ring = [4, 5, 6, 7, 0, 1], [2, 3]
+
         def multiply(kind, first, second):
-            bank = next_bank()
+            if kind in ("score", "last"):
+                ring = score_ring
+            else:
+                ring = key_ring
+            number = ring.pop(0)
+            bank = take_bank(number)
+            (score_ring if number in SCORE_BANKS else key_ring).append(number)
             if kind == "score":
                 score_pass(bank[:], second, span(first, CHUNK))
             elif kind == "last":
                 for u in range(2):
                     score_pass(bank[:, span(u, HALF)], 2 * second + u, span(2 * last + first, HALF))
             else:
-                for t in range(PACK):
-                    for a in range(PASSES):
+                for a in range(PASSES):
+                    for t in range(PACK):
                         if kind == "key":
-                            lhsT, lhsT_scale = wk_codes[:, a, span(t, P)].bitcast(FP8X4), wk_plane[:, a, span(t, P)]
-                            rhs, rhs_scale = table_operand(a, first * (CHUNK // P) + second, P)
+                            key_pass(bank, first * QUARTERS + second, a, t)
                         else:
-                            lhsT = wq_codes[:, t, a].bitcast(FP4X4)
-                            lhsT_scale = planes[:, a, WQ_AT:PLANE][:, span(t, P // 4)].bitcast(U8)
-                            rhs = x_codes[:, first, a, span(second, P)].bitcast(FP8X4)
-                            rhs_scale = x_plane[:, first, a, span(second, P)]
-                        nc.tensor.matmul_mx(
-                            out=bank[:, span(t, P)], lhsT=lhsT, lhsT_scale=lhsT_scale, rhs=rhs, rhs_scale=rhs_scale,
-                            start=(a == 0), stop=(a == PASSES - 1),
-                        )
+                            query_pass(bank, first * (HALF // P) + second, a, t)
             return bank
 
         def sigmoid(out, bank):
-            nc.scalar.activation(out=out, in_=bank[:], func=mybir.ActivationFunctionType.Sigmoid, scale=SCORE_SCALE)
+            nc.scalar.activation(out=out, in_=bank[:], func=SIGMOID, scale=SCORE_SCALE)
 
         def empty(bank, kind, first, second, engine):
             if kind == "score":
-                sigmoid(scores[:, first, second], bank)
-                nc.sync.dma_start(out_0[span(second, P), span(first, CHUNK)], scores[:, first, second])
+                sigmoid(scores[:, second, span(first, CHUNK)], bank)
+                cols = span(first, CHUNK)
+                nc.sync.dma_start(out_0[span(second, P), cols], scores[:, second, cols])
             elif kind == "last":
-                staged = scores[:, last, 2 * first + second]
+                staged = last_scores[:, 2 * first + second]
                 sigmoid(staged, bank)
                 nc.sync.dma_start(
                     out_0[span(second, HALF), span(2 * last + first, HALF)].rearrange("(u p) n -> p u n", p=P),
@@ -289,30 +300,57 @@ def tile_list_kvt_dl_sig_kernel(
                 )
             else:
                 if kind == "key":
-                    rounded, codes, plane = key_bf, key_codes, key_plane
-                    number, run = first * (CHUNK // P) + second, HALF if first == last else CHUNK
+                    index, part = divmod(first * QUARTERS + second, 2)
+                    if part == 0:
+                        on = LATE.get(index)
+                        key_bf[index] = mx_tile("key_bf%d" % index, [P, PACK * HALF], BF16, on=on)
+                    rounded = key_bf[index][:]
                 else:
-                    rounded, codes, plane = query_bf, query_codes, query_plane
-                    number, run = first * (HALF // P) + second, HALF
+                    index, part = first * 2 + second, 0
+                    rounded = query_bf[:, span(index, PACK * P)]
                 copy_on(
                     engine,
-                    rounded[:, span(number, BANK)].rearrange("p (n t) -> p n t", t=PACK),
+                    rounded[:, span(part, BANK)].rearrange("p (n t) -> p n t", t=PACK),
                     bank[:].rearrange("p (t n) -> p n t", t=PACK),
                 )
-                if (number + 1) * P % run == 0:
-                    index = number * P // run
-                    quantise(codes[:, span(index, run)], plane[:, span(index, run)], rounded[:, span(index, PACK * run)])
+                if kind == "query":
+                    quantise(query_codes[:, span(index, P)], query_plane[:, span(index, P)], rounded)
+                elif part == 1 and index >= 2:
+                    quantise_keys(index)
+
+        def quantise_keys(index):
+            quantise(late["key_codes"][:, span(index, HALF)], key_plane[:, span(index, HALF)], key_bf[index][:])
+
+        first_banks = [take_bank(quarter) for quarter in range(QUARTERS)]
+        for quarter, bank in enumerate(first_banks):
+            for t in range(PACK):
+                key_pass(bank, quarter, 0, t)
+        for t in range(PACK):
+            for quarter, bank in enumerate(first_banks):
+                key_pass(bank, quarter, 1, t)
+        for quarter, bank in enumerate(first_banks):
+            empty(bank, "key", 0, quarter, "S")
+        prepare_x(0, HALF)
+        order_wq_words()
+        prepare_x(1, P)
+        late["key_codes"] = mx_tile("key_codes", [P, J], U32, on="x_raw1")
+
+        jobs = [("key", 1, quarter, "S") for quarter in range(2)]
+        jobs.extend(("query", half, tile, QE[2 * half + tile]) for half in range(2) for tile in range(HALF // P))
+        codes_at = 4
+        waiting = [("score", chunk, tile, "S") for chunk in range(NCH) for tile in range(TILES)]
+        keys_left = [("key", number // QUARTERS, number % QUARTERS, KE[number - 6]) for number in range(6, 4 * QUARTERS)]
+        for letter in "kskssksskskkskskskskss":
+            jobs.append((keys_left if letter == "k" else waiting).pop(0))
+        jobs.extend(("last", half, pair, "S") for half in range(2) for pair in range(2))
 
         filled = []
-        for number, (kind, first, second, engine) in enumerate(JOBS):
-            if number == WQ_BEFORE:
-                order_wq_words()
-            if number in X_SECOND_BEFORE:
-                round_x(1, X_SECOND_BEFORE.index(number))
-            if number == X_SECOND_CODES_BEFORE:
-                quantise_x(1)
+        for number, (kind, first, second, engine) in enumerate(jobs):
+            if number == codes_at:
+                for index in range(2):
+                    quantise_keys(index)
             filled.append(multiply(kind, first, second))
             if number >= LAG:
-                empty(filled[number - LAG], *JOBS[number - LAG])
-        for number in range(len(JOBS) - LAG, len(JOBS)):
-            empty(filled[number], *JOBS[number])
+                empty(filled[number - LAG], *jobs[number - LAG])
+        for number in range(len(jobs) - LAG, len(jobs)):
+            empty(filled[number], *jobs[number])

@@ -29,15 +29,22 @@ QUARTERS = CHUNK // P
 TILES = M // P
 HALF = 256
 
-WV4_AT = J // 4
-WQ_AT = WV4_AT + N // 4
+WQ_AT = N // 4
 PLANE = WQ_AT + R // 4
 
-LATE = {}
-SCORE_BANKS = (2, 3, 4, 5)
+WKE = "SSVV"
+VE = "SSSSSSSS"
+X0E = "VV"
+X1E = "VVVV"
 QE = "SSVV"
-KE = "VVVVVVVVVV"
-NCH = 3
+KE = "SSSSSSSVVVVVVVVV"
+EARLY_KEYS = 7
+SCORES_PER_KEY = (1,1,1,1,2,2,2,2,2)
+WAITJ = 2
+SCORE_BANKS = (3, 4, 5, 6)
+RUNS = ((0, 4), (4, 4), (8, 4), (12, 2), (14, 1), (15, 1))
+QRUNS = ((0, 2), (2, 2), (4, 2), (6, 2), (8, 2), (10, 2), (12, 2), (14, 1), (15, 1))
+RING = (4, 5, 6, 7, 0, 1, 2)
 LAG = 2
 
 
@@ -68,7 +75,9 @@ def tile_list_kvt_dl_sig_kernel(
             return source[span(a, PASS_K), :].rearrange("(p j) n -> p j n", j=PACK)
 
         def round_and_interleave(engine, dst, src):
-            copy_on(engine, dst.rearrange("p (c i j) -> p c j i", i=4, j=PACK), src)
+            copy_on(
+                engine, dst.rearrange("p (c i j) -> p c j i", i=2, j=PACK), src.rearrange("p j (c i) -> p c j i", i=2)
+            )
 
         def quantise(codes, scales, values):
             nc.vector.quantize_mx(out=codes.bitcast(FP8X4), scales=scales, in_=values)
@@ -78,21 +87,27 @@ def tile_list_kvt_dl_sig_kernel(
 
         offsets = sbuf.tile([P, J // 16], U16, name="offsets")
         nc.sync.dma_start(offsets[:], offs)
-        scale_rows = mx_tile("scale_rows", [PASSES * BLOCKS, PLANE], I32)
-        wq_scale_rows = mx_tile("wq_scale_rows", [PASSES * BLOCKS, R // 4], I32)
+        weight_rows = mx_tile("weight_rows", [BLOCKS, PASSES, PLANE], I32)
+        wq_scale_rows = mx_tile("wq_scale_rows", [BLOCKS, PASSES, R // 4], I32)
+        weight_plane = mx_tile("weight_plane", [P, PASSES, PLANE], I32)
         scale_window = mx_tile("scale_window", [P, T // 4], I32)
-        planes = per_pass("plane", [P, PLANE], I32)
+        planes = per_pass("plane", [P, J // 4], I32)
         warm_in = sbuf.tile([P, 1], F32, name="warm_in")
         warm_out = sbuf.tile([P, 1], F32, name="warm_out")
         nc.gpsimd.memset(warm_in[:], 0.0)
         nc.scalar.activation(out=warm_out[:], in_=warm_in[:], func=SIGMOID)
         nc.vector.memset(scale_window[32:64, :], 0)
         nc.vector.memset(scale_window[64:128, :], 0)
+        nc.gpsimd.memset(weight_plane[:], 0)
         for a in range(PASSES):
             nc.gpsimd.memset(planes[a][:], 0)
+        nc.sync.dma_start(wq_scale_rows[:], wq_scales.rearrange("a b r -> b a r").bitcast(I32))
+        nc.sync.dma_start(weight_rows[:, :, 0:WQ_AT], wv4_scales.rearrange("a b n -> b a n").bitcast(I32))
         nc.sync.dma_start(scale_window[0:32, :], tab_scales.rearrange("a b t -> (a b) t").bitcast(I32))
-        nc.sync.dma_start(wq_scale_rows[:], wq_scales.rearrange("a b r -> (a b) r").bitcast(I32))
-        nc.sync.dma_start(scale_rows[:, WV4_AT:WQ_AT], wv4_scales.rearrange("a b n -> (a b) n").bitcast(I32))
+        nc.vector.tensor_copy(
+            out=weight_rows[:, :, WQ_AT:PLANE].rearrange("p a (t g) -> p a t g", t=PACK),
+            in_=wq_scale_rows[:].rearrange("p a (g t) -> p a t g", t=PACK),
+        )
 
         windows = per_pass("window", [P, T], I32)
         wv4_codes = mx_tile("wv4_codes", [P, PASSES, N // 2], I32)
@@ -106,20 +121,17 @@ def tile_list_kvt_dl_sig_kernel(
 
         def move_scale_rows(a):
             for row in range(4):
-                nc.sync.dma_start(planes[a][row:P:32, :], scale_rows[a * BLOCKS + row : (a + 1) * BLOCKS : 4, :])
+                nc.sync.dma_start(planes[a][row:P:32, :], picked_scales[a * BLOCKS + row : (a + 1) * BLOCKS : 4, :])
 
         load_window(0)
+        for row in range(4):
+            nc.sync.dma_start(weight_plane[row:P:32], weight_rows[row:BLOCKS:4])
         nc.sync.dma_start(wv4_codes[:], wv4_words.rearrange("a p b -> p a b").bitcast(I32))
         for a in range(PASSES):
             nc.sync.dma_start(wvd_raw[a][:], k_rows(wvd, a))
 
-        nc.vector.tensor_copy(
-            out=scale_rows[:, WQ_AT:PLANE].rearrange("p (t g) -> p t g", t=PACK),
-            in_=wq_scale_rows[:].rearrange("p (g t) -> p t g", t=PACK),
-        )
         picked_scales = mx_tile("picked_scales", [P, J // 4], I32)
         nc.vector.tensor_copy(picked_scales[:].bitcast(U8), scale_window[:].bitcast(U8).indirect(offsets[:]))
-        nc.vector.tensor_copy(out=scale_rows[:, 0:WV4_AT], in_=picked_scales[0:32, :])
 
         move_scale_rows(0)
         load_window(1)
@@ -146,39 +158,38 @@ def tile_list_kvt_dl_sig_kernel(
 
         value_banks = [take_bank(number) for number in range(BANKS)]
 
-        def value_passes(a, packed, chunks):
-            for chunk in chunks:
-                rhs, rhs_scale = table_operand(a, chunk, CHUNK)
-                for tile in range(N // P):
-                    if packed:
-                        lhsT = wv4_codes[:, a, span(tile, P // 2)].bitcast(FP4X4)
-                        lhsT_scale = planes[a][:, WV4_AT:WQ_AT][:, span(tile, P // 4)].bitcast(U8)
-                    else:
-                        lhsT = wvd_codes[a][:, span(tile, P)].bitcast(FP8X4)
-                        lhsT_scale = wvd_plane[a][:, span(tile, P)]
-                    nc.tensor.matmul_mx(
-                        out=value_banks[chunk * (N // P) + tile][:], lhsT=lhsT, lhsT_scale=lhsT_scale,
-                        rhs=rhs, rhs_scale=rhs_scale,
-                        start=(packed and a == 0), stop=(not packed and a == PASSES - 1),
-                    )
+        def value_passes(a, packed, chunk):
+            rhs, rhs_scale = table_operand(a, chunk, CHUNK)
+            for tile in range(N // P):
+                if packed:
+                    lhsT = wv4_codes[:, a, span(tile, P // 2)].bitcast(FP4X4)
+                    lhsT_scale = weight_plane[:, a, span(tile, P // 4)].bitcast(U8)
+                else:
+                    lhsT = wvd_codes[a][:, span(tile, P)].bitcast(FP8X4)
+                    lhsT_scale = wvd_plane[a][:, span(tile, P)]
+                nc.tensor.matmul_mx(
+                    out=value_banks[chunk * (N // P) + tile][:], lhsT=lhsT, lhsT_scale=lhsT_scale,
+                    rhs=rhs, rhs_scale=rhs_scale,
+                    start=(packed and a == 0), stop=(not packed and a == PASSES - 1),
+                )
 
         for a in range(PASSES):
-            round_and_interleave("S", wvd_bf[a][:], wvd_raw[a][:].rearrange("p j (c i) -> p c j i", i=4))
+            round_and_interleave("S", wvd_bf[a][:], wvd_raw[a][:])
         for chunk in range(CHUNKS):
             gather(0, chunk)
         for a in range(PASSES):
             quantise(wvd_codes[a][:], wvd_plane[a][:], wvd_bf[a][:])
         for packed in (True, False):
-            value_passes(0, packed, range(CHUNKS))
+            for chunk in range(CHUNKS):
+                value_passes(0, packed, chunk)
         for chunk in range(CHUNKS):
             gather(1, chunk)
             for packed in (True, False):
-                value_passes(1, packed, [chunk])
+                value_passes(1, packed, chunk)
 
         wk_bf = per_pass("wk_bf", [P, PACK, PACK * P], BF16)
         wk_codes = per_pass("wk_codes", [P, R], U32)
         wk_plane = per_pass("wk_plane", [P, R], U8)
-        values = [sbuf.tile([P, N // P, CHUNK], F32, name="values_first")]
 
         def round_wk(engine, a, pair):
             by_tile = wk_raw[a][:].rearrange("p j (g t i) -> p t g j i", t=PACK, i=4)
@@ -186,62 +197,49 @@ def tile_list_kvt_dl_sig_kernel(
             copy_on(engine, dst[:, span(pair, 2)], by_tile[:, span(pair, 2)])
 
         def quantise_wk(a, pair):
-            values_bf = wk_bf[a][:, span(pair, 2)].rearrange("p t c -> p (t c)")
-            quantise(wk_codes[a][:, span(pair, 2 * P)], wk_plane[a][:, span(pair, 2 * P)], values_bf)
+            rounded = wk_bf[a][:, span(pair, 2)].rearrange("p t c -> p (t c)")
+            quantise(wk_codes[a][:, span(pair, 2 * P)], wk_plane[a][:, span(pair, 2 * P)], rounded)
 
-        def empty_values(engine, number):
-            chunk, tile = divmod(number, N // P)
-            copy_on(engine, values[min(chunk, 1)][:, tile, span(max(chunk - 1, 0), CHUNK)], value_banks[number][:])
-
-        for number in range(2):
-            empty_values("S", number)
         for a in range(PASSES):
             for pair in range(2):
-                round_wk("S" if a == pair == 0 else "V", a, pair)
+                round_wk(WKE[2 * a + pair], a, pair)
             for pair in range(2):
                 quantise_wk(a, pair)
-        values.append(mx_tile("values_second", [P, N // P, J - CHUNK], F32, on="wk_raw0"))
-        for number in range(2, BANKS):
-            empty_values("S", number)
-        nc.sync.dma_start(out_1[:, 0:CHUNK].rearrange("(u p) n -> p u n", p=P), values[0][:])
+        values = mx_tile("values", [P, N // P, J], F32, on="wk_raw0")
+        for number, bank in enumerate(value_banks):
+            chunk, tile = divmod(number, N // P)
+            copy_on(VE[number], values[:, tile, span(chunk, CHUNK)], bank[:])
         for tile in range(N // P):
-            nc.sync.dma_start(out_1[span(tile, P), CHUNK:J], values[1][:, tile, :])
+            nc.sync.dma_start(out_1[span(tile, P), :], values[:, tile, :])
 
         x_bf = per_pass("x_bf", [P, PACK * M], BF16)
         x_codes = per_pass("x_codes", [P, M], U32)
         x_plane = per_pass("x_plane", [P, M], U8)
         wq_codes = mx_tile("wq_codes", [P, PACK, PASSES, P // 2], I32)
 
-        def prepare_x(a, width):
+        def prepare_x(a, width, engines):
             for step in range(M // width + 1):
                 if step < M // width:
-                    src = x_raw[a][:, :, span(step, width)].rearrange("p j (c i) -> p c j i", i=4)
-                    round_and_interleave("V", x_bf[a][:, span(step, PACK * width)], src)
+                    src = x_raw[a][:, :, span(step, width)]
+                    round_and_interleave(engines[step], x_bf[a][:, span(step, PACK * width)], src)
                 if step > 0:
                     cols = span(step - 1, width)
                     quantise(x_codes[a][:, cols], x_plane[a][:, cols], x_bf[a][:, span(step - 1, PACK * width)])
 
-        def order_wq_words():
-            nc.vector.tensor_copy(
-                out=wq_codes[:].rearrange("p t a (g w) -> p t (a g) w", w=2),
-                in_=wq_raw[:].rearrange("p a (g t w) -> p t (a g) w", t=PACK, w=2),
-            )
+        prepare_x(0, HALF, X0E)
+        nc.vector.tensor_copy(
+            out=wq_codes[:].rearrange("p t a (g w) -> p t (a g) w", w=2),
+            in_=wq_raw[:].rearrange("p a (g t w) -> p t (a g) w", t=PACK, w=2),
+        )
+        prepare_x(1, P, X1E)
 
-        key_bf = {}
-        late = {}
+        key_bf = mx_tile("key_bf", [P, PACK * J], BF16)
+        key_codes = mx_tile("key_codes", [P, J], U32, on="x_raw1")
         key_plane = mx_tile("key_plane", [P, J], U8)
         query_bf = mx_tile("query_bf", [P, PACK * M], BF16)
         query_codes = mx_tile("query_codes", [P, M], U32)
         query_plane = mx_tile("query_plane", [P, M], U8)
-        scores = sbuf.tile([P, TILES, J - CHUNK], F32, name="scores")
-        last_scores = sbuf.tile([P, 4, BANK], F32, name="last_scores")
-        last = CHUNKS - 1
-
-        def score_pass(out, tile, cols):
-            nc.tensor.matmul_mx(
-                out=out, lhsT=query_codes[:, span(tile, P)].bitcast(FP8X4), lhsT_scale=query_plane[:, span(tile, P)],
-                rhs=late["key_codes"][:, cols].bitcast(FP8X4), rhs_scale=key_plane[:, cols], start=True, stop=True,
-            )
+        scores = sbuf.tile([P, J // P, BANK], F32, name="scores")
 
         def key_pass(bank, number, a, t):
             rhs, rhs_scale = table_operand(a, number, P)
@@ -254,102 +252,86 @@ def tile_list_kvt_dl_sig_kernel(
         def query_pass(bank, number, a, t):
             nc.tensor.matmul_mx(
                 out=bank[:, span(t, P)], lhsT=wq_codes[:, t, a].bitcast(FP4X4),
-                lhsT_scale=planes[a][:, WQ_AT:PLANE][:, span(t, P // 4)].bitcast(U8),
+                lhsT_scale=weight_plane[:, a, WQ_AT:PLANE][:, span(t, P // 4)].bitcast(U8),
                 rhs=x_codes[a][:, span(number, P)].bitcast(FP8X4), rhs_scale=x_plane[a][:, span(number, P)],
                 start=(a == 0 and t == 0), stop=(a == PASSES - 1 and t == PACK - 1),
             )
 
-        key_ring, score_ring = [4, 5, 6, 7, 0, 1], [2, 3]
+        def round_bank(engine, rounded, number, bank):
+            round_and_interleave(engine, rounded[:, span(number, BANK)], bank[:].rearrange("p (t n) -> p t n", t=PACK))
+
+        def quantise_keys(first, count):
+            cols = slice(first * P, (first + count) * P)
+            quantise(key_codes[:, cols], key_plane[:, cols], key_bf[:, first * BANK : (first + count) * BANK])
+
+        product_ring, score_ring = list(RING), [b for b in SCORE_BANKS if b not in RING]
 
         def multiply(kind, first, second):
-            if kind in ("score", "last"):
-                ring = score_ring
-            else:
-                ring = key_ring
-            number = ring.pop(0)
+            number = (score_ring if kind == "score" else product_ring).pop(0)
+            (score_ring if number in SCORE_BANKS else product_ring).append(number)
             bank = take_bank(number)
-            (score_ring if number in SCORE_BANKS else key_ring).append(number)
             if kind == "score":
-                score_pass(bank[:], second, span(first, CHUNK))
-            elif kind == "last":
-                for u in range(2):
-                    score_pass(bank[:, span(u, HALF)], 2 * second + u, span(2 * last + first, HALF))
+                start, count = RUNS[first]
+                cols = slice(start * P, (start + count) * P)
+                for u in range(TILES // count):
+                    tile = second * (TILES // count) + u
+                    nc.tensor.matmul_mx(
+                        out=bank[:, span(u, count * P)], lhsT=query_codes[:, span(tile, P)].bitcast(FP8X4),
+                        lhsT_scale=query_plane[:, span(tile, P)],
+                        rhs=key_codes[:, cols].bitcast(FP8X4), rhs_scale=key_plane[:, cols], start=True, stop=True,
+                    )
             else:
                 for a in range(PASSES):
                     for t in range(PACK):
-                        if kind == "key":
-                            key_pass(bank, first * QUARTERS + second, a, t)
-                        else:
-                            query_pass(bank, first * (HALF // P) + second, a, t)
+                        (key_pass if kind == "key" else query_pass)(bank, first, a, t)
             return bank
 
-        def sigmoid(out, bank):
-            nc.scalar.activation(out=out, in_=bank[:], func=SIGMOID, scale=SCORE_SCALE)
-
-        def empty(bank, kind, first, second, engine):
+        def empty(bank, kind, first, second):
             if kind == "score":
-                sigmoid(scores[:, second, span(first, CHUNK)], bank)
-                cols = span(first, CHUNK)
-                nc.sync.dma_start(out_0[span(second, P), cols], scores[:, second, cols])
-            elif kind == "last":
-                staged = last_scores[:, 2 * first + second]
-                sigmoid(staged, bank)
+                start, count = RUNS[first]
+                staged = scores[:, start + second]
+                nc.scalar.activation(out=staged, in_=bank[:], func=SIGMOID, scale=SCORE_SCALE)
                 nc.sync.dma_start(
-                    out_0[span(second, HALF), span(2 * last + first, HALF)].rearrange("(u p) n -> p u n", p=P),
-                    staged.rearrange("p (u n) -> p u n", u=2),
+                    out_0[span(second, M // count), start * P : (start + count) * P].rearrange("(u p) n -> p u n", p=P),
+                    staged.rearrange("p (u n) -> p u n", n=count * P),
                 )
+            elif kind == "query":
+                round_bank(second, query_bf, first, bank)
+                quantise(query_codes[:, span(first, P)], query_plane[:, span(first, P)], query_bf[:, span(first, BANK)])
             else:
-                if kind == "key":
-                    index, part = divmod(first * QUARTERS + second, 2)
-                    if part == 0:
-                        on = LATE.get(index)
-                        key_bf[index] = mx_tile("key_bf%d" % index, [P, PACK * HALF], BF16, on=on)
-                    rounded = key_bf[index][:]
-                else:
-                    index, part = first * 2 + second, 0
-                    rounded = query_bf[:, span(index, PACK * P)]
-                copy_on(
-                    engine,
-                    rounded[:, span(part, BANK)].rearrange("p (n t) -> p n t", t=PACK),
-                    bank[:].rearrange("p (t n) -> p n t", t=PACK),
-                )
-                if kind == "query":
-                    quantise(query_codes[:, span(index, P)], query_plane[:, span(index, P)], rounded)
-                elif part == 1 and index >= 2:
-                    quantise_keys(index)
+                round_bank(second, key_bf, first, bank)
+                for start, count in QRUNS:
+                    if first == start + count - 1:
+                        quantise_keys(start, count)
 
-        def quantise_keys(index):
-            quantise(late["key_codes"][:, span(index, HALF)], key_plane[:, span(index, HALF)], key_bf[index][:])
-
-        first_banks = [take_bank(quarter) for quarter in range(QUARTERS)]
-        for quarter, bank in enumerate(first_banks):
+        first_banks = [take_bank(number) for number in range(QUARTERS)]
+        for number, bank in enumerate(first_banks):
             for t in range(PACK):
-                key_pass(bank, quarter, 0, t)
-        for t in range(PACK):
-            for quarter, bank in enumerate(first_banks):
-                key_pass(bank, quarter, 1, t)
-        for quarter, bank in enumerate(first_banks):
-            empty(bank, "key", 0, quarter, "S")
-        prepare_x(0, HALF)
-        order_wq_words()
-        prepare_x(1, P)
-        late["key_codes"] = mx_tile("key_codes", [P, J], U32, on="x_raw1")
+                key_pass(bank, number, 0, t)
+        for pair in range(2):
+            for number, bank in enumerate(first_banks):
+                for t in (2 * pair, 2 * pair + 1):
+                    key_pass(bank, number, 1, t)
+        for number, bank in enumerate(first_banks):
+            empty(bank, "key", number, KE[number])
 
-        jobs = [("key", 1, quarter, "S") for quarter in range(2)]
-        jobs.extend(("query", half, tile, QE[2 * half + tile]) for half in range(2) for tile in range(HALF // P))
-        codes_at = 4
-        waiting = [("score", chunk, tile, "S") for chunk in range(NCH) for tile in range(TILES)]
-        keys_left = [("key", number // QUARTERS, number % QUARTERS, KE[number - 6]) for number in range(6, 4 * QUARTERS)]
-        for letter in "kskssksskskkskskskskss":
-            jobs.append((keys_left if letter == "k" else waiting).pop(0))
-        jobs.extend(("last", half, pair, "S") for half in range(2) for pair in range(2))
+        jobs = [("key", number, KE[number]) for number in range(QUARTERS, EARLY_KEYS)]
+        jobs.extend(("query", tile, QE[tile]) for tile in range(TILES))
+        ready_at = {0: 0}
+        waiting = [("score", run, part) for run, (start, count) in enumerate(RUNS) for part in range(count)]
+        for number in range(EARLY_KEYS, J // P):
+            jobs.append(("key", number, KE[number]))
+            for run, (start, count) in enumerate(RUNS):
+                if number == start + count - 1:
+                    ready_at[run] = len(jobs) + WAITJ
+            for turn in range(SCORES_PER_KEY[number - EARLY_KEYS]):
+                if ready_at.get(waiting[0][1], len(jobs) + 1) <= len(jobs):
+                    jobs.append(waiting.pop(0))
+        jobs.extend(waiting)
 
         filled = []
-        for number, (kind, first, second, engine) in enumerate(jobs):
-            if number == codes_at:
-                for index in range(2):
-                    quantise_keys(index)
-            filled.append(multiply(kind, first, second))
+        for number, job in enumerate(jobs):
+            filled.append(multiply(*job))
             if number >= LAG:
                 empty(filled[number - LAG], *jobs[number - LAG])
         for number in range(len(jobs) - LAG, len(jobs)):

@@ -32,19 +32,27 @@ HALF = 256
 WQ_AT = N // 4
 PLANE = WQ_AT + R // 4
 
-WKE = "SSVV"
+WKE = "SVVV"
 VE = "SSSSSSSS"
 X0E = "VV"
 X1E = "VVVV"
-QE = "SSVV"
-KE = "SSSSSSSVVVVVVVVV"
-EARLY_KEYS = 7
-SCORES_PER_KEY = (1,1,1,1,2,2,2,2,2)
+QE = "VSVS"
+KE = "SSSSSSSSVVVVVVVV"
+EARLY_KEYS = 8
+SCORES_PER_KEY = (2,2,2,2,2,2,2,2)
 WAITJ = 2
-SCORE_BANKS = (3, 4, 5, 6)
+SCORE_BANKS = (4,5,6,7)
 RUNS = ((0, 4), (4, 4), (8, 4), (12, 2), (14, 1), (15, 1))
 QRUNS = ((0, 2), (2, 2), (4, 2), (6, 2), (8, 2), (10, 2), (12, 2), (14, 1), (15, 1))
-RING = (4, 5, 6, 7, 0, 1, 2)
+RING = (0,1,2,3)
+ON = {(1, 3): "wvd_bf1", (1, 2): "wvd_raw1"}
+CB = 2
+GROUPS = ((0, 1), (2,), (3,))
+FV = 1
+PAIRED = 0
+CODES_ON = "x_bf1"
+EARLY = (4,5,6,7,0,1,2,3)
+DEFER_TO = 3
 LAG = 2
 
 
@@ -116,8 +124,8 @@ def tile_list_kvt_dl_sig_kernel(
         x_raw = per_pass("x_raw", [P, PACK, M], F32)
         wq_raw = sbuf.tile([P, PASSES, R // 2], I32, name="wq_raw")
 
-        def load_window(a):
-            nc.sync.dma_start(windows[a][:], tab_words[a].rearrange("p t i -> p (t i)").bitcast(I32))
+        def load_window(a, cols=slice(0, T)):
+            nc.sync.dma_start(windows[a][:, cols], tab_words[a].rearrange("p t i -> p (t i)").bitcast(I32)[:, cols])
 
         def move_scale_rows(a):
             for row in range(4):
@@ -127,34 +135,37 @@ def tile_list_kvt_dl_sig_kernel(
         for row in range(4):
             nc.sync.dma_start(weight_plane[row:P:32], weight_rows[row:BLOCKS:4])
         nc.sync.dma_start(wv4_codes[:], wv4_words.rearrange("a p b -> p a b").bitcast(I32))
-        for a in range(PASSES):
-            nc.sync.dma_start(wvd_raw[a][:], k_rows(wvd, a))
+        nc.sync.dma_start(wvd_raw[0][:], k_rows(wvd, 0))
+        load_window(1, slice(0, T // 4))
 
         picked_scales = mx_tile("picked_scales", [P, J // 4], I32)
         nc.vector.tensor_copy(picked_scales[:].bitcast(U8), scale_window[:].bitcast(U8).indirect(offsets[:]))
 
         move_scale_rows(0)
-        load_window(1)
+        load_window(1, slice(T // 4, T))
+        nc.sync.dma_start(wvd_raw[1][:], k_rows(wvd, 1))
         move_scale_rows(1)
         for a in range(PASSES):
             nc.sync.dma_start(wk_raw[a][:], k_rows(wk, a))
         nc.sync.dma_start(x_raw[0][:], k_rows(x, 0))
-        nc.sync.dma_start(wq_raw[:], wq_words.rearrange("a p b -> p a b").bitcast(I32))
         nc.sync.dma_start(x_raw[1][:], k_rows(x, 1))
+        nc.sync.dma_start(wq_raw[:], wq_words.rearrange("a p b -> p a b").bitcast(I32))
 
-        picked = per_pass("picked", [P, J], I32)
+        picked = {}
         wvd_bf = per_pass("wvd_bf", [P, PACK * N], BF16)
         wvd_codes = per_pass("wvd_codes", [P, N], U32)
         wvd_plane = per_pass("wvd_plane", [P, N], U8)
 
         def gather(a, chunk):
+            picked[a, chunk] = mx_tile("picked%d%d" % (a, chunk), [P, CHUNK], I32, on=ON.get((a, chunk)))
             nc.vector.tensor_copy(
-                picked[a][:, span(chunk, CHUNK)].bitcast(U32),
+                picked[a, chunk][:].bitcast(U32),
                 windows[a][:].bitcast(U32).indirect(offsets[:, span(chunk, CHUNK // 16)]),
             )
 
         def table_operand(a, index, width):
-            return picked[a][:, span(index, width)].bitcast(FP8X4), planes[a][:, span(index, width // 4)].bitcast(U8)
+            chunk, part = divmod(index, CHUNK // width)
+            return picked[a, chunk][:, span(part, width)].bitcast(FP8X4), planes[a][:, span(index, width // 4)].bitcast(U8)
 
         value_banks = [take_bank(number) for number in range(BANKS)]
 
@@ -177,40 +188,49 @@ def tile_list_kvt_dl_sig_kernel(
             round_and_interleave("S", wvd_bf[a][:], wvd_raw[a][:])
         for chunk in range(CHUNKS):
             gather(0, chunk)
-        for a in range(PASSES):
-            quantise(wvd_codes[a][:], wvd_plane[a][:], wvd_bf[a][:])
+        quantise(wvd_codes[0][:], wvd_plane[0][:], wvd_bf[0][:])
         for packed in (True, False):
             for chunk in range(CHUNKS):
                 value_passes(0, packed, chunk)
         for chunk in range(CHUNKS):
+            if chunk == CB:
+                quantise(wvd_codes[1][:], wvd_plane[1][:], wvd_bf[1][:])
             gather(1, chunk)
+        for chunks in GROUPS:
             for packed in (True, False):
-                value_passes(1, packed, chunk)
+                for chunk in chunks:
+                    value_passes(1, packed, chunk)
 
         wk_bf = per_pass("wk_bf", [P, PACK, PACK * P], BF16)
         wk_codes = per_pass("wk_codes", [P, R], U32)
         wk_plane = per_pass("wk_plane", [P, R], U8)
 
         def round_wk(engine, a, pair):
-            by_tile = wk_raw[a][:].rearrange("p j (g t i) -> p t g j i", t=PACK, i=4)
-            dst = wk_bf[a][:].rearrange("p t (g i j) -> p t g j i", i=4, j=PACK)
-            copy_on(engine, dst[:, span(pair, 2)], by_tile[:, span(pair, 2)])
+            by_tile = wk_raw[a][:].rearrange("p j (g t h i) -> p t g h j i", t=PACK, h=2, i=2)
+            dst = wk_bf[a][:].rearrange("p t (g h i j) -> p t g h j i", h=2, i=2, j=PACK)
+            for t in (2 * pair, 2 * pair + 1):
+                copy_on(engine, dst[:, t], by_tile[:, t])
 
         def quantise_wk(a, pair):
             rounded = wk_bf[a][:, span(pair, 2)].rearrange("p t c -> p (t c)")
             quantise(wk_codes[a][:, span(pair, 2 * P)], wk_plane[a][:, span(pair, 2 * P)], rounded)
 
+        first_values = mx_tile("first_values", [P, N // P, FV * CHUNK], F32)
+        for number in range(2 * FV):
+            chunk, tile = divmod(number, N // P)
+            copy_on(VE[number], first_values[:, tile, span(chunk, CHUNK)], value_banks[number][:])
         for a in range(PASSES):
             for pair in range(2):
                 round_wk(WKE[2 * a + pair], a, pair)
             for pair in range(2):
                 quantise_wk(a, pair)
-        values = mx_tile("values", [P, N // P, J], F32, on="wk_raw0")
-        for number, bank in enumerate(value_banks):
+        values = mx_tile("values", [P, N // P, J - FV * CHUNK], F32, on="wk_raw0")
+        for number in range(2 * FV, BANKS):
             chunk, tile = divmod(number, N // P)
-            copy_on(VE[number], values[:, tile, span(chunk, CHUNK)], bank[:])
+            copy_on(VE[number], values[:, tile, span(chunk - FV, CHUNK)], value_banks[number][:])
+        nc.sync.dma_start(out_1[:, 0 : FV * CHUNK].rearrange("(u p) n -> p u n", p=P), first_values[:])
         for tile in range(N // P):
-            nc.sync.dma_start(out_1[span(tile, P), :], values[:, tile, :])
+            nc.sync.dma_start(out_1[span(tile, P), FV * CHUNK : J], values[:, tile, :])
 
         x_bf = per_pass("x_bf", [P, PACK * M], BF16)
         x_codes = per_pass("x_codes", [P, M], U32)
@@ -233,13 +253,14 @@ def tile_list_kvt_dl_sig_kernel(
         )
         prepare_x(1, P, X1E)
 
-        key_bf = mx_tile("key_bf", [P, PACK * J], BF16)
-        key_codes = mx_tile("key_codes", [P, J], U32, on="x_raw1")
+        key_bf = [mx_tile("key_bf", [P, PACK * J // 2], BF16), mx_tile("key_bf_late", [P, PACK * J // 2], BF16, on="x_raw1")]
+        key_codes = mx_tile("key_codes", [P, J], U32, on=CODES_ON)
         key_plane = mx_tile("key_plane", [P, J], U8)
         query_bf = mx_tile("query_bf", [P, PACK * M], BF16)
         query_codes = mx_tile("query_codes", [P, M], U32)
         query_plane = mx_tile("query_plane", [P, M], U8)
         scores = sbuf.tile([P, J // P, BANK], F32, name="scores")
+        paired = PAIRED
 
         def key_pass(bank, number, a, t):
             rhs, rhs_scale = table_operand(a, number, P)
@@ -262,13 +283,17 @@ def tile_list_kvt_dl_sig_kernel(
 
         def quantise_keys(first, count):
             cols = slice(first * P, (first + count) * P)
-            quantise(key_codes[:, cols], key_plane[:, cols], key_bf[:, first * BANK : (first + count) * BANK])
+            quantise(key_codes[:, cols], key_plane[:, cols], key_bf[first // 8][:, first % 8 * BANK : (first % 8 + count) * BANK])
 
-        product_ring, score_ring = list(RING), [b for b in SCORE_BANKS if b not in RING]
+        early, product_ring, score_ring = list(EARLY), list(RING), list(SCORE_BANKS)
 
         def multiply(kind, first, second):
-            number = (score_ring if kind == "score" else product_ring).pop(0)
-            (score_ring if number in SCORE_BANKS else product_ring).append(number)
+            if early:
+                number = early.pop(0)
+            else:
+                ring = score_ring if kind == "score" else product_ring
+                number = ring.pop(0)
+                ring.append(number)
             bank = take_bank(number)
             if kind == "score":
                 start, count = RUNS[first]
@@ -289,6 +314,15 @@ def tile_list_kvt_dl_sig_kernel(
         def empty(bank, kind, first, second):
             if kind == "score":
                 start, count = RUNS[first]
+                if first < paired:
+                    slot = paired * second + first
+                    nc.scalar.activation(out=scores[:, slot], in_=bank[:], func=SIGMOID, scale=SCORE_SCALE)
+                    if first == paired - 1:
+                        nc.sync.dma_start(
+                            out_0[span(second, P), 0 : paired * CHUNK],
+                            scores[:, paired * second : paired * (second + 1)].rearrange("p c n -> p (c n)"),
+                        )
+                    return
                 staged = scores[:, start + second]
                 nc.scalar.activation(out=staged, in_=bank[:], func=SIGMOID, scale=SCORE_SCALE)
                 nc.sync.dma_start(
@@ -298,10 +332,13 @@ def tile_list_kvt_dl_sig_kernel(
             elif kind == "query":
                 round_bank(second, query_bf, first, bank)
                 quantise(query_codes[:, span(first, P)], query_plane[:, span(first, P)], query_bf[:, span(first, BANK)])
+                if first == DEFER_TO:
+                    for start in range(QUARTERS, EARLY_KEYS, 2):
+                        quantise_keys(start, 2)
             else:
-                round_bank(second, key_bf, first, bank)
+                round_bank(second, key_bf[first // 8], first % 8, bank)
                 for start, count in QRUNS:
-                    if first == start + count - 1:
+                    if first == start + count - 1 and not QUARTERS <= first < EARLY_KEYS:
                         quantise_keys(start, count)
 
         first_banks = [take_bank(number) for number in range(QUARTERS)]
@@ -317,12 +354,13 @@ def tile_list_kvt_dl_sig_kernel(
 
         jobs = [("key", number, KE[number]) for number in range(QUARTERS, EARLY_KEYS)]
         jobs.extend(("query", tile, QE[tile]) for tile in range(TILES))
-        ready_at = {0: 0}
-        waiting = [("score", run, part) for run, (start, count) in enumerate(RUNS) for part in range(count)]
+        ready_at = {run: 0 for run, (start, count) in enumerate(RUNS) if start + count <= EARLY_KEYS}
+        waiting = [("score", run, tile) for tile in range(TILES) for run in range(paired)]
+        waiting.extend(("score", run, part) for run, (start, count) in enumerate(RUNS) for part in range(count) if run >= paired)
         for number in range(EARLY_KEYS, J // P):
             jobs.append(("key", number, KE[number]))
             for run, (start, count) in enumerate(RUNS):
-                if number == start + count - 1:
+                if number == start + count - 1 and start < J // P - QUARTERS:
                     ready_at[run] = len(jobs) + WAITJ
             for turn in range(SCORES_PER_KEY[number - EARLY_KEYS]):
                 if ready_at.get(waiting[0][1], len(jobs) + 1) <= len(jobs):
@@ -330,9 +368,12 @@ def tile_list_kvt_dl_sig_kernel(
         jobs.extend(waiting)
 
         filled = []
-        for number, job in enumerate(jobs):
-            filled.append(multiply(*job))
-            if number >= LAG:
-                empty(filled[number - LAG], *jobs[number - LAG])
-        for number in range(len(jobs) - LAG, len(jobs)):
-            empty(filled[number], *jobs[number])
+        for job in jobs:
+            if job[0] == "score":
+                while any(kind == "key" and first < sum(RUNS[job[1]]) for bank, kind, first, second in filled):
+                    empty(*filled.pop(0))
+            filled.append((multiply(*job), *job))
+            if len(filled) > LAG:
+                empty(*filled.pop(0))
+        for entry in filled:
+            empty(*entry)

@@ -82,9 +82,9 @@ def tile_list_kvt_dl_sig_kernel(
         def k_rows(source, a):
             return source[span(a, PASS_K), :].rearrange("(p j) n -> p j n", j=PACK)
 
-        def round_and_interleave(engine, dst, src):
+        def round_and_interleave(engine, dst, src, run=4):
             copy_on(
-                engine, dst.rearrange("p (c i j) -> p c j i", i=2, j=PACK), src.rearrange("p j (c i) -> p c j i", i=2)
+                engine, dst.rearrange("p (c i j) -> p c j i", i=run, j=PACK), src.rearrange("p j (c i) -> p c j i", i=run)
             )
 
         def quantise(codes, scales, values):
@@ -206,10 +206,9 @@ def tile_list_kvt_dl_sig_kernel(
         wk_plane = per_pass("wk_plane", [P, R], U8)
 
         def round_wk(engine, a, pair):
-            by_tile = wk_raw[a][:].rearrange("p j (g t h i) -> p t g h j i", t=PACK, h=2, i=2)
-            dst = wk_bf[a][:].rearrange("p t (g h i j) -> p t g h j i", h=2, i=2, j=PACK)
-            for t in (2 * pair, 2 * pair + 1):
-                copy_on(engine, dst[:, t], by_tile[:, t])
+            by_tile = wk_raw[a][:].rearrange("p j (g t i) -> p t g j i", t=PACK, i=4)
+            dst = wk_bf[a][:].rearrange("p t (g i j) -> p t g j i", i=4, j=PACK)
+            copy_on(engine, dst[:, span(pair, 2)], by_tile[:, span(pair, 2)])
 
         def quantise_wk(a, pair):
             rounded = wk_bf[a][:, span(pair, 2)].rearrange("p t c -> p (t c)")
@@ -279,7 +278,7 @@ def tile_list_kvt_dl_sig_kernel(
             )
 
         def round_bank(engine, rounded, number, bank):
-            round_and_interleave(engine, rounded[:, span(number, BANK)], bank[:].rearrange("p (t n) -> p t n", t=PACK))
+            round_and_interleave(engine, rounded[:, span(number, BANK)], bank[:].rearrange("p (t n) -> p t n", t=PACK), run=2)
 
         def quantise_keys(first, count):
             cols = slice(first * P, (first + count) * P)

@@ -32,27 +32,10 @@ HALF = 256
 WQ_AT = N // 4
 PLANE = WQ_AT + R // 4
 
-WKE = "SVVV"
-VE = "SSSSSSSS"
-X0E = "VV"
-X1E = "VVVV"
-QE = "VSVS"
-KE = "SSSSSSSSVVVVVVVV"
-EARLY_KEYS = 8
-SCORES_PER_KEY = (2,2,2,2,2,2,2,2)
-WAITJ = 2
-SCORE_BANKS = (4,5,6,7)
-RUNS = ((0, 4), (4, 4), (8, 4), (12, 2), (14, 1), (15, 1))
-QRUNS = ((0, 2), (2, 2), (4, 2), (6, 2), (8, 2), (10, 2), (12, 2), (14, 1), (15, 1))
-RING = (0,1,2,3)
-ON = {(1, 3): "wvd_bf1", (1, 2): "wvd_raw1"}
-CB = 2
-GROUPS = ((0, 1), (2,), (3,))
-FV = 1
-PAIRED = 0
-CODES_ON = "x_bf1"
-EARLY = (4,5,6,7,0,1,2,3)
-DEFER_TO = 3
+KEY_TILES = J // P
+EARLY_KEYS = 2 * QUARTERS
+CODES_BEFORE = 2
+SCORES_PER_KEY = 2
 LAG = 2
 
 
@@ -82,9 +65,11 @@ def tile_list_kvt_dl_sig_kernel(
         def k_rows(source, a):
             return source[span(a, PASS_K), :].rearrange("(p j) n -> p j n", j=PACK)
 
-        def round_and_interleave(engine, dst, src, run=4):
+        def round_and_interleave(engine, dst, src, run):
             copy_on(
-                engine, dst.rearrange("p (c i j) -> p c j i", i=run, j=PACK), src.rearrange("p j (c i) -> p c j i", i=run)
+                engine,
+                dst.rearrange("p (c i j) -> p c j i", i=run, j=PACK),
+                src.rearrange("p j (c i) -> p c j i", i=run),
             )
 
         def quantise(codes, scales, values):
@@ -147,8 +132,8 @@ def tile_list_kvt_dl_sig_kernel(
         move_scale_rows(1)
         for a in range(PASSES):
             nc.sync.dma_start(wk_raw[a][:], k_rows(wk, a))
-        nc.sync.dma_start(x_raw[0][:], k_rows(x, 0))
-        nc.sync.dma_start(x_raw[1][:], k_rows(x, 1))
+        for a in range(PASSES):
+            nc.sync.dma_start(x_raw[a][:], k_rows(x, a))
         nc.sync.dma_start(wq_raw[:], wq_words.rearrange("a p b -> p a b").bitcast(I32))
 
         picked = {}
@@ -156,8 +141,8 @@ def tile_list_kvt_dl_sig_kernel(
         wvd_codes = per_pass("wvd_codes", [P, N], U32)
         wvd_plane = per_pass("wvd_plane", [P, N], U8)
 
-        def gather(a, chunk):
-            picked[a, chunk] = mx_tile("picked%d%d" % (a, chunk), [P, CHUNK], I32, on=ON.get((a, chunk)))
+        def gather(a, chunk, on=None):
+            picked[a, chunk] = mx_tile("picked%d%d" % (a, chunk), [P, CHUNK], I32, on=on)
             nc.vector.tensor_copy(
                 picked[a, chunk][:].bitcast(U32),
                 windows[a][:].bitcast(U32).indirect(offsets[:, span(chunk, CHUNK // 16)]),
@@ -165,7 +150,8 @@ def tile_list_kvt_dl_sig_kernel(
 
         def table_operand(a, index, width):
             chunk, part = divmod(index, CHUNK // width)
-            return picked[a, chunk][:, span(part, width)].bitcast(FP8X4), planes[a][:, span(index, width // 4)].bitcast(U8)
+            codes = picked[a, chunk][:, span(part, width)].bitcast(FP8X4)
+            return codes, planes[a][:, span(index, width // 4)].bitcast(U8)
 
         value_banks = [take_bank(number) for number in range(BANKS)]
 
@@ -185,21 +171,24 @@ def tile_list_kvt_dl_sig_kernel(
                 )
 
         for a in range(PASSES):
-            round_and_interleave("S", wvd_bf[a][:], wvd_raw[a][:])
+            round_and_interleave("S", wvd_bf[a][:], wvd_raw[a][:], run=4)
         for chunk in range(CHUNKS):
             gather(0, chunk)
         quantise(wvd_codes[0][:], wvd_plane[0][:], wvd_bf[0][:])
         for packed in (True, False):
             for chunk in range(CHUNKS):
                 value_passes(0, packed, chunk)
-        for chunk in range(CHUNKS):
-            if chunk == CB:
-                quantise(wvd_codes[1][:], wvd_plane[1][:], wvd_bf[1][:])
+        for chunk in range(CODES_BEFORE):
             gather(1, chunk)
-        for chunks in GROUPS:
+        quantise(wvd_codes[1][:], wvd_plane[1][:], wvd_bf[1][:])
+        gather(1, CODES_BEFORE, on="wvd_raw1")
+        gather(1, CODES_BEFORE + 1, on="wvd_bf1")
+        for packed in (True, False):
+            for chunk in range(CODES_BEFORE):
+                value_passes(1, packed, chunk)
+        for chunk in range(CODES_BEFORE, CHUNKS):
             for packed in (True, False):
-                for chunk in chunks:
-                    value_passes(1, packed, chunk)
+                value_passes(1, packed, chunk)
 
         wk_bf = per_pass("wk_bf", [P, PACK, PACK * P], BF16)
         wk_codes = per_pass("wk_codes", [P, R], U32)
@@ -214,52 +203,53 @@ def tile_list_kvt_dl_sig_kernel(
             rounded = wk_bf[a][:, span(pair, 2)].rearrange("p t c -> p (t c)")
             quantise(wk_codes[a][:, span(pair, 2 * P)], wk_plane[a][:, span(pair, 2 * P)], rounded)
 
-        first_values = mx_tile("first_values", [P, N // P, FV * CHUNK], F32)
-        for number in range(2 * FV):
-            chunk, tile = divmod(number, N // P)
-            copy_on(VE[number], first_values[:, tile, span(chunk, CHUNK)], value_banks[number][:])
+        first_values = mx_tile("first_values", [P, N // P, CHUNK], F32)
+        for tile in range(N // P):
+            nc.scalar.copy(out=first_values[:, tile], in_=value_banks[tile][:])
         for a in range(PASSES):
             for pair in range(2):
-                round_wk(WKE[2 * a + pair], a, pair)
+                round_wk("S" if a == 0 and pair == 0 else "V", a, pair)
             for pair in range(2):
                 quantise_wk(a, pair)
-        values = mx_tile("values", [P, N // P, J - FV * CHUNK], F32, on="wk_raw0")
-        for number in range(2 * FV, BANKS):
+        values = mx_tile("values", [P, N // P, J - CHUNK], F32, on="wk_raw0")
+        for number in range(N // P, BANKS):
             chunk, tile = divmod(number, N // P)
-            copy_on(VE[number], values[:, tile, span(chunk - FV, CHUNK)], value_banks[number][:])
-        nc.sync.dma_start(out_1[:, 0 : FV * CHUNK].rearrange("(u p) n -> p u n", p=P), first_values[:])
+            nc.scalar.copy(out=values[:, tile, span(chunk - 1, CHUNK)], in_=value_banks[number][:])
+        nc.sync.dma_start(out_1[:, 0:CHUNK].rearrange("(u p) n -> p u n", p=P), first_values[:])
         for tile in range(N // P):
-            nc.sync.dma_start(out_1[span(tile, P), FV * CHUNK : J], values[:, tile, :])
+            nc.sync.dma_start(out_1[span(tile, P), CHUNK:J], values[:, tile, :])
 
         x_bf = per_pass("x_bf", [P, PACK * M], BF16)
         x_codes = per_pass("x_codes", [P, M], U32)
         x_plane = per_pass("x_plane", [P, M], U8)
         wq_codes = mx_tile("wq_codes", [P, PACK, PASSES, P // 2], I32)
 
-        def prepare_x(a, width, engines):
+        def prepare_x(a, width):
             for step in range(M // width + 1):
                 if step < M // width:
                     src = x_raw[a][:, :, span(step, width)]
-                    round_and_interleave(engines[step], x_bf[a][:, span(step, PACK * width)], src)
+                    round_and_interleave("V", x_bf[a][:, span(step, PACK * width)], src, run=4)
                 if step > 0:
                     cols = span(step - 1, width)
                     quantise(x_codes[a][:, cols], x_plane[a][:, cols], x_bf[a][:, span(step - 1, PACK * width)])
 
-        prepare_x(0, HALF, X0E)
+        prepare_x(0, HALF)
         nc.vector.tensor_copy(
             out=wq_codes[:].rearrange("p t a (g w) -> p t (a g) w", w=2),
             in_=wq_raw[:].rearrange("p a (g t w) -> p t (a g) w", t=PACK, w=2),
         )
-        prepare_x(1, P, X1E)
+        prepare_x(1, P)
 
-        key_bf = [mx_tile("key_bf", [P, PACK * J // 2], BF16), mx_tile("key_bf_late", [P, PACK * J // 2], BF16, on="x_raw1")]
-        key_codes = mx_tile("key_codes", [P, J], U32, on=CODES_ON)
+        early_bf = mx_tile("early_bf", [P, EARLY_KEYS * BANK], BF16)
+        late_bf = mx_tile("late_bf", [P, (KEY_TILES - EARLY_KEYS) * BANK], BF16, on="x_raw1")
+        key_codes = mx_tile("key_codes", [P, J], U32, on="x_bf1")
         key_plane = mx_tile("key_plane", [P, J], U8)
         query_bf = mx_tile("query_bf", [P, PACK * M], BF16)
         query_codes = mx_tile("query_codes", [P, M], U32)
         query_plane = mx_tile("query_plane", [P, M], U8)
-        scores = sbuf.tile([P, J // P, BANK], F32, name="scores")
-        paired = PAIRED
+        scores = sbuf.tile([P, KEY_TILES, BANK], F32, name="scores")
+        runs = [(first, QUARTERS) for first in range(0, KEY_TILES - QUARTERS, QUARTERS)]
+        runs.extend((first, 2) for first in range(KEY_TILES - QUARTERS, KEY_TILES, 2))
 
         def key_pass(bank, number, a, t):
             rhs, rhs_scale = table_operand(a, number, P)
@@ -277,28 +267,30 @@ def tile_list_kvt_dl_sig_kernel(
                 start=(a == 0 and t == 0), stop=(a == PASSES - 1 and t == PACK - 1),
             )
 
-        def round_bank(engine, rounded, number, bank):
-            round_and_interleave(engine, rounded[:, span(number, BANK)], bank[:].rearrange("p (t n) -> p t n", t=PACK), run=2)
+        def keys_bf(first, count):
+            tile, at = (early_bf, first) if first < EARLY_KEYS else (late_bf, first - EARLY_KEYS)
+            return tile[:, at * BANK : (at + count) * BANK]
+
+        def round_bank(engine, rounded, bank):
+            round_and_interleave(engine, rounded, bank[:].rearrange("p (t n) -> p t n", t=PACK), run=2)
 
         def quantise_keys(first, count):
             cols = slice(first * P, (first + count) * P)
-            quantise(key_codes[:, cols], key_plane[:, cols], key_bf[first // 8][:, first % 8 * BANK : (first % 8 + count) * BANK])
+            quantise(key_codes[:, cols], key_plane[:, cols], keys_bf(first, count))
 
-        early, product_ring, score_ring = list(EARLY), list(RING), list(SCORE_BANKS)
+        rings = {"low": list(range(BANKS // 2)), "high": list(range(BANKS // 2, BANKS))}
 
-        def multiply(kind, first, second):
-            if early:
-                number = early.pop(0)
-            else:
-                ring = score_ring if kind == "score" else product_ring
-                number = ring.pop(0)
-                ring.append(number)
-            bank = take_bank(number)
+        def next_bank(ring):
+            rings[ring].append(rings[ring].pop(0))
+            return take_bank(rings[ring][-1])
+
+        def multiply(kind, number, part):
+            bank = next_bank("high" if kind == "score" or (kind == "key" and number < EARLY_KEYS) else "low")
             if kind == "score":
-                start, count = RUNS[first]
-                cols = slice(start * P, (start + count) * P)
+                first, count = runs[number]
+                cols = slice(first * P, (first + count) * P)
                 for u in range(TILES // count):
-                    tile = second * (TILES // count) + u
+                    tile = part * (TILES // count) + u
                     nc.tensor.matmul_mx(
                         out=bank[:, span(u, count * P)], lhsT=query_codes[:, span(tile, P)].bitcast(FP8X4),
                         lhsT_scale=query_plane[:, span(tile, P)],
@@ -307,40 +299,33 @@ def tile_list_kvt_dl_sig_kernel(
             else:
                 for a in range(PASSES):
                     for t in range(PACK):
-                        (key_pass if kind == "key" else query_pass)(bank, first, a, t)
+                        (key_pass if kind == "key" else query_pass)(bank, number, a, t)
             return bank
 
-        def empty(bank, kind, first, second):
+        def empty(bank, kind, number, part):
             if kind == "score":
-                start, count = RUNS[first]
-                if first < paired:
-                    slot = paired * second + first
-                    nc.scalar.activation(out=scores[:, slot], in_=bank[:], func=SIGMOID, scale=SCORE_SCALE)
-                    if first == paired - 1:
-                        nc.sync.dma_start(
-                            out_0[span(second, P), 0 : paired * CHUNK],
-                            scores[:, paired * second : paired * (second + 1)].rearrange("p c n -> p (c n)"),
-                        )
-                    return
-                staged = scores[:, start + second]
+                first, count = runs[number]
+                staged = scores[:, first + part]
                 nc.scalar.activation(out=staged, in_=bank[:], func=SIGMOID, scale=SCORE_SCALE)
                 nc.sync.dma_start(
-                    out_0[span(second, M // count), start * P : (start + count) * P].rearrange("(u p) n -> p u n", p=P),
+                    out_0[span(part, M // count), first * P : (first + count) * P].rearrange("(u p) n -> p u n", p=P),
                     staged.rearrange("p (u n) -> p u n", n=count * P),
                 )
             elif kind == "query":
-                round_bank(second, query_bf, first, bank)
-                quantise(query_codes[:, span(first, P)], query_plane[:, span(first, P)], query_bf[:, span(first, BANK)])
-                if first == DEFER_TO:
-                    for start in range(QUARTERS, EARLY_KEYS, 2):
-                        quantise_keys(start, 2)
+                rounded = query_bf[:, span(number, BANK)]
+                round_bank("VS"[number % 2], rounded, bank)
+                quantise(query_codes[:, span(number, P)], query_plane[:, span(number, P)], rounded)
+                if number == TILES - 1:
+                    for first in range(QUARTERS, EARLY_KEYS, 2):
+                        quantise_keys(first, 2)
             else:
-                round_bank(second, key_bf[first // 8], first % 8, bank)
-                for start, count in QRUNS:
-                    if first == start + count - 1 and not QUARTERS <= first < EARLY_KEYS:
-                        quantise_keys(start, count)
+                round_bank("S" if number < EARLY_KEYS else "V", keys_bf(number, 1), bank)
+                if number >= KEY_TILES - 2:
+                    quantise_keys(number, 1)
+                elif number % 2 == 1 and not QUARTERS <= number < EARLY_KEYS:
+                    quantise_keys(number - 1, 2)
 
-        first_banks = [take_bank(number) for number in range(QUARTERS)]
+        first_banks = [next_bank("low") for number in range(QUARTERS)]
         for number, bank in enumerate(first_banks):
             for t in range(PACK):
                 key_pass(bank, number, 0, t)
@@ -349,29 +334,27 @@ def tile_list_kvt_dl_sig_kernel(
                 for t in (2 * pair, 2 * pair + 1):
                     key_pass(bank, number, 1, t)
         for number, bank in enumerate(first_banks):
-            empty(bank, "key", number, KE[number])
+            empty(bank, "key", number, 0)
 
-        jobs = [("key", number, KE[number]) for number in range(QUARTERS, EARLY_KEYS)]
-        jobs.extend(("query", tile, QE[tile]) for tile in range(TILES))
-        ready_at = {run: 0 for run, (start, count) in enumerate(RUNS) if start + count <= EARLY_KEYS}
-        waiting = [("score", run, tile) for tile in range(TILES) for run in range(paired)]
-        waiting.extend(("score", run, part) for run, (start, count) in enumerate(RUNS) for part in range(count) if run >= paired)
-        for number in range(EARLY_KEYS, J // P):
-            jobs.append(("key", number, KE[number]))
-            for run, (start, count) in enumerate(RUNS):
-                if number == start + count - 1 and start < J // P - QUARTERS:
-                    ready_at[run] = len(jobs) + WAITJ
-            for turn in range(SCORES_PER_KEY[number - EARLY_KEYS]):
-                if ready_at.get(waiting[0][1], len(jobs) + 1) <= len(jobs):
+        jobs = [("key", number, 0) for number in range(QUARTERS, EARLY_KEYS)]
+        jobs.extend(("query", tile, 0) for tile in range(TILES))
+        waiting = [("score", run, part) for run, (first, count) in enumerate(runs) for part in range(count)]
+        written_at = {number: 0 for number in range(EARLY_KEYS)}
+        for number in range(EARLY_KEYS, KEY_TILES):
+            jobs.append(("key", number, 0))
+            written_at[number] = len(jobs) + LAG
+            for turn in range(SCORES_PER_KEY):
+                first, count = runs[waiting[0][1]]
+                if count == QUARTERS and written_at.get(first + count - 1, len(jobs) + 1) <= len(jobs):
                     jobs.append(waiting.pop(0))
         jobs.extend(waiting)
 
         filled = []
-        for job in jobs:
-            if job[0] == "score":
-                while any(kind == "key" and first < sum(RUNS[job[1]]) for bank, kind, first, second in filled):
+        for kind, number, part in jobs:
+            if kind == "score":
+                while any(entry[1] == "key" and entry[2] < sum(runs[number]) for entry in filled):
                     empty(*filled.pop(0))
-            filled.append((multiply(*job), *job))
+            filled.append((multiply(kind, number, part), kind, number, part))
             if len(filled) > LAG:
                 empty(*filled.pop(0))
         for entry in filled:

@@ -203,21 +203,26 @@ def tile_list_kvt_dl_sig_kernel(
             rounded = wk_bf[a][:, span(pair, 2)].rearrange("p t c -> p (t c)")
             quantise(wk_codes[a][:, span(pair, 2 * P)], wk_plane[a][:, span(pair, 2 * P)], rounded)
 
-        first_values = mx_tile("first_values", [P, N // P, CHUNK], F32)
-        for tile in range(N // P):
-            nc.scalar.copy(out=first_values[:, tile], in_=value_banks[tile][:])
-        for a in range(PASSES):
-            for pair in range(2):
-                round_wk("S" if a == 0 and pair == 0 else "V", a, pair)
-            for pair in range(2):
-                quantise_wk(a, pair)
-        values = mx_tile("values", [P, N // P, J - CHUNK], F32, on="wk_raw0")
-        for number in range(N // P, BANKS):
+        round_wk("S", 0, 0)
+        for t in (2, 3):
+            nc.gpsimd.tensor_scalar(
+                out=wk_bf[0][:, t].rearrange("p (g i j) -> p g i j", i=4, j=PACK),
+                in0=wk_raw[0][:].rearrange("p j (g t i) -> p t g i j", t=PACK, i=4)[:, t],
+                scalar1=1.0, scalar2=0.0, op0=mybir.AluOpType.mult, op1=mybir.AluOpType.add,
+            )
+        for pair in range(2):
+            quantise_wk(0, pair)
+        for pair in range(2):
+            round_wk("V", 1, pair)
+        for pair in range(2):
+            quantise_wk(1, pair)
+        values = mx_tile("values", [P, N // P, J], F32, on="wk_raw0")
+        for number, bank in enumerate(value_banks):
             chunk, tile = divmod(number, N // P)
-            nc.scalar.copy(out=values[:, tile, span(chunk - 1, CHUNK)], in_=value_banks[number][:])
-        nc.sync.dma_start(out_1[:, 0:CHUNK].rearrange("(u p) n -> p u n", p=P), first_values[:])
-        for tile in range(N // P):
-            nc.sync.dma_start(out_1[span(tile, P), CHUNK:J], values[:, tile, :])
+            nc.scalar.copy(out=values[:, tile, span(chunk, CHUNK)], in_=bank[:])
+        for half in range(2):
+            for tile in range(N // P):
+                nc.sync.dma_start(out_1[span(tile, P), span(half, J // 2)], values[:, tile, span(half, J // 2)])
 
         x_bf = per_pass("x_bf", [P, PACK * M], BF16)
         x_codes = per_pass("x_codes", [P, M], U32)

@@ -37,6 +37,7 @@ EARLY_KEYS = 2 * QUARTERS
 CODES_BEFORE = 2
 SCORES_PER_KEY = 2
 LAG = 2
+PRELOAD = 1280
 
 
 def tile_list_kvt_dl_sig_kernel(
@@ -79,12 +80,12 @@ def tile_list_kvt_dl_sig_kernel(
             return psum.tile([P, BANK], F32, name="bank", tag="bank%d" % number)
 
         offsets = sbuf.tile([P, J // 16], U16, name="offsets")
-        nc.sync.dma_start(offsets[:], offs)
         weight_rows = mx_tile("weight_rows", [BLOCKS, PASSES, PLANE], I32)
         wq_scale_rows = mx_tile("wq_scale_rows", [BLOCKS, PASSES, R // 4], I32)
         weight_plane = mx_tile("weight_plane", [P, PASSES, PLANE], I32)
         scale_window = mx_tile("scale_window", [P, T // 4], I32)
         planes = per_pass("plane", [P, J // 4], I32)
+        nc.scalar.dma_start(scale_window[0:32, :], tab_scales.rearrange("a b t -> (a b) t").bitcast(I32))
         warm_in = sbuf.tile([P, 1], F32, name="warm_in")
         warm_out = sbuf.tile([P, 1], F32, name="warm_out")
         nc.gpsimd.memset(warm_in[:], 0.0)
@@ -95,8 +96,8 @@ def tile_list_kvt_dl_sig_kernel(
         for a in range(PASSES):
             nc.gpsimd.memset(planes[a][:], 0)
         nc.sync.dma_start(wq_scale_rows[:], wq_scales.rearrange("a b r -> b a r").bitcast(I32))
+        nc.sync.dma_start(offsets[:], offs)
         nc.sync.dma_start(weight_rows[:, :, 0:WQ_AT], wv4_scales.rearrange("a b n -> b a n").bitcast(I32))
-        nc.sync.dma_start(scale_window[0:32, :], tab_scales.rearrange("a b t -> (a b) t").bitcast(I32))
         nc.vector.tensor_copy(
             out=weight_rows[:, :, WQ_AT:PLANE].rearrange("p a (t g) -> p a t g", t=PACK),
             in_=wq_scale_rows[:].rearrange("p a (g t) -> p a t g", t=PACK),
@@ -121,13 +122,13 @@ def tile_list_kvt_dl_sig_kernel(
             nc.sync.dma_start(weight_plane[row:P:32], weight_rows[row:BLOCKS:4])
         nc.sync.dma_start(wv4_codes[:], wv4_words.rearrange("a p b -> p a b").bitcast(I32))
         nc.sync.dma_start(wvd_raw[0][:], k_rows(wvd, 0))
-        load_window(1, slice(0, T // 4))
+        load_window(1, slice(0, PRELOAD))
 
         picked_scales = mx_tile("picked_scales", [P, J // 4], I32)
         nc.vector.tensor_copy(picked_scales[:].bitcast(U8), scale_window[:].bitcast(U8).indirect(offsets[:]))
 
         move_scale_rows(0)
-        load_window(1, slice(T // 4, T))
+        load_window(1, slice(PRELOAD, T))
         nc.sync.dma_start(wvd_raw[1][:], k_rows(wvd, 1))
         move_scale_rows(1)
         for a in range(PASSES):

@@ -38,6 +38,7 @@ CODES_BEFORE = 2
 SCORES_PER_KEY = 2
 LAG = 2
 PRELOAD = 1280
+ROWS_AT = 96
 
 
 def tile_list_kvt_dl_sig_kernel(
@@ -49,7 +50,7 @@ def tile_list_kvt_dl_sig_kernel(
         psum = ctx.enter_context(tc.psum_pool(name="psum", bufs=1))
 
         def mx_tile(name, shape, dtype, on=None):
-            return sbuf.tile(shape, dtype, name=name, tag=on or name, align_bytes=64)
+            return sbuf.tile(shape, dtype, name=name, tag=on or name, align_bytes=256)
 
         def per_pass(name, shape, dtype):
             return [mx_tile("%s%d" % (name, a), shape, dtype) for a in range(PASSES)]
@@ -85,20 +86,19 @@ def tile_list_kvt_dl_sig_kernel(
         weight_plane = mx_tile("weight_plane", [P, PASSES, PLANE], I32)
         scale_window = mx_tile("scale_window", [P, T // 4], I32)
         planes = per_pass("plane", [P, J // 4], I32)
-        nc.scalar.dma_start(scale_window[0:32, :], tab_scales.rearrange("a b t -> (a b) t").bitcast(I32))
+        nc.scalar.dma_start(scale_window[ROWS_AT:P, :], tab_scales.rearrange("a b t -> (a b) t").bitcast(I32))
         warm_in = sbuf.tile([P, 1], F32, name="warm_in")
         warm_out = sbuf.tile([P, 1], F32, name="warm_out")
         nc.gpsimd.memset(warm_in[:], 0.0)
         nc.scalar.activation(out=warm_out[:], in_=warm_in[:], func=SIGMOID)
-        nc.vector.memset(scale_window[32:64, :], 0)
-        nc.vector.memset(scale_window[64:128, :], 0)
+        nc.vector.memset(scale_window[0:ROWS_AT, :], 0)
         nc.gpsimd.memset(weight_plane[:], 0)
         for a in range(PASSES):
             nc.gpsimd.memset(planes[a][:], 0)
-        nc.sync.dma_start(wq_scale_rows[:], wq_scales.rearrange("a b r -> b a r").bitcast(I32))
         nc.sync.dma_start(offsets[:], offs)
+        nc.sync.dma_start(wq_scale_rows[:], wq_scales.rearrange("a b r -> b a r").bitcast(I32))
         nc.sync.dma_start(weight_rows[:, :, 0:WQ_AT], wv4_scales.rearrange("a b n -> b a n").bitcast(I32))
-        nc.vector.tensor_copy(
+        nc.gpsimd.tensor_copy(
             out=weight_rows[:, :, WQ_AT:PLANE].rearrange("p a (t g) -> p a t g", t=PACK),
             in_=wq_scale_rows[:].rearrange("p a (g t) -> p a t g", t=PACK),
         )
@@ -114,8 +114,9 @@ def tile_list_kvt_dl_sig_kernel(
             nc.sync.dma_start(windows[a][:, cols], tab_words[a].rearrange("p t i -> p (t i)").bitcast(I32)[:, cols])
 
         def move_scale_rows(a):
+            first = ROWS_AT + a * BLOCKS
             for row in range(4):
-                nc.sync.dma_start(planes[a][row:P:32, :], picked_scales[a * BLOCKS + row : (a + 1) * BLOCKS : 4, :])
+                nc.sync.dma_start(planes[a][row:P:32, :], picked_scales[first + row : first + BLOCKS : 4, :])
 
         load_window(0)
         for row in range(4):

@@ -206,10 +206,15 @@ def tile_list_kvt_dl_sig_kernel(
             quantise(wk_codes[a][:, span(pair, 2 * P)], wk_plane[a][:, span(pair, 2 * P)], rounded)
 
         round_wk("S", 0, 0)
-        for t in (2, 3):
+        groups = P // 4
+        nc.scalar.copy(
+            out=wk_bf[0][:, 2].rearrange("p (g i j) -> p g j i", i=4, j=PACK)[:, 0 : groups // 2],
+            in_=wk_raw[0][:].rearrange("p j (g t i) -> p t g j i", t=PACK, i=4)[:, 2, 0 : groups // 2],
+        )
+        for t, first in ((2, groups // 2), (3, 0)):
             nc.gpsimd.tensor_scalar(
-                out=wk_bf[0][:, t].rearrange("p (g i j) -> p g i j", i=4, j=PACK),
-                in0=wk_raw[0][:].rearrange("p j (g t i) -> p t g i j", t=PACK, i=4)[:, t],
+                out=wk_bf[0][:, t].rearrange("p (g i j) -> p g i j", i=4, j=PACK)[:, first:groups],
+                in0=wk_raw[0][:].rearrange("p j (g t i) -> p t g i j", t=PACK, i=4)[:, t, first:groups],
                 scalar1=1.0, scalar2=0.0, op0=mybir.AluOpType.mult, op1=mybir.AluOpType.add,
             )
         for pair in range(2):

from contextlib import ExitStack

import concourse.mybir as mybir

K, R, M, N, T, J = 1024, 512, 512, 256, 4096, 2048
FLOPS = 2 * (K * R * M + K * R * J + R * M * J + 2 * K * N * J)
SCORE_SCALE = 0.03125

F32 = mybir.dt.float32
BF16 = mybir.dt.bfloat16
I32 = mybir.dt.int32
U32 = mybir.dt.uint32
U16 = mybir.dt.uint16
U8 = mybir.dt.uint8
FP8X4 = mybir.dt.float8_e4m3fn_x4
FP4X4 = mybir.dt.float4_e2m1fn_x4
SIGMOID = mybir.ActivationFunctionType.Sigmoid

P = 128
PACK = 4
PASS_K = P * PACK
PASSES = K // PASS_K
BLOCKS = PASS_K // 32
BANK = 512
BANKS = 8
CHUNK = 512
CHUNKS = J // CHUNK
QUARTERS = CHUNK // P
TILES = M // P
HALF = 256

WQ_AT = N // 4
PLANE = WQ_AT + R // 4

KEY_TILES = J // P
EARLY_KEYS = 2 * QUARTERS
CODES_BEFORE = 2
SCORES_PER_KEY = 2
LAG = 2
PRELOAD = 1280
ROWS_AT = 96


def tile_list_kvt_dl_sig_kernel(
    tc, tab_words, tab_scales, x, wq_words, wq_scales, wk, wv4_words, wv4_scales, wvd, offs, out_0, out_1
):
    nc = tc.nc
    with ExitStack() as ctx:
        sbuf = ctx.enter_context(tc.tile_pool(name="sbuf", bufs=1))
        psum = ctx.enter_context(tc.psum_pool(name="psum", bufs=1))

        def mx_tile(name, shape, dtype, on=None):
            return sbuf.tile(shape, dtype, name=name, tag=on or name, align_bytes=256)

        def per_pass(name, shape, dtype):
            return [mx_tile("%s%d" % (name, a), shape, dtype) for a in range(PASSES)]

        def copy_on(engine, out, in_):
            if engine == "S":
                nc.scalar.copy(out=out, in_=in_)
            else:
                nc.vector.tensor_copy(out=out, in_=in_)

        def span(index, width):
            return slice(index * width, (index + 1) * width)

        def k_rows(source, a):
            return source[span(a, PASS_K), :].rearrange("(p j) n -> p j n", j=PACK)

        def round_and_interleave(engine, dst, src, run):
            copy_on(
                engine,
                dst.rearrange("p (c i j) -> p c j i", i=run, j=PACK),
                src.rearrange("p j (c i) -> p c j i", i=run),
            )

        def quantise(codes, scales, values):
            nc.vector.quantize_mx(out=codes.bitcast(FP8X4), scales=scales, in_=values)

        def take_bank(number):
            return psum.tile([P, BANK], F32, name="bank", tag="bank%d" % number)

        offsets = sbuf.tile([P, J // 16], U16, name="offsets")
        weight_rows = mx_tile("weight_rows", [BLOCKS, PASSES, PLANE], I32)
        wq_scale_rows = mx_tile("wq_scale_rows", [BLOCKS, PASSES, R // 4], I32)
        weight_plane = mx_tile("weight_plane", [P, PASSES, PLANE], I32)
        scale_window = mx_tile("scale_window", [P, T // 4], I32)
        planes = per_pass("plane", [P, J // 4], I32)
        nc.scalar.dma_start(scale_window[ROWS_AT:P, :], tab_scales.rearrange("a b t -> (a b) t").bitcast(I32))
        warm_in = sbuf.tile([P, 1], F32, name="warm_in")
        warm_out = sbuf.tile([P, 1], F32, name="warm_out")
        nc.gpsimd.memset(warm_in[:], 0.0)
        nc.scalar.activation(out=warm_out[:], in_=warm_in[:], func=SIGMOID)
        nc.vector.memset(scale_window[0:ROWS_AT, :], 0)
        nc.gpsimd.memset(weight_plane[:], 0)
        for a in range(PASSES):
            nc.gpsimd.memset(planes[a][:], 0)
        nc.sync.dma_start(offsets[:], offs)
        nc.sync.dma_start(wq_scale_rows[:], wq_scales.rearrange("a b r -> b a r").bitcast(I32))
        nc.sync.dma_start(weight_rows[:, :, 0:WQ_AT], wv4_scales.rearrange("a b n -> b a n").bitcast(I32))
        nc.gpsimd.tensor_copy(
            out=weight_rows[:, :, WQ_AT:PLANE].rearrange("p a (t g) -> p a t g", t=PACK),
            in_=wq_scale_rows[:].rearrange("p a (g t) -> p a t g", t=PACK),
        )

        windows = per_pass("window", [P, T], I32)
        wv4_codes = mx_tile("wv4_codes", [P, PASSES, N // 2], I32)
        wvd_raw = per_pass("wvd_raw", [P, PACK, N], F32)
        wk_raw = per_pass("wk_raw", [P, PACK, R], F32)
        x_raw = per_pass("x_raw", [P, PACK, M], F32)
        wq_raw = sbuf.tile([P, PASSES, R // 2], I32, name="wq_raw")

        def load_window(a, cols=slice(0, T)):
            nc.sync.dma_start(windows[a][:, cols], tab_words[a].rearrange("p t i -> p (t i)").bitcast(I32)[:, cols])

        def move_scale_rows(a):
            first = ROWS_AT + a * BLOCKS
            for row in range(4):
                nc.sync.dma_start(planes[a][row:P:32, :], picked_scales[first + row : first + BLOCKS : 4, :])

        load_window(0)
        for row in range(4):
            nc.sync.dma_start(weight_plane[row:P:32], weight_rows[row:BLOCKS:4])
        nc.sync.dma_start(wv4_codes[:], wv4_words.rearrange("a p b -> p a b").bitcast(I32))
        nc.sync.dma_start(wvd_raw[0][:], k_rows(wvd, 0))
        load_window(1, slice(0, PRELOAD))

        picked_scales = mx_tile("picked_scales", [P, J // 4], I32)
        nc.vector.tensor_copy(picked_scales[:].bitcast(U8), scale_window[:].bitcast(U8).indirect(offsets[:]))

        move_scale_rows(0)
        load_window(1, slice(PRELOAD, T))
        nc.sync.dma_start(wvd_raw[1][:], k_rows(wvd, 1))
        move_scale_rows(1)
        for a in range(PASSES):
            nc.sync.dma_start(wk_raw[a][:], k_rows(wk, a))
        for a in range(PASSES):
            nc.sync.dma_start(x_raw[a][:], k_rows(x, a))
        nc.sync.dma_start(wq_raw[:], wq_words.rearrange("a p b -> p a b").bitcast(I32))

        picked = {}
        wvd_bf = per_pass("wvd_bf", [P, PACK * N], BF16)
        wvd_codes = per_pass("wvd_codes", [P, N], U32)
        wvd_plane = per_pass("wvd_plane", [P, N], U8)

        def gather(a, chunk, on=None):
            picked[a, chunk] = mx_tile("picked%d%d" % (a, chunk), [P, CHUNK], I32, on=on)
            nc.vector.tensor_copy(
                picked[a, chunk][:].bitcast(U32),
                windows[a][:].bitcast(U32).indirect(offsets[:, span(chunk, CHUNK // 16)]),
            )

        def table_operand(a, index, width):
            chunk, part = divmod(index, CHUNK // width)
            codes = picked[a, chunk][:, span(part, width)].bitcast(FP8X4)
            return codes, planes[a][:, span(index, width // 4)].bitcast(U8)

        value_banks = [take_bank(number) for number in range(BANKS)]

        def value_passes(a, packed, chunk):
            rhs, rhs_scale = table_operand(a, chunk, CHUNK)
            for tile in range(N // P):
                if packed:
                    lhsT = wv4_codes[:, a, span(tile, P // 2)].bitcast(FP4X4)
                    lhsT_scale = weight_plane[:, a, span(tile, P // 4)].bitcast(U8)
                else:
                    lhsT = wvd_codes[a][:, span(tile, P)].bitcast(FP8X4)
                    lhsT_scale = wvd_plane[a][:, span(tile, P)]
                nc.tensor.matmul_mx(
                    out=value_banks[chunk * (N // P) + tile][:], lhsT=lhsT, lhsT_scale=lhsT_scale,
                    rhs=rhs, rhs_scale=rhs_scale,
                    start=(packed and a == 0), stop=(not packed and a == PASSES - 1),
                )

        for a in range(PASSES):
            round_and_interleave("S", wvd_bf[a][:], wvd_raw[a][:], run=4)
        for chunk in range(CHUNKS):
            gather(0, chunk)
        quantise(wvd_codes[0][:], wvd_plane[0][:], wvd_bf[0][:])
        for packed in (True, False):
            for chunk in range(CHUNKS):
                value_passes(0, packed, chunk)
        for chunk in range(CODES_BEFORE):
            gather(1, chunk)
        quantise(wvd_codes[1][:], wvd_plane[1][:], wvd_bf[1][:])
        gather(1, CODES_BEFORE, on="wvd_raw1")
        gather(1, CODES_BEFORE + 1, on="wvd_bf1")
        for packed in (True, False):
            for chunk in range(CODES_BEFORE):
                value_passes(1, packed, chunk)
        for chunk in range(CODES_BEFORE, CHUNKS):
            for packed in (True, False):
                value_passes(1, packed, chunk)

        wk_bf = per_pass("wk_bf", [P, PACK, PACK * P], BF16)
        wk_codes = per_pass("wk_codes", [P, R], U32)
        wk_plane = per_pass("wk_plane", [P, R], U8)

        def round_wk(engine, a, pair):
            by_tile = wk_raw[a][:].rearrange("p j (g t i) -> p t g j i", t=PACK, i=4)
            dst = wk_bf[a][:].rearrange("p t (g i j) -> p t g j i", i=4, j=PACK)
            copy_on(engine, dst[:, span(pair, 2)], by_tile[:, span(pair, 2)])

        def quantise_wk(a, pair):
            rounded = wk_bf[a][:, span(pair, 2)].rearrange("p t c -> p (t c)")
            quantise(wk_codes[a][:, span(pair, 2 * P)], wk_plane[a][:, span(pair, 2 * P)], rounded)

        round_wk("S", 0, 0)
        groups = P // 4
        nc.scalar.copy(
            out=wk_bf[0][:, 2].rearrange("p (g i j) -> p g j i", i=4, j=PACK)[:, 0 : groups // 2],
            in_=wk_raw[0][:].rearrange("p j (g t i) -> p t g j i", t=PACK, i=4)[:, 2, 0 : groups // 2],
        )
        for t, first in ((2, groups // 2), (3, 0)):
            nc.gpsimd.tensor_scalar(
                out=wk_bf[0][:, t].rearrange("p (g i j) -> p g i j", i=4, j=PACK)[:, first:groups],
                in0=wk_raw[0][:].rearrange("p j (g t i) -> p t g i j", t=PACK, i=4)[:, t, first:groups],
                scalar1=1.0, scalar2=0.0, op0=mybir.AluOpType.mult, op1=mybir.AluOpType.add,
            )
        for pair in range(2):
            quantise_wk(0, pair)
        for pair in range(2):
            round_wk("V", 1, pair)
        for pair in range(2):
            quantise_wk(1, pair)
        values = mx_tile("values", [P, N // P, J], F32, on="wk_raw0")
        for number, bank in enumerate(value_banks):
            chunk, tile = divmod(number, N // P)
            nc.scalar.copy(out=values[:, tile, span(chunk, CHUNK)], in_=bank[:])
        for half in range(2):
            for tile in range(N // P):
                nc.sync.dma_start(out_1[span(tile, P), span(half, J // 2)], values[:, tile, span(half, J // 2)])

        x_bf = per_pass("x_bf", [P, PACK * M], BF16)
        x_codes = per_pass("x_codes", [P, M], U32)
        x_plane = per_pass("x_plane", [P, M], U8)
        wq_codes = mx_tile("wq_codes", [P, PACK, PASSES, P // 2], I32)

        def prepare_x(a, width):
            for step in range(M // width + 1):
                if step < M // width:
                    src = x_raw[a][:, :, span(step, width)]
                    round_and_interleave("V", x_bf[a][:, span(step, PACK * width)], src, run=4)
                if step > 0:
                    cols = span(step - 1, width)
                    quantise(x_codes[a][:, cols], x_plane[a][:, cols], x_bf[a][:, span(step - 1, PACK * width)])

        prepare_x(0, HALF)
        nc.vector.tensor_copy(
            out=wq_codes[:].rearrange("p t a (g w) -> p t (a g) w", w=2),
            in_=wq_raw[:].rearrange("p a (g t w) -> p t (a g) w", t=PACK, w=2),
        )
        prepare_x(1, P)

        early_bf = mx_tile("early_bf", [P, EARLY_KEYS * BANK], BF16)
        late_bf = mx_tile("late_bf", [P, (KEY_TILES - EARLY_KEYS) * BANK], BF16, on="x_raw1")
        key_codes = mx_tile("key_codes", [P, J], U32, on="x_bf1")
        key_plane = mx_tile("key_plane", [P, J], U8)
        query_bf = mx_tile("query_bf", [P, PACK * M], BF16)
        query_codes = mx_tile("query_codes", [P, M], U32)
        query_plane = mx_tile("query_plane", [P, M], U8)
        scores = sbuf.tile([P, KEY_TILES, BANK], F32, name="scores")
        runs = [(first, QUARTERS) for first in range(0, KEY_TILES - QUARTERS, QUARTERS)]
        runs.extend((first, 2) for first in range(KEY_TILES - QUARTERS, KEY_TILES, 2))

        def key_pass(bank, number, a, t):
            rhs, rhs_scale = table_operand(a, number, P)
            nc.tensor.matmul_mx(
                out=bank[:, span(t, P)], lhsT=wk_codes[a][:, span(t, P)].bitcast(FP8X4),
                lhsT_scale=wk_plane[a][:, span(t, P)], rhs=rhs, rhs_scale=rhs_scale,
                start=(a == 0 and t == 0), stop=(a == PASSES - 1 and t == PACK - 1),
            )

        def query_pass(bank, number, a, t):
            nc.tensor.matmul_mx(
                out=bank[:, span(t, P)], lhsT=wq_codes[:, t, a].bitcast(FP4X4),
                lhsT_scale=weight_plane[:, a, WQ_AT:PLANE][:, span(t, P // 4)].bitcast(U8),
                rhs=x_codes[a][:, span(number, P)].bitcast(FP8X4), rhs_scale=x_plane[a][:, span(number, P)],
                start=(a == 0 and t == 0), stop=(a == PASSES - 1 and t == PACK - 1),
            )

        def keys_bf(first, count):
            tile, at = (early_bf, first) if first < EARLY_KEYS else (late_bf, first - EARLY_KEYS)
            return tile[:, at * BANK : (at + count) * BANK]

        def round_bank(engine, rounded, bank):
            round_and_interleave(engine, rounded, bank[:].rearrange("p (t n) -> p t n", t=PACK), run=2)

        def quantise_keys(first, count):
            cols = slice(first * P, (first + count) * P)
            quantise(key_codes[:, cols], key_plane[:, cols], keys_bf(first, count))

        rings = {"low": list(range(BANKS // 2)), "high": list(range(BANKS // 2, BANKS))}

        def next_bank(ring):
            rings[ring].append(rings[ring].pop(0))
            return take_bank(rings[ring][-1])

        def multiply(kind, number, part):
            bank = next_bank("high" if kind == "score" or (kind == "key" and number < EARLY_KEYS) else "low")
            if kind == "score":
                first, count = runs[number]
                cols = slice(first * P, (first + count) * P)
                for u in range(TILES // count):
                    tile = part * (TILES // count) + u
                    nc.tensor.matmul_mx(
                        out=bank[:, span(u, count * P)], lhsT=query_codes[:, span(tile, P)].bitcast(FP8X4),
                        lhsT_scale=query_plane[:, span(tile, P)],
                        rhs=key_codes[:, cols].bitcast(FP8X4), rhs_scale=key_plane[:, cols], start=True, stop=True,
                    )
            else:
                for a in range(PASSES):
                    for t in range(PACK):
                        (key_pass if kind == "key" else query_pass)(bank, number, a, t)
            return bank

        def empty(bank, kind, number, part):
            if kind == "score":
                first, count = runs[number]
                staged = scores[:, first + part]
                nc.scalar.activation(out=staged, in_=bank[:], func=SIGMOID, scale=SCORE_SCALE)
                nc.sync.dma_start(
                    out_0[span(part, M // count), first * P : (first + count) * P].rearrange("(u p) n -> p u n", p=P),
                    staged.rearrange("p (u n) -> p u n", n=count * P),
                )
            elif kind == "query":
                rounded = query_bf[:, span(number, BANK)]
                round_bank("VS"[number % 2], rounded, bank)
                quantise(query_codes[:, span(number, P)], query_plane[:, span(number, P)], rounded)
                if number == TILES - 1:
                    for first in range(QUARTERS, EARLY_KEYS, 2):
                        quantise_keys(first, 2)
            else:
                round_bank("S" if number < EARLY_KEYS else "V", keys_bf(number, 1), bank)
                if number >= KEY_TILES - 2:
                    quantise_keys(number, 1)
                elif number % 2 == 1 and not QUARTERS <= number < EARLY_KEYS:
                    quantise_keys(number - 1, 2)

        first_banks = [next_bank("low") for number in range(QUARTERS)]
        for number, bank in enumerate(first_banks):
            for t in range(PACK):
                key_pass(bank, number, 0, t)
        for pair in range(2):
            for number, bank in enumerate(first_banks):
                for t in (2 * pair, 2 * pair + 1):
                    key_pass(bank, number, 1, t)
        for number, bank in enumerate(first_banks):
            empty(bank, "key", number, 0)

        jobs = [("key", number, 0) for number in range(QUARTERS, EARLY_KEYS)]
        jobs.extend(("query", tile, 0) for tile in range(TILES))
        waiting = [("score", run, part) for run, (first, count) in enumerate(runs) for part in range(count)]
        written_at = {number: 0 for number in range(EARLY_KEYS)}
        for number in range(EARLY_KEYS, KEY_TILES):
            jobs.append(("key", number, 0))
            written_at[number] = len(jobs) + LAG
            for turn in range(SCORES_PER_KEY):
                first, count = runs[waiting[0][1]]
                if count == QUARTERS and written_at.get(first + count - 1, len(jobs) + 1) <= len(jobs):
                    jobs.append(waiting.pop(0))
        jobs.extend(waiting)

        filled = []
        for kind, number, part in jobs:
            if kind == "score":
                while any(entry[1] == "key" and entry[2] < sum(runs[number]) for entry in filled):
                    empty(*filled.pop(0))
            filled.append((multiply(kind, number, part), kind, number, part))
            if len(filled) > LAG:
                empty(*filled.pop(0))
        for entry in filled:
            empty(*entry)
